import numpy as np
import ml_dtypes


def mxq(x, axis, fmt="e4m3"):
    dtype, down = {"e4m3": (ml_dtypes.float8_e4m3fn, 7), "e5m2": (ml_dtypes.float8_e5m2, 14)}[fmt]
    v = np.moveaxis(np.asarray(x, np.float32).astype(ml_dtypes.bfloat16).astype(np.float64), axis, -1)
    blocks = v.reshape(v.shape[:-1] + (-1, 32))
    amax = np.abs(blocks).max(-1, keepdims=True)
    byte = np.maximum(np.where(amax > 0, np.frexp(amax)[1] - 1 + 127, 0) - down, 1)
    scale = np.exp2(byte - 127.0)
    codes = (blocks / scale).astype(np.float32).astype(dtype).astype(np.float64)
    return np.moveaxis((codes * scale).reshape(v.shape), -1, axis)


WIDE = False


def mx_kscale(k):
    if not WIDE:
        return np.ones(k)
    levels = np.array([10, -10, 5, -5, 0])
    if k % 512:
        return np.exp2(np.random.permutation(np.resize(levels, k // 32))).repeat(32)
    a = np.empty((k // 512, 16))
    for p in range(k // 512):
        a[p, :8] = np.random.permutation(np.resize(levels, 8))
        for g in range(8):
            far = levels[np.abs(levels - a[p, g]) >= 10]
            a[p, g + 8] = far[np.random.randint(len(far))]
    return np.exp2(a.ravel()).repeat(32)


def f64(x):
    return np.asarray(x).astype(np.float64)


def striped(idx):
    return np.tile(idx.reshape(-1, 16).T, (8, 1)).astype(np.uint16)


def unstriped(offs):
    return offs[:16].T.reshape(-1).astype(np.int64)


E2M1 = np.array([0.0, 0.5, 1.0, 1.5, 2.0, 3.0, 4.0, 6.0, -0.0, -0.5, -1.0, -1.5, -2.0, -3.0, -4.0, -6.0])


def pack_weight(w, fmt):
    k, n = w.shape
    w = f64(np.asarray(w, np.float32).astype(ml_dtypes.bfloat16)).reshape(k // 32, 32, n)
    amax = np.abs(w).max(1)
    if fmt == "e4m3":
        byte = np.frexp(amax)[1] - 1 + 127 - 7
    else:
        mant, ex = np.frexp(amax / 6.0)
        byte = np.where(mant > 0.5, ex, ex - 1) + 127
    byte = np.clip(np.where(amax > 0, byte, 1), 1, 254)
    scaled = (w * np.exp2(127.0 - byte)[:, None, :]).reshape(k, n).astype(np.float32)
    by_word = np.ascontiguousarray(scaled.reshape(k // 512, 128, 4, n).transpose(0, 1, 3, 2))
    if fmt == "e4m3":
        words = by_word.astype(ml_dtypes.float8_e4m3fn).view(np.uint8)
    else:
        c = by_word.astype(ml_dtypes.float4_e2m1fn).view(np.uint8) & 0xF
        words = (c[..., 0::2] | (c[..., 1::2] << 4)).reshape(k // 512, 128, 2 * n)
    return np.ascontiguousarray(words), np.ascontiguousarray(byte.astype(np.uint8).reshape(k // 512, 16, n))


def unpack_weight(words, scales, fmt):
    g, _, n = scales.shape
    words = np.ascontiguousarray(words).reshape(g, 128, n, -1)
    if fmt == "e4m3":
        vals = words.view(ml_dtypes.float8_e4m3fn).astype(np.float64)
    else:
        nib = np.empty((g, 128, n, 4), np.uint8)
        nib[..., 0::2] = words & 0xF
        nib[..., 1::2] = words >> 4
        vals = E2M1[nib]
    vals = vals * np.repeat(np.exp2(scales.astype(np.float64) - 127.0), 8, axis=1)[..., None]
    return vals.transpose(0, 1, 3, 2).reshape(g * 512, n)


def gelu(v):
    return 0.5 * v * (1.0 + np.tanh(np.sqrt(2.0 / np.pi) * (v + 0.044715 * v**3)))


def bf(x):
    return np.asarray(x, np.float32).astype(ml_dtypes.bfloat16)


def planes(Y):
    n, m = Y.shape
    b = f64(bf(Y)).reshape(n // 32, 32, m)
    amax = np.abs(b).max(1)
    byte = np.clip(np.where(amax > 0, np.frexp(amax)[1] - 1 + 127 - 7, 1), 1, 254)
    codes = (b * np.exp2(127.0 - byte)[:, None, :]).reshape(n, m).astype(np.float32).astype(ml_dtypes.float8_e4m3fn).view(np.uint8)
    words = codes.reshape(n // 512, 128, 4, m).transpose(0, 1, 3, 2)
    return np.ascontiguousarray(words), np.ascontiguousarray(byte.astype(np.uint8).reshape(n // 512, 16, m))


K, T, S, H, N = 512, 2048, 1024, 1024, 512

def setup_inputs():
    n = np.random.standard_normal
    s = mx_kscale(K)[:, None]
    u = mx_kscale(H)[:, None]
    tab_words, tab_scales = pack_weight(n((K, T)) * s, "e4m3")
    w2_words, w2_scales = pack_weight(n((K, H)) / np.sqrt(K) / s, "e2m1")
    w4_words, w4_scales = pack_weight(0.6 * n((K, N)) / np.sqrt(K) / s, "e4m3")
    w5_words, w5_scales = pack_weight(0.6 * n((H, N)) / np.sqrt(H) / u, "e2m1")
    return {
        "tab_words": tab_words, "tab_scales": tab_scales,
        "offs": striped(np.random.permutation(T)[:S]),
        "offs2": striped(np.random.permutation(S)),
        "w1": (n((K, H)) / np.sqrt(K) / s * u.T).astype(np.float32),
        "w2_words": w2_words, "w2_scales": w2_scales,
        "w3": (0.6 * n((H, N)) / np.sqrt(H) / u).astype(np.float32),
        "w4_words": w4_words, "w4_scales": w4_scales,
        "w5_words": w5_words, "w5_scales": w5_scales,
        "w6": (0.6 * n((K, N)) / np.sqrt(K) / s).astype(np.float32),
        "wgo": np.exp(0.3 * n((128, S))).astype(np.float32),
        "x0": n((N, S)).astype(np.float32),
        "amp": np.exp(0.8 * n(N)).astype(np.float32),
    }

def reference(tab_words, tab_scales, offs, offs2, w1, w2_words, w2_scales, w3, w4_words, w4_scales, w5_words, w5_scales, w6, wgo, x0, amp):
    v = unpack_weight(tab_words, tab_scales, "e4m3")[:, unstriped(offs)]
    a = mxq(f64(w1), 0, "e4m3").T @ v
    b = unpack_weight(w2_words, w2_scales, "e2m1").T @ v
    hq = mxq(a * b, 0, "e4m3")
    d = mxq(f64(w3), 0, "e4m3").T @ hq + unpack_weight(w4_words, w4_scales, "e4m3").T @ v
    e = unpack_weight(w5_words, w5_scales, "e2m1").T @ hq + mxq(f64(w6), 0, "e4m3").T @ v
    vote = d * e
    page = np.zeros((N, S))
    page[:, unstriped(offs2)] = np.tile(f64(wgo), (N // 128, 1)) * vote
    z = f64(x0) - page
    y = f64(amp)[:, None] * (1.0 / (1.0 + np.exp(-z)))
    words, scales = planes(y)
    return y, words, scales

@@ -1,0 +1,287 @@
+from contextlib import ExitStack
+
+import concourse.mybir as mybir
+from concourse.masks import make_identity
+
+K, T, S, H, N = 512, 2048, 1024, 1024, 512
+FLOPS = 2 * S * (2 * K * H + 2 * H * N + 2 * K * N)
+
+F32 = mybir.dt.float32
+BF16 = mybir.dt.bfloat16
+I32 = mybir.dt.int32
+U32 = mybir.dt.uint32
+U16 = mybir.dt.uint16
+U8 = mybir.dt.uint8
+FP8 = mybir.dt.float8_e4m3fn_x4
+FP4 = mybir.dt.float4_e2m1fn_x4
+MULT = mybir.AluOpType.mult
+ACT = mybir.ActivationFunctionType
+
+P = 128
+HALF = 512
+WINDOW = 1376
+
+
+def tile_list_herbarium_expert_votes_kernel(
+    tc, tab_words, tab_scales, offs, offs2, w1, w2_words, w2_scales, w3, w4_words, w4_scales,
+    w5_words, w5_scales, w6, wgo, x0, amp, out_0, out_1, out_2,
+):
+    nc = tc.nc
+    with ExitStack() as ctx:
+        keep = ctx.enter_context(tc.tile_pool(name="keep", bufs=1))
+        ring = ctx.enter_context(tc.tile_pool(name="ring", bufs=2))
+        psum = ctx.enter_context(tc.psum_pool(name="psum", bufs=1))
+
+        def held(shape, dtype, name):
+            return keep.tile(shape, dtype, name=name, align_bytes=64)
+
+        taken = {"low": [], "high": []}
+
+        def bank(side, shape):
+            tile = psum.tile(shape, F32, name="bank", tag="%s%d" % (side, len(taken[side]) % 4))
+            taken[side].append(tile)
+            return tile
+
+        def load_scale_rows(queue, plane, rows):
+            for q in range(4):
+                queue.dma_start(out=plane[32 * q : 32 * q + 4].bitcast(I32), in_=rows[4 * q : 4 * q + 4].bitcast(I32))
+
+        idx = keep.tile([P, S // 16], U16, name="idx")
+        idx2 = keep.tile([P, S // 16], U16, name="idx2")
+        tab_w = held([P, T], U32, "tab_w")
+        tab_s = held([P, T], U8, "tab_s")
+        tab_rows = held([P, T], U8, "tab_rows")
+        w2_raw = held([P, 2 * H], U8, "w2_raw")
+        w2_raw_s = held([P, H], U8, "w2_raw_s")
+        w4_w = held([P, N], U32, "w4_w")
+        w4_s = held([P, N], U8, "w4_s")
+        w5_w = held([P, 2, 2 * N], U8, "w5_w")
+        w5_s = held([P, 2, N], U8, "w5_s")
+        w1_raw = [held([P, 4, 512], F32, "w1_raw%d" % g) for g in range(2)]
+        w3_raw = [held([P, 4, N], F32, "w3_raw%d" % g) for g in range(2)]
+        w6_raw = held([P, 4, N], F32, "w6_raw")
+        wgo_sb = held([P, S], F32, "wgo_sb")
+        x0_sb = [held([P, S], F32, "x0_sb%d" % c) for c in range(4)]
+        amp_sb = held([P, 4, 4], F32, "amp_sb")
+        ident = held([P, P], F32, "ident")
+
+        nc.vector.memset(tab_s[:].bitcast(I32), 0)
+        nc.gpsimd.memset(w2_raw_s[:].bitcast(I32), 0)
+        nc.gpsimd.memset(w4_s[:].bitcast(I32), 0)
+        nc.gpsimd.memset(w5_s[:].rearrange("p a n -> p (a n)").bitcast(I32), 0)
+        make_identity(nc, ident[:])
+
+        w1_rows = w1.rearrange("(p j) c -> p j c", j=4)
+        load_scale_rows(nc.sync, tab_rows, tab_scales[0])
+        nc.sync.dma_start(out=tab_w[:].bitcast(I32), in_=tab_words[0].rearrange("p n t -> p (n t)").bitcast(I32))
+        nc.sync.dma_start(out=idx[:], in_=offs)
+        nc.sync.dma_start(out=w1_raw[0][:], in_=w1_rows[:, :, 0:512])
+        nc.sync.dma_start(out=w2_raw[:].bitcast(I32), in_=w2_words[0].bitcast(I32))
+        load_scale_rows(nc.scalar, w2_raw_s, w2_scales[0])
+        nc.sync.dma_start(out=w1_raw[1][:], in_=w1_rows[:, :, 512:1024])
+        for g in range(2):
+            nc.sync.dma_start(out=w3_raw[g][:], in_=w3[512 * g : 512 * (g + 1), :].rearrange("(p j) n -> p j n", j=4))
+        nc.sync.dma_start(out=w6_raw[:], in_=w6.rearrange("(p j) n -> p j n", j=4))
+        nc.sync.dma_start(out=w4_w[:].bitcast(I32), in_=w4_words[0].rearrange("p n t -> p (n t)").bitcast(I32))
+        nc.sync.dma_start(out=w5_w[:].bitcast(I32), in_=w5_words.rearrange("a p b -> p a b").bitcast(I32))
+        load_scale_rows(nc.sync, w4_s, w4_scales[0])
+        load_scale_rows(nc.sync, w5_s, w5_scales.rearrange("a r n -> r a n"))
+        nc.sync.dma_start(out=idx2[:], in_=offs2)
+        nc.sync.dma_start(out=wgo_sb[:], in_=wgo)
+        for c in range(4):
+            nc.sync.dma_start(out=x0_sb[c][:], in_=x0[P * c : P * (c + 1), :])
+        for u in range(4):
+            nc.sync.dma_start(out=amp_sb[32 * u : 32 * (u + 1)], in_=amp.rearrange("(c a t) -> a c t", c=4, t=4))
+
+        for q in range(4):
+            nc.vector.tensor_copy(out=tab_s[32 * q : 32 * q + 4].bitcast(I32), in_=tab_rows[32 * q : 32 * q + 4].bitcast(I32))
+
+        v_w = [held([P, HALF], U32, "v_w%d" % b) for b in range(2)]
+        v_s = {}
+        w1_q = [held([P, 512], U32, "w1_q%d" % g) for g in range(2)]
+        w1_s = [held([P, 512], U8, "w1_s%d" % g) for g in range(2)]
+        w2_w = [held([P, 1024], U8, "w2_w%d" % g) for g in range(2)]
+        w2_s = [held([P, 512], U8, "w2_s%d" % g) for g in range(2)]
+        h_q = [[held([P, HALF], U32, "h_q%d%d" % (g, b)) for b in range(2)] for g in range(2)]
+        h_s = [[held([P, HALF], U8, "h_s%d%d" % (g, b)) for b in range(2)] for g in range(2)]
+
+        def gather(b):
+            cut = idx[:, 32 * b : 32 * (b + 1)]
+            nc.vector.tensor_copy(out=v_w[b][:], in_=tab_w[:].indirect(cut))
+            v_s[b] = keep.tile([P, HALF], U8, name="v_s%d" % b, tag="w1_bf0" if b == 1 else "v_s0", align_bytes=64)
+            nc.vector.tensor_copy(out=v_s[b][:], in_=tab_s[:].indirect(cut))
+
+        def deal_w2(g):
+            nc.vector.tensor_copy(
+                out=w2_w[g][:].bitcast(U16).rearrange("p (t m) -> p t m", t=4),
+                in_=w2_raw[:, 1024 * g : 1024 * (g + 1)].bitcast(U16).rearrange("p (m t) -> p t m", t=4),
+            )
+            nc.vector.tensor_copy(
+                out=w2_s[g][:].rearrange("p (t m) -> p t m", t=4),
+                in_=w2_raw_s[:, 512 * g : 512 * (g + 1)].rearrange("p (m t) -> p t m", t=4),
+            )
+
+        def quantise_w1(g):
+            w1_bf = keep.tile([P, 2048], BF16, name="w1_bf%d" % g, tag="w1_bf%d" % g, align_bytes=64)
+            nc.scalar.copy(
+                out=w1_bf[:].rearrange("p (t m j) -> p m j t", t=4, j=4),
+                in_=w1_raw[g][:].rearrange("p j (m t) -> p m j t", t=4),
+            )
+            nc.vector.quantize_mx(out=w1_q[g][:].bitcast(FP8), scales=w1_s[g][:], in_=w1_bf[:])
+
+        def features(g, b):
+            h_bf = keep.tile([P, HALF, 4], BF16, name="h_bf", tag="h_bf%d" % g, align_bytes=64)
+            for jb in range(4):
+                cols = slice(P * jb, P * (jb + 1))
+                a_ps = bank("low", [P, 4, P])
+                for t in range(4):
+                    nc.tensor.matmul_mx(
+                        out=a_ps[:, t, :],
+                        lhsT=w1_q[g][:, P * t : P * (t + 1)].bitcast(FP8), lhsT_scale=w1_s[g][:, P * t : P * (t + 1)],
+                        rhs=v_w[b][:, cols].bitcast(FP8), rhs_scale=v_s[b][:, cols], start=True, stop=True,
+                    )
+                a_sb = ring.tile([P, P, 4], F32, tag="a_sb", bufs=8)
+                nc.scalar.copy(out=a_sb[:], in_=a_ps[:].rearrange("p t n -> p n t"))
+                b_ps = bank("high", [P, 4, P])
+                for t in range(4):
+                    nc.tensor.matmul_mx(
+                        out=b_ps[:, t, :],
+                        lhsT=w2_w[g][:, 2 * P * t : 2 * P * (t + 1)].bitcast(FP4), lhsT_scale=w2_s[g][:, P * t : P * (t + 1)],
+                        rhs=v_w[b][:, cols].bitcast(FP8), rhs_scale=v_s[b][:, cols], start=True, stop=True,
+                    )
+                nc.vector.tensor_tensor(out=h_bf[:, cols, :], in0=b_ps[:].rearrange("p t n -> p n t"), in1=a_sb[:], op=MULT)
+            nc.vector.quantize_mx(
+                out=h_q[g][b][:].bitcast(FP8), scales=h_s[g][b][:], in_=h_bf[:].rearrange("p n t -> p (n t)")
+            )
+
+        w36_q = [held([P, 3 * P], U32, "w36_q%d" % c) for c in range(4)]
+        w36_s = [held([P, 3 * P], U8, "w36_s%d" % c) for c in range(4)]
+        page = [held([P, WINDOW], F32, "page%d" % c) for c in range(4)]
+        d_neg = {}
+        votes = {}
+        y_q = [held([P, 256], U32, "y_q%d" % c) for c in range(4)]
+        y_s = held([P, 256], U8, "y_s")
+
+        def quantise_w36(c, w36_bf):
+            for s, raw in enumerate((w3_raw[0], w3_raw[1], w6_raw)):
+                nc.scalar.copy(
+                    out=w36_bf[:, 512 * s : 512 * (s + 1)].rearrange("p (a i j) -> p a j i", i=4, j=4),
+                    in_=raw[:, :, P * c : P * (c + 1)].rearrange("p j (a i) -> p a j i", i=4),
+                )
+            nc.vector.quantize_mx(out=w36_q[c][:, 0:256].bitcast(FP8), scales=w36_s[c][:, 0:256], in_=w36_bf[:, 0:1024])
+            nc.vector.quantize_mx(out=w36_q[c][:, 256:384].bitcast(FP8), scales=w36_s[c][:, 256:384], in_=w36_bf[:, 1024:1536])
+
+        def first_factor(c, b):
+            rows = slice(P * c, P * (c + 1))
+            d_ps = bank("low", [P, HALF])
+            nc.tensor.matmul_mx(
+                out=d_ps[:], lhsT=w4_w[:, rows].bitcast(FP8), lhsT_scale=w4_s[:, rows],
+                rhs=v_w[b][:].bitcast(FP8), rhs_scale=v_s[b][:], start=True, stop=False,
+            )
+            for g in range(2):
+                nc.tensor.matmul_mx(
+                    out=d_ps[:], lhsT=w36_q[c][:, P * g : P * (g + 1)].bitcast(FP8), lhsT_scale=w36_s[c][:, P * g : P * (g + 1)],
+                    rhs=h_q[g][b][:].bitcast(FP8), rhs_scale=h_s[g][b][:], start=False, stop=(g == 1),
+                )
+            d_neg[c, b] = ring.tile([P, HALF], F32, name="d_neg", tag="d_neg", bufs=4)
+            nc.scalar.activation(out=d_neg[c, b][:], in_=d_ps[:], func=ACT.Copy, scale=-1.0)
+
+        def vote(c, b):
+            rows = slice(P * c, P * (c + 1))
+            e_ps = bank("high", [P, HALF])
+            nc.tensor.matmul_mx(
+                out=e_ps[:], lhsT=w36_q[c][:, 2 * P : 3 * P].bitcast(FP8), lhsT_scale=w36_s[c][:, 2 * P : 3 * P],
+                rhs=v_w[b][:].bitcast(FP8), rhs_scale=v_s[b][:], start=True, stop=False,
+            )
+            for g in range(2):
+                nc.tensor.matmul_mx(
+                    out=e_ps[:], lhsT=w5_w[:, g, 2 * P * c : 2 * P * (c + 1)].bitcast(FP4), lhsT_scale=w5_s[:, g, rows],
+                    rhs=h_q[g][b][:].bitcast(FP8), rhs_scale=h_s[g][b][:], start=False, stop=(g == 1),
+                )
+            if b == 0:
+                votes[c] = keep.tile([P, S], F32, name="votes", tag="votes%d" % (c % 2), align_bytes=64)
+            nc.vector.tensor_tensor(out=votes[c][:, HALF * b : HALF * (b + 1)], in0=e_ps[:], in1=d_neg[c, b][:], op=MULT)
+
+        def place(c, lo, hi):
+            nc.vector.tensor_tensor(
+                out=page[c][:].indirect(idx2[:, lo // 16 : hi // 16]), in0=votes[c][:, lo:hi], in1=wgo_sb[:, lo:hi], op=MULT
+            )
+
+        def finish(c):
+            y = ring.tile([P, 4, 256], F32, tag="y")
+            y_bf = keep.tile([P, 1024], BF16, name="y_bf", tag="votes%d" % (c % 2), align_bytes=64)
+            for hh in range(2):
+                z_ps = bank("low", [P, 4, P])
+                for src in (x0_sb[c], page[c]):
+                    for u in range(4):
+                        lo = 256 * u + P * hh
+                        nc.tensor.matmul(
+                            out=z_ps[:, u, :], lhsT=src[:, lo : lo + P], rhs=ident[:], is_transpose=True,
+                            start=(src is x0_sb[c] and u == 0), stop=(src is page[c] and u == 3),
+                        )
+                sig = ring.tile([P, 4, P], F32, tag="sig")
+                nc.scalar.activation(
+                    out=sig[:].rearrange("p t q -> p q t"),
+                    in_=z_ps[:].rearrange("p u (a t) -> p (u a) t", t=4),
+                    func=ACT.Sigmoid,
+                )
+                y_ps = bank("high", [P, 4, P])
+                for t in range(4):
+                    nc.tensor.transpose(y_ps[:, t, :], sig[:, t, :], ident[:])
+                cols = slice(P * hh, P * (hh + 1))
+                if c == 3:
+                    nc.vector.tensor_tensor(
+                        out=y[:, :, cols], in0=y_ps[:], in1=amp_sb[:, c, :].unsqueeze(2).to_broadcast([P, 4, P]), op=MULT
+                    )
+                else:
+                    for t in range(4):
+                        nc.scalar.activation(out=y[:, t, cols], in_=y_ps[:, t, :], func=ACT.Copy, scale=amp_sb[:, c, t : t + 1])
+                copy = nc.vector.tensor_copy if (c, hh) == (3, 1) else nc.scalar.copy
+                copy(
+                    out=y_bf[:, 512 * hh : 512 * (hh + 1)].rearrange("p (a i t) -> p a t i", i=4, t=4),
+                    in_=y[:, :, cols].rearrange("p t (a i) -> p a t i", i=4),
+                )
+            rows = out_0[P * c : P * (c + 1), :].rearrange("(a t) m -> a t m", t=4)
+            for u in range(4):
+                nc.sync.dma_start(out=rows[:, :, 256 * u : 256 * (u + 1)], in_=y[32 * u : 32 * (u + 1)])
+            nc.vector.quantize_mx(out=y_q[c][:].bitcast(FP8), scales=y_s[4 * c : P, :], in_=y_bf[:])
+            words = out_1[0, 32 * c : 32 * (c + 1)].rearrange("a m t -> a (m t)").bitcast(I32)
+            for u in range(4):
+                nc.sync.dma_start(out=words[:, 256 * u : 256 * (u + 1)], in_=y_q[c][32 * u : 32 * (u + 1), :].bitcast(I32))
+
+        gather(0)
+        deal_w2(0)
+        quantise_w1(0)
+        gather(1)
+        deal_w2(1)
+        quantise_w1(1)
+        features(0, 0)
+        features(1, 0)
+        features(0, 1)
+        quantise_w36(0, held([P, 1536], BF16, "w36_first")[:])
+        features(1, 1)
+        first_factor(0, 0)
+        w36_rest = keep.tile([P, 3 * 1536], BF16, name="w36_rest", tag="h_bf1", align_bytes=64)
+        for c in range(4):
+            vote(c, 0)
+            if c == 0:
+                place(c, 0, HALF)
+                quantise_w36(1, w36_rest[:, 0:1536])
+                first_factor(0, 1)
+                vote(c, 1)
+                place(c, HALF, S)
+                quantise_w36(2, w36_rest[:, 1536:3072])
+                quantise_w36(3, w36_rest[:, 3072:4608])
+            else:
+                vote(c, 1)
+                place(c, 0, S)
+            if c < 3:
+                first_factor(c + 1, 0)
+                first_factor(c + 1, 1)
+            if c > 0:
+                finish(c - 1)
+        finish(3)
+        for u in range(4):
+            nc.sync.dma_start(
+                out=out_2[0][:, 256 * u : 256 * (u + 1)].bitcast(I32), in_=y_s[32 * u : 32 * u + 16, :].bitcast(I32)
+            )

@@ -42,6 +42,9 @@ def tile_list_herbarium_expert_votes_kernel(
             taken[side].append(tile)
             return tile
 
+        def named_bank(side, number, shape):
+            return psum.tile(shape, F32, name="bank", tag="%s%d" % (side, number))
+
         def load_scale_rows(queue, plane, rows):
             for q in range(4):
                 queue.dma_start(out=plane[32 * q : 32 * q + 4].bitcast(I32), in_=rows[4 * q : 4 * q + 4].bitcast(I32))
@@ -57,7 +60,7 @@ def tile_list_herbarium_expert_votes_kernel(
         w4_s = held([P, N], U8, "w4_s")
         w5_w = held([P, 2, 2 * N], U8, "w5_w")
         w5_s = held([P, 2, N], U8, "w5_s")
-        w1_raw = [held([P, 4, 512], F32, "w1_raw%d" % g) for g in range(2)]
+        w1_raw = [[held([P, 4, 256], F32, "w1_raw%d%d" % (g, half)) for half in range(2)] for g in range(2)]
         w3_raw = [held([P, 4, N], F32, "w3_raw%d" % g) for g in range(2)]
         w6_raw = held([P, 4, N], F32, "w6_raw")
         wgo_sb = held([P, S], F32, "wgo_sb")
@@ -65,6 +68,9 @@ def tile_list_herbarium_expert_votes_kernel(
         amp_sb = held([P, 4, 4], F32, "amp_sb")
         ident = held([P, P], F32, "ident")
 
+        warm = held([P, 2], F32, "warm")
+        nc.gpsimd.memset(warm[:, 0:1], 0.0)
+        nc.scalar.activation(out=warm[:, 1:2], in_=warm[:, 0:1], func=ACT.Sigmoid)
         nc.vector.memset(tab_s[:].bitcast(I32), 0)
         nc.gpsimd.memset(w2_raw_s[:].bitcast(I32), 0)
         nc.gpsimd.memset(w4_s[:].bitcast(I32), 0)
@@ -75,16 +81,19 @@ def tile_list_herbarium_expert_votes_kernel(
         load_scale_rows(nc.sync, tab_rows, tab_scales[0])
         nc.sync.dma_start(out=tab_w[:].bitcast(I32), in_=tab_words[0].rearrange("p n t -> p (n t)").bitcast(I32))
         nc.sync.dma_start(out=idx[:], in_=offs)
-        nc.sync.dma_start(out=w1_raw[0][:], in_=w1_rows[:, :, 0:512])
+        for half in range(2):
+            nc.sync.dma_start(out=w1_raw[0][half][:], in_=w1_rows[:, :, 256 * half : 256 * (half + 1)])
         nc.sync.dma_start(out=w2_raw[:].bitcast(I32), in_=w2_words[0].bitcast(I32))
         load_scale_rows(nc.scalar, w2_raw_s, w2_scales[0])
-        nc.sync.dma_start(out=w1_raw[1][:], in_=w1_rows[:, :, 512:1024])
-        for g in range(2):
-            nc.sync.dma_start(out=w3_raw[g][:], in_=w3[512 * g : 512 * (g + 1), :].rearrange("(p j) n -> p j n", j=4))
-        nc.sync.dma_start(out=w6_raw[:], in_=w6.rearrange("(p j) n -> p j n", j=4))
+        for half in range(2):
+            nc.sync.dma_start(out=w1_raw[1][half][:], in_=w1_rows[:, :, 512 + 256 * half : 512 + 256 * (half + 1)])
+        w3_rows = w3.rearrange("(g p j) n -> g p j n", g=2, j=4)
+        nc.sync.dma_start(out=w3_raw[0][:], in_=w3_rows[0])
         nc.sync.dma_start(out=w4_w[:].bitcast(I32), in_=w4_words[0].rearrange("p n t -> p (n t)").bitcast(I32))
-        nc.sync.dma_start(out=w5_w[:].bitcast(I32), in_=w5_words.rearrange("a p b -> p a b").bitcast(I32))
         load_scale_rows(nc.sync, w4_s, w4_scales[0])
+        nc.sync.dma_start(out=w3_raw[1][:], in_=w3_rows[1])
+        nc.sync.dma_start(out=w5_w[:].bitcast(I32), in_=w5_words.rearrange("a p b -> p a b").bitcast(I32))
+        nc.sync.dma_start(out=w6_raw[:], in_=w6.rearrange("(p j) n -> p j n", j=4))
         load_scale_rows(nc.sync, w5_s, w5_scales.rearrange("a r n -> r a n"))
         nc.sync.dma_start(out=idx2[:], in_=offs2)
         nc.sync.dma_start(out=wgo_sb[:], in_=wgo)
@@ -123,10 +132,11 @@ def tile_list_herbarium_expert_votes_kernel(
 
         def quantise_w1(g):
             w1_bf = keep.tile([P, 2048], BF16, name="w1_bf%d" % g, tag="w1_bf%d" % g, align_bytes=64)
-            nc.scalar.copy(
-                out=w1_bf[:].rearrange("p (t m j) -> p m j t", t=4, j=4),
-                in_=w1_raw[g][:].rearrange("p j (m t) -> p m j t", t=4),
-            )
+            dealt = w1_bf[:].rearrange("p (t m j) -> p m j t", t=4, j=4)
+            for half in range(2):
+                nc.scalar.copy(
+                    out=dealt[:, 64 * half : 64 * (half + 1)], in_=w1_raw[g][half][:].rearrange("p j (m t) -> p m j t", t=4)
+                )
             nc.vector.quantize_mx(out=w1_q[g][:].bitcast(FP8), scales=w1_s[g][:], in_=w1_bf[:])
 
         def features(g, b):
@@ -156,13 +166,14 @@ def tile_list_herbarium_expert_votes_kernel(
 
         w36_q = [held([P, 3 * P], U32, "w36_q%d" % c) for c in range(4)]
         w36_s = [held([P, 3 * P], U8, "w36_s%d" % c) for c in range(4)]
-        page = [held([P, WINDOW], F32, "page%d" % c) for c in range(4)]
+        page = {}
         d_neg = {}
         votes = {}
-        y_q = [held([P, 256], U32, "y_q%d" % c) for c in range(4)]
+        y_bf = [keep.tile([P, 1024], BF16, name="y_bf%d" % c, tag="y_bf%d" % c, align_bytes=64) for c in range(4)]
         y_s = held([P, 256], U8, "y_s")
 
-        def quantise_w36(c, w36_bf):
+        def quantise_w36(c, tag):
+            w36_bf = keep.tile([P, 1536], BF16, name="w36_bf", tag=tag, align_bytes=64)
             for s, raw in enumerate((w3_raw[0], w3_raw[1], w6_raw)):
                 nc.scalar.copy(
                     out=w36_bf[:, 512 * s : 512 * (s + 1)].rearrange("p (a i j) -> p a j i", i=4, j=4),
@@ -173,7 +184,7 @@ def tile_list_herbarium_expert_votes_kernel(
 
         def first_factor(c, b):
             rows = slice(P * c, P * (c + 1))
-            d_ps = bank("low", [P, HALF])
+            d_ps = named_bank("low", b, [P, HALF])
             nc.tensor.matmul_mx(
                 out=d_ps[:], lhsT=w4_w[:, rows].bitcast(FP8), lhsT_scale=w4_s[:, rows],
                 rhs=v_w[b][:].bitcast(FP8), rhs_scale=v_s[b][:], start=True, stop=False,
@@ -183,12 +194,15 @@ def tile_list_herbarium_expert_votes_kernel(
                     out=d_ps[:], lhsT=w36_q[c][:, P * g : P * (g + 1)].bitcast(FP8), lhsT_scale=w36_s[c][:, P * g : P * (g + 1)],
                     rhs=h_q[g][b][:].bitcast(FP8), rhs_scale=h_s[g][b][:], start=False, stop=(g == 1),
                 )
-            d_neg[c, b] = ring.tile([P, HALF], F32, name="d_neg", tag="d_neg", bufs=4)
+            if c == 0:
+                d_neg[c, b] = keep.tile([P, HALF], F32, name="d_neg", tag="late%d" % b, align_bytes=64)
+            else:
+                d_neg[c, b] = ring.tile([P, HALF], F32, name="d_neg", tag="d_neg", bufs=4)
             nc.scalar.activation(out=d_neg[c, b][:], in_=d_ps[:], func=ACT.Copy, scale=-1.0)
 
         def vote(c, b):
             rows = slice(P * c, P * (c + 1))
-            e_ps = bank("high", [P, HALF])
+            e_ps = named_bank("high", b, [P, HALF])
             nc.tensor.matmul_mx(
                 out=e_ps[:], lhsT=w36_q[c][:, 2 * P : 3 * P].bitcast(FP8), lhsT_scale=w36_s[c][:, 2 * P : 3 * P],
                 rhs=v_w[b][:].bitcast(FP8), rhs_scale=v_s[b][:], start=True, stop=False,
@@ -200,18 +214,21 @@ def tile_list_herbarium_expert_votes_kernel(
                 )
             if b == 0:
                 votes[c] = keep.tile([P, S], F32, name="votes", tag="votes%d" % (c % 2), align_bytes=64)
+            elif c == 0:
+                votes[c] = keep.tile([P, S], F32, name="votes", tag="late0", align_bytes=64)
             nc.vector.tensor_tensor(out=votes[c][:, HALF * b : HALF * (b + 1)], in0=e_ps[:], in1=d_neg[c, b][:], op=MULT)
 
         def place(c, lo, hi):
+            if lo == 0:
+                page[c] = keep.tile([P, WINDOW], F32, name="page", tag={1: "late1", 2: "late0"}.get(c, "page%d" % c), align_bytes=64)
             nc.vector.tensor_tensor(
                 out=page[c][:].indirect(idx2[:, lo // 16 : hi // 16]), in0=votes[c][:, lo:hi], in1=wgo_sb[:, lo:hi], op=MULT
             )
 
         def finish(c):
             y = ring.tile([P, 4, 256], F32, tag="y")
-            y_bf = keep.tile([P, 1024], BF16, name="y_bf", tag="votes%d" % (c % 2), align_bytes=64)
             for hh in range(2):
-                z_ps = bank("low", [P, 4, P])
+                z_ps = named_bank(("low", "high")[c % 2], 3 - hh, [P, 4, P])
                 for src in (x0_sb[c], page[c]):
                     for u in range(4):
                         lo = 256 * u + P * hh
@@ -219,13 +236,18 @@ def tile_list_herbarium_expert_votes_kernel(
                             out=z_ps[:, u, :], lhsT=src[:, lo : lo + P], rhs=ident[:], is_transpose=True,
                             start=(src is x0_sb[c] and u == 0), stop=(src is page[c] and u == 3),
                         )
-                sig = ring.tile([P, 4, P], F32, tag="sig")
+                if hh == 1 and c < 2:
+                    sig = keep.tile([P, 4, P], F32, name="sig", tag="votes%d" % c, align_bytes=64)
+                elif (c, hh) == (3, 0):
+                    sig = keep.tile([P, 4, P], F32, name="sig", tag="y_bf2", align_bytes=64)
+                else:
+                    sig = ring.tile([P, 4, P], F32, name="sig", tag="sig")
                 nc.scalar.activation(
                     out=sig[:].rearrange("p t q -> p q t"),
                     in_=z_ps[:].rearrange("p u (a t) -> p (u a) t", t=4),
                     func=ACT.Sigmoid,
                 )
-                y_ps = bank("high", [P, 4, P])
+                y_ps = named_bank(("high", "low")[c % 2], 2 + hh, [P, 4, P])
                 for t in range(4):
                     nc.tensor.transpose(y_ps[:, t, :], sig[:, t, :], ident[:])
                 cols = slice(P * hh, P * (hh + 1))
@@ -238,16 +260,28 @@ def tile_list_herbarium_expert_votes_kernel(
                         nc.scalar.activation(out=y[:, t, cols], in_=y_ps[:, t, :], func=ACT.Copy, scale=amp_sb[:, c, t : t + 1])
                 copy = nc.vector.tensor_copy if (c, hh) == (3, 1) else nc.scalar.copy
                 copy(
-                    out=y_bf[:, 512 * hh : 512 * (hh + 1)].rearrange("p (a i t) -> p a t i", i=4, t=4),
+                    out=y_bf[c][:, 512 * hh : 512 * (hh + 1)].rearrange("p (a i t) -> p a t i", i=4, t=4),
                     in_=y[:, :, cols].rearrange("p t (a i) -> p a t i", i=4),
                 )
             rows = out_0[P * c : P * (c + 1), :].rearrange("(a t) m -> a t m", t=4)
             for u in range(4):
                 nc.sync.dma_start(out=rows[:, :, 256 * u : 256 * (u + 1)], in_=y[32 * u : 32 * (u + 1)])
-            nc.vector.quantize_mx(out=y_q[c][:].bitcast(FP8), scales=y_s[4 * c : P, :], in_=y_bf[:])
-            words = out_1[0, 32 * c : 32 * (c + 1)].rearrange("a m t -> a (m t)").bitcast(I32)
+
+        def store_words(c):
+            y_q = held([P, 256], U32, "y_q%d" % c)
+            nc.vector.quantize_mx(out=y_q[:].bitcast(FP8), scales=y_s[4 * c : P, :], in_=y_bf[c][:])
+            nc.sync.dma_start(
+                out=out_1[0, 32 * c : 32 * (c + 1)].rearrange("a (u m) t -> u a (m t)", u=4).bitcast(I32), in_=y_q[:].bitcast(I32)
+            )
+
+        def store_planes(tiles, y_q):
+            for c in tiles:
+                nc.vector.quantize_mx(out=y_q[:, c, :].bitcast(FP8), scales=y_s[4 * c : P, :], in_=y_bf[c][:])
+            words = out_1[0].rearrange("(c a) m t -> a c (m t)", c=4).bitcast(I32)
             for u in range(4):
-                nc.sync.dma_start(out=words[:, 256 * u : 256 * (u + 1)], in_=y_q[c][32 * u : 32 * (u + 1), :].bitcast(I32))
+                nc.sync.dma_start(
+                    out=words[:, 0:3, 256 * u : 256 * (u + 1)], in_=y_q[32 * u : 32 * (u + 1)].bitcast(I32)
+                )
 
         gather(0)
         deal_w2(0)
@@ -257,30 +291,33 @@ def tile_list_herbarium_expert_votes_kernel(
         quantise_w1(1)
         features(0, 0)
         features(1, 0)
+        quantise_w36(0, "w36_first")
         features(0, 1)
-        quantise_w36(0, held([P, 1536], BF16, "w36_first")[:])
         features(1, 1)
         first_factor(0, 0)
-        w36_rest = keep.tile([P, 3 * 1536], BF16, name="w36_rest", tag="h_bf1", align_bytes=64)
         for c in range(4):
             vote(c, 0)
             if c == 0:
                 place(c, 0, HALF)
-                quantise_w36(1, w36_rest[:, 0:1536])
+                quantise_w36(1, "late0")
                 first_factor(0, 1)
                 vote(c, 1)
                 place(c, HALF, S)
-                quantise_w36(2, w36_rest[:, 1536:3072])
-                quantise_w36(3, w36_rest[:, 3072:4608])
             else:
                 vote(c, 1)
                 place(c, 0, S)
             if c < 3:
                 first_factor(c + 1, 0)
                 first_factor(c + 1, 1)
+            if c == 0:
+                quantise_w36(2, "late1")
             if c > 0:
                 finish(c - 1)
+            if c == 1:
+                quantise_w36(3, "late0")
+        store_planes((2, 1, 0), keep.tile([P, 3, 256], U32, name="y_q_early", tag="votes1", align_bytes=64))
         finish(3)
+        store_words(3)
         for u in range(4):
             nc.sync.dma_start(
                 out=out_2[0][:, 256 * u : 256 * (u + 1)].bitcast(I32), in_=y_s[32 * u : 32 * u + 16, :].bitcast(I32)

@@ -61,8 +61,8 @@ def tile_list_herbarium_expert_votes_kernel(
         w5_w = held([P, 2, 2 * N], U8, "w5_w")
         w5_s = held([P, 2, N], U8, "w5_s")
         w1_raw = [[held([P, 4, 256], F32, "w1_raw%d%d" % (g, half)) for half in range(2)] for g in range(2)]
-        w3_raw = [held([P, 4, N], F32, "w3_raw%d" % g) for g in range(2)]
-        w6_raw = held([P, 4, N], F32, "w6_raw")
+        w36_first = [held([P, 4, P], F32, "w36_first%d" % s) for s in range(3)]
+        w36_rest = [held([P, 4, N - P], F32, "w36_rest%d" % s) for s in range(3)]
         wgo_sb = held([P, S], F32, "wgo_sb")
         x0_sb = [held([P, S], F32, "x0_sb%d" % c) for c in range(4)]
         amp_sb = held([P, 4, 4], F32, "amp_sb")
@@ -88,13 +88,16 @@ def tile_list_herbarium_expert_votes_kernel(
         for half in range(2):
             nc.sync.dma_start(out=w1_raw[1][half][:], in_=w1_rows[:, :, 512 + 256 * half : 512 + 256 * (half + 1)])
         w3_rows = w3.rearrange("(g p j) n -> g p j n", g=2, j=4)
-        nc.sync.dma_start(out=w3_raw[0][:], in_=w3_rows[0])
+        w36_rows = (w3_rows[0], w3_rows[1], w6.rearrange("(p j) n -> p j n", j=4))
+        for s in range(3):
+            nc.sync.dma_start(out=w36_first[s][:], in_=w36_rows[s][:, :, 0:P])
         nc.sync.dma_start(out=w4_w[:].bitcast(I32), in_=w4_words[0].rearrange("p n t -> p (n t)").bitcast(I32))
-        load_scale_rows(nc.sync, w4_s, w4_scales[0])
-        nc.sync.dma_start(out=w3_raw[1][:], in_=w3_rows[1])
         nc.sync.dma_start(out=w5_w[:].bitcast(I32), in_=w5_words.rearrange("a p b -> p a b").bitcast(I32))
-        nc.sync.dma_start(out=w6_raw[:], in_=w6.rearrange("(p j) n -> p j n", j=4))
+        load_scale_rows(nc.sync, w4_s, w4_scales[0])
+        nc.sync.dma_start(out=w36_rest[0][:], in_=w36_rows[0][:, :, P:N])
         load_scale_rows(nc.sync, w5_s, w5_scales.rearrange("a r n -> r a n"))
+        for s in range(1, 3):
+            nc.sync.dma_start(out=w36_rest[s][:], in_=w36_rows[s][:, :, P:N])
         nc.sync.dma_start(out=idx2[:], in_=offs2)
         nc.sync.dma_start(out=wgo_sb[:], in_=wgo)
         for c in range(4):
@@ -111,7 +114,8 @@ def tile_list_herbarium_expert_votes_kernel(
         w1_s = [held([P, 512], U8, "w1_s%d" % g) for g in range(2)]
         w2_w = [held([P, 1024], U8, "w2_w%d" % g) for g in range(2)]
         w2_s = [held([P, 512], U8, "w2_s%d" % g) for g in range(2)]
-        h_q = [[held([P, HALF], U32, "h_q%d%d" % (g, b)) for b in range(2)] for g in range(2)]
+        h_q = [[None, None], [None, None]]
+        h_bf = {}
         h_s = [[held([P, HALF], U8, "h_s%d%d" % (g, b)) for b in range(2)] for g in range(2)]
 
         def gather(b):
@@ -139,8 +143,8 @@ def tile_list_herbarium_expert_votes_kernel(
                 )
             nc.vector.quantize_mx(out=w1_q[g][:].bitcast(FP8), scales=w1_s[g][:], in_=w1_bf[:])
 
-        def features(g, b):
-            h_bf = keep.tile([P, HALF, 4], BF16, name="h_bf", tag="h_bf%d" % g, align_bytes=64)
+        def features(g, b, before):
+            h_bf[g, b] = keep.tile([P, HALF, 4], BF16, name="h_bf", tag="h_bf%d" % g, align_bytes=64)
             for jb in range(4):
                 cols = slice(P * jb, P * (jb + 1))
                 a_ps = bank("low", [P, 4, P])
@@ -150,7 +154,10 @@ def tile_list_herbarium_expert_votes_kernel(
                         lhsT=w1_q[g][:, P * t : P * (t + 1)].bitcast(FP8), lhsT_scale=w1_s[g][:, P * t : P * (t + 1)],
                         rhs=v_w[b][:, cols].bitcast(FP8), rhs_scale=v_s[b][:, cols], start=True, stop=True,
                     )
-                a_sb = ring.tile([P, P, 4], F32, tag="a_sb", bufs=8)
+                if jb == 0 and before:
+                    a_sb = keep.tile([P, P, 4], F32, name="a_sb", tag="h_q%d%d" % before, align_bytes=64)
+                else:
+                    a_sb = ring.tile([P, P, 4], F32, name="a_sb", tag="a_sb", bufs=8)
                 nc.scalar.copy(out=a_sb[:], in_=a_ps[:].rearrange("p t n -> p n t"))
                 b_ps = bank("high", [P, 4, P])
                 for t in range(4):
@@ -159,9 +166,14 @@ def tile_list_herbarium_expert_votes_kernel(
                         lhsT=w2_w[g][:, 2 * P * t : 2 * P * (t + 1)].bitcast(FP4), lhsT_scale=w2_s[g][:, P * t : P * (t + 1)],
                         rhs=v_w[b][:, cols].bitcast(FP8), rhs_scale=v_s[b][:, cols], start=True, stop=True,
                     )
-                nc.vector.tensor_tensor(out=h_bf[:, cols, :], in0=b_ps[:].rearrange("p t n -> p n t"), in1=a_sb[:], op=MULT)
+                nc.vector.tensor_tensor(out=h_bf[g, b][:, cols, :], in0=b_ps[:].rearrange("p t n -> p n t"), in1=a_sb[:], op=MULT)
+                if jb == 0 and before:
+                    quantise_h(*before)
+
+        def quantise_h(g, b):
+            h_q[g][b] = keep.tile([P, HALF], U32, name="h_q", tag="h_q%d%d" % (g, b), align_bytes=64)
             nc.vector.quantize_mx(
-                out=h_q[g][b][:].bitcast(FP8), scales=h_s[g][b][:], in_=h_bf[:].rearrange("p n t -> p (n t)")
+                out=h_q[g][b][:].bitcast(FP8), scales=h_s[g][b][:], in_=h_bf[g, b][:].rearrange("p n t -> p (n t)")
             )
 
         w36_q = [held([P, 3 * P], U32, "w36_q%d" % c) for c in range(4)]
@@ -174,17 +186,18 @@ def tile_list_herbarium_expert_votes_kernel(
 
         def quantise_w36(c, tag):
             w36_bf = keep.tile([P, 1536], BF16, name="w36_bf", tag=tag, align_bytes=64)
-            for s, raw in enumerate((w3_raw[0], w3_raw[1], w6_raw)):
+            for s in range(3):
+                raw = w36_first[s][:] if c == 0 else w36_rest[s][:, :, P * (c - 1) : P * c]
                 nc.scalar.copy(
                     out=w36_bf[:, 512 * s : 512 * (s + 1)].rearrange("p (a i j) -> p a j i", i=4, j=4),
-                    in_=raw[:, :, P * c : P * (c + 1)].rearrange("p j (a i) -> p a j i", i=4),
+                    in_=raw.rearrange("p j (a i) -> p a j i", i=4),
                 )
             nc.vector.quantize_mx(out=w36_q[c][:, 0:256].bitcast(FP8), scales=w36_s[c][:, 0:256], in_=w36_bf[:, 0:1024])
             nc.vector.quantize_mx(out=w36_q[c][:, 256:384].bitcast(FP8), scales=w36_s[c][:, 256:384], in_=w36_bf[:, 1024:1536])
 
         def first_factor(c, b):
             rows = slice(P * c, P * (c + 1))
-            d_ps = named_bank("low", b, [P, HALF])
+            d_ps = named_bank("high", 0, [P, HALF]) if (c, b) == (0, 1) else named_bank("low", b, [P, HALF])
             nc.tensor.matmul_mx(
                 out=d_ps[:], lhsT=w4_w[:, rows].bitcast(FP8), lhsT_scale=w4_s[:, rows],
                 rhs=v_w[b][:].bitcast(FP8), rhs_scale=v_s[b][:], start=True, stop=False,
@@ -195,14 +208,14 @@ def tile_list_herbarium_expert_votes_kernel(
                     rhs=h_q[g][b][:].bitcast(FP8), rhs_scale=h_s[g][b][:], start=False, stop=(g == 1),
                 )
             if c == 0:
-                d_neg[c, b] = keep.tile([P, HALF], F32, name="d_neg", tag="late%d" % b, align_bytes=64)
+                d_neg[c, b] = keep.tile([P, HALF], F32, name="d_neg", tag=("h_q11", "late1")[b], align_bytes=64)
             else:
                 d_neg[c, b] = ring.tile([P, HALF], F32, name="d_neg", tag="d_neg", bufs=4)
             nc.scalar.activation(out=d_neg[c, b][:], in_=d_ps[:], func=ACT.Copy, scale=-1.0)
 
         def vote(c, b):
             rows = slice(P * c, P * (c + 1))
-            e_ps = named_bank("high", b, [P, HALF])
+            e_ps = named_bank("low", 0, [P, HALF]) if (c, b) == (0, 1) else named_bank("high", b, [P, HALF])
             nc.tensor.matmul_mx(
                 out=e_ps[:], lhsT=w36_q[c][:, 2 * P : 3 * P].bitcast(FP8), lhsT_scale=w36_s[c][:, 2 * P : 3 * P],
                 rhs=v_w[b][:].bitcast(FP8), rhs_scale=v_s[b][:], start=True, stop=False,
@@ -215,18 +228,20 @@ def tile_list_herbarium_expert_votes_kernel(
             if b == 0:
                 votes[c] = keep.tile([P, S], F32, name="votes", tag="votes%d" % (c % 2), align_bytes=64)
             elif c == 0:
-                votes[c] = keep.tile([P, S], F32, name="votes", tag="late0", align_bytes=64)
+                votes[c] = keep.tile([P, S], F32, name="votes", tag="h_bf1", align_bytes=64)
             nc.vector.tensor_tensor(out=votes[c][:, HALF * b : HALF * (b + 1)], in0=e_ps[:], in1=d_neg[c, b][:], op=MULT)
 
         def place(c, lo, hi):
             if lo == 0:
-                page[c] = keep.tile([P, WINDOW], F32, name="page", tag={1: "late1", 2: "late0"}.get(c, "page%d" % c), align_bytes=64)
+                page[c] = keep.tile([P, WINDOW], F32, name="page", tag={1: "late1", 2: "h_bf1"}.get(c, "page%d" % c), align_bytes=64)
             nc.vector.tensor_tensor(
                 out=page[c][:].indirect(idx2[:, lo // 16 : hi // 16]), in0=votes[c][:, lo:hi], in1=wgo_sb[:, lo:hi], op=MULT
             )
 
         def finish(c):
+            last = c == 3
             y = ring.tile([P, 4, 256], F32, tag="y")
+            y_ps = [named_bank(("high", "low")[c % 2], 2 + i, [P, 512]) for i in range(2)]
             for hh in range(2):
                 z_ps = named_bank(("low", "high")[c % 2], 3 - hh, [P, 4, P])
                 for src in (x0_sb[c], page[c]):
@@ -238,7 +253,7 @@ def tile_list_herbarium_expert_votes_kernel(
                         )
                 if hh == 1 and c < 2:
                     sig = keep.tile([P, 4, P], F32, name="sig", tag="votes%d" % c, align_bytes=64)
-                elif (c, hh) == (3, 0):
+                elif last and hh == 0:
                     sig = keep.tile([P, 4, P], F32, name="sig", tag="y_bf2", align_bytes=64)
                 else:
                     sig = ring.tile([P, 4, P], F32, name="sig", tag="sig")
@@ -247,21 +262,30 @@ def tile_list_herbarium_expert_votes_kernel(
                     in_=z_ps[:].rearrange("p u (a t) -> p (u a) t", t=4),
                     func=ACT.Sigmoid,
                 )
-                y_ps = named_bank(("high", "low")[c % 2], 2 + hh, [P, 4, P])
                 for t in range(4):
-                    nc.tensor.transpose(y_ps[:, t, :], sig[:, t, :], ident[:])
-                cols = slice(P * hh, P * (hh + 1))
-                if c == 3:
+                    if last:
+                        spot = y_ps[hh][:, P * t : P * (t + 1)]
+                    else:
+                        spot = y_ps[t // 2][:, 256 * (t % 2) + P * hh : 256 * (t % 2) + P * (hh + 1)]
+                    nc.tensor.transpose(spot, sig[:, t, :], ident[:])
+                if last:
+                    cols = slice(P * hh, P * (hh + 1))
                     nc.vector.tensor_tensor(
-                        out=y[:, :, cols], in0=y_ps[:], in1=amp_sb[:, c, :].unsqueeze(2).to_broadcast([P, 4, P]), op=MULT
+                        out=y[:, :, cols], in0=y_ps[hh][:].rearrange("p (t m) -> p t m", t=4),
+                        in1=amp_sb[:, c, :].unsqueeze(2).to_broadcast([P, 4, P]), op=MULT,
                     )
-                else:
-                    for t in range(4):
-                        nc.scalar.activation(out=y[:, t, cols], in_=y_ps[:, t, :], func=ACT.Copy, scale=amp_sb[:, c, t : t + 1])
-                copy = nc.vector.tensor_copy if (c, hh) == (3, 1) else nc.scalar.copy
-                copy(
-                    out=y_bf[c][:, 512 * hh : 512 * (hh + 1)].rearrange("p (a i t) -> p a t i", i=4, t=4),
-                    in_=y[:, :, cols].rearrange("p t (a i) -> p a t i", i=4),
+                    (nc.scalar.copy, nc.vector.tensor_copy)[hh](
+                        out=y_bf[c][:, 512 * hh : 512 * (hh + 1)].rearrange("p (a i t) -> p a t i", i=4, t=4),
+                        in_=y[:, :, cols].rearrange("p t (a i) -> p a t i", i=4),
+                    )
+            if not last:
+                for t in range(4):
+                    nc.scalar.activation(
+                        out=y[:, t, :], in_=y_ps[t // 2][:, 256 * (t % 2) : 256 * (t % 2 + 1)], func=ACT.Copy,
+                        scale=amp_sb[:, c, t : t + 1],
+                    )
+                nc.scalar.copy(
+                    out=y_bf[c][:].rearrange("p (a i t) -> p a t i", i=4, t=4), in_=y[:].rearrange("p t (a i) -> p a t i", i=4)
                 )
             rows = out_0[P * c : P * (c + 1), :].rearrange("(a t) m -> a t m", t=4)
             for u in range(4):
@@ -289,17 +313,18 @@ def tile_list_herbarium_expert_votes_kernel(
         gather(1)
         deal_w2(1)
         quantise_w1(1)
-        features(0, 0)
-        features(1, 0)
-        quantise_w36(0, "w36_first")
-        features(0, 1)
-        features(1, 1)
+        features(0, 0, None)
+        quantise_w36(0, "w36_bf0")
+        features(1, 0, (0, 0))
+        features(0, 1, (1, 0))
+        features(1, 1, (0, 1))
         first_factor(0, 0)
         for c in range(4):
             vote(c, 0)
             if c == 0:
+                quantise_h(1, 1)
                 place(c, 0, HALF)
-                quantise_w36(1, "late0")
+                quantise_w36(1, "h_bf1")
                 first_factor(0, 1)
                 vote(c, 1)
                 place(c, HALF, S)
@@ -314,7 +339,7 @@ def tile_list_herbarium_expert_votes_kernel(
             if c > 0:
                 finish(c - 1)
             if c == 1:
-                quantise_w36(3, "late0")
+                quantise_w36(3, "h_bf1")
         store_planes((2, 1, 0), keep.tile([P, 3, 256], U32, name="y_q_early", tag="votes1", align_bytes=64))
         finish(3)
         store_words(3)

@@ -15,6 +15,7 @@ U8 = mybir.dt.uint8
 FP8 = mybir.dt.float8_e4m3fn_x4
 FP4 = mybir.dt.float4_e2m1fn_x4
 MULT = mybir.AluOpType.mult
+ADD = mybir.AluOpType.add
 ACT = mybir.ActivationFunctionType
 
 P = 128
@@ -53,14 +54,16 @@ def tile_list_herbarium_expert_votes_kernel(
         idx2 = keep.tile([P, S // 16], U16, name="idx2")
         tab_w = held([P, T], U32, "tab_w")
         tab_s = held([P, T], U8, "tab_s")
-        tab_rows = held([P, T], U8, "tab_rows")
         w2_raw = held([P, 2 * H], U8, "w2_raw")
         w2_raw_s = held([P, H], U8, "w2_raw_s")
         w4_w = held([P, N], U32, "w4_w")
         w4_s = held([P, N], U8, "w4_s")
         w5_w = held([P, 2, 2 * N], U8, "w5_w")
         w5_s = held([P, 2, N], U8, "w5_s")
-        w1_raw = [[held([P, 4, 256], F32, "w1_raw%d%d" % (g, half)) for half in range(2)] for g in range(2)]
+        w1_raw = [
+            [keep.tile([P, 4, 256], F32, name="w1_raw", tag="w1_raw%d%d" % (g, half), align_bytes=64) for half in range(2)]
+            for g in range(2)
+        ]
         w36_first = [held([P, 4, P], F32, "w36_first%d" % s) for s in range(3)]
         w36_rest = [held([P, 4, N - P], F32, "w36_rest%d" % s) for s in range(3)]
         wgo_sb = held([P, S], F32, "wgo_sb")
@@ -68,23 +71,24 @@ def tile_list_herbarium_expert_votes_kernel(
         amp_sb = held([P, 4, 4], F32, "amp_sb")
         ident = held([P, P], F32, "ident")
 
-        warm = held([P, 2], F32, "warm")
-        nc.gpsimd.memset(warm[:, 0:1], 0.0)
-        nc.scalar.activation(out=warm[:, 1:2], in_=warm[:, 0:1], func=ACT.Sigmoid)
-        nc.vector.memset(tab_s[:].bitcast(I32), 0)
+        amp_last = held([P, 1], F32, "amp_last")
         nc.gpsimd.memset(w2_raw_s[:].bitcast(I32), 0)
         nc.gpsimd.memset(w4_s[:].bitcast(I32), 0)
         nc.gpsimd.memset(w5_s[:].rearrange("p a n -> p (a n)").bitcast(I32), 0)
         make_identity(nc, ident[:])
 
         w1_rows = w1.rearrange("(p j) c -> p j c", j=4)
-        load_scale_rows(nc.sync, tab_rows, tab_scales[0])
-        nc.sync.dma_start(out=tab_w[:].bitcast(I32), in_=tab_words[0].rearrange("p n t -> p (n t)").bitcast(I32))
         nc.sync.dma_start(out=idx[:], in_=offs)
+        for q in range(4):
+            nc.sync.dma_start(
+                out=tab_s[32 * q : 32 * (q + 1)].bitcast(I32),
+                in_=tab_scales[0][4 * q : 4 * q + 4].bitcast(I32).unsqueeze(0).to_broadcast([8, 4, T // 4]),
+            )
         for half in range(2):
             nc.sync.dma_start(out=w1_raw[0][half][:], in_=w1_rows[:, :, 256 * half : 256 * (half + 1)])
         nc.sync.dma_start(out=w2_raw[:].bitcast(I32), in_=w2_words[0].bitcast(I32))
-        load_scale_rows(nc.scalar, w2_raw_s, w2_scales[0])
+        load_scale_rows(nc.sync, w2_raw_s, w2_scales[0])
+        nc.sync.dma_start(out=tab_w[:].bitcast(I32), in_=tab_words[0].rearrange("p n t -> p (n t)").bitcast(I32))
         for half in range(2):
             nc.sync.dma_start(out=w1_raw[1][half][:], in_=w1_rows[:, :, 512 + 256 * half : 512 + 256 * (half + 1)])
         w3_rows = w3.rearrange("(g p j) n -> g p j n", g=2, j=4)
@@ -104,12 +108,11 @@ def tile_list_herbarium_expert_votes_kernel(
             nc.sync.dma_start(out=x0_sb[c][:], in_=x0[P * c : P * (c + 1), :])
         for u in range(4):
             nc.sync.dma_start(out=amp_sb[32 * u : 32 * (u + 1)], in_=amp.rearrange("(c a t) -> a c t", c=4, t=4))
-
-        for q in range(4):
-            nc.vector.tensor_copy(out=tab_s[32 * q : 32 * q + 4].bitcast(I32), in_=tab_rows[32 * q : 32 * q + 4].bitcast(I32))
+        nc.sync.dma_start(out=amp_last[:], in_=amp[N - P : N].unsqueeze(1))
 
         v_w = [held([P, HALF], U32, "v_w%d" % b) for b in range(2)]
-        v_s = {}
+        v_s_all = held([P, S], U8, "v_s_all")
+        v_s = [v_s_all[:, HALF * b : HALF * (b + 1)] for b in range(2)]
         w1_q = [held([P, 512], U32, "w1_q%d" % g) for g in range(2)]
         w1_s = [held([P, 512], U8, "w1_s%d" % g) for g in range(2)]
         w2_w = [held([P, 1024], U8, "w2_w%d" % g) for g in range(2)]
@@ -118,11 +121,9 @@ def tile_list_herbarium_expert_votes_kernel(
         h_bf = {}
         h_s = [[held([P, HALF], U8, "h_s%d%d" % (g, b)) for b in range(2)] for g in range(2)]
 
-        def gather(b):
-            cut = idx[:, 32 * b : 32 * (b + 1)]
-            nc.vector.tensor_copy(out=v_w[b][:], in_=tab_w[:].indirect(cut))
-            v_s[b] = keep.tile([P, HALF], U8, name="v_s%d" % b, tag="w1_bf0" if b == 1 else "v_s0", align_bytes=64)
-            nc.vector.tensor_copy(out=v_s[b][:], in_=tab_s[:].indirect(cut))
+        def gather(lo, hi):
+            b = lo // HALF
+            nc.vector.tensor_copy(out=v_w[b][:, lo - HALF * b : hi - HALF * b], in_=tab_w[:].indirect(idx[:, lo // 16 : hi // 16]))
 
         def deal_w2(g):
             nc.vector.tensor_copy(
@@ -134,17 +135,19 @@ def tile_list_herbarium_expert_votes_kernel(
                 in_=w2_raw_s[:, 512 * g : 512 * (g + 1)].rearrange("p (m t) -> p t m", t=4),
             )
 
+        w1_bf = [held([P, 2048], BF16, "w1_bf%d" % g) for g in range(2)]
+
+        def cast_w1(g, half):
+            dealt = w1_bf[g][:].rearrange("p (t m j) -> p m j t", t=4, j=4)
+            (nc.vector.tensor_copy if (g, half) == (1, 1) else nc.scalar.copy)(
+                out=dealt[:, 64 * half : 64 * (half + 1)], in_=w1_raw[g][half][:].rearrange("p j (m t) -> p m j t", t=4)
+            )
+
         def quantise_w1(g):
-            w1_bf = keep.tile([P, 2048], BF16, name="w1_bf%d" % g, tag="w1_bf%d" % g, align_bytes=64)
-            dealt = w1_bf[:].rearrange("p (t m j) -> p m j t", t=4, j=4)
-            for half in range(2):
-                nc.scalar.copy(
-                    out=dealt[:, 64 * half : 64 * (half + 1)], in_=w1_raw[g][half][:].rearrange("p j (m t) -> p m j t", t=4)
-                )
-            nc.vector.quantize_mx(out=w1_q[g][:].bitcast(FP8), scales=w1_s[g][:], in_=w1_bf[:])
+            nc.vector.quantize_mx(out=w1_q[g][:].bitcast(FP8), scales=w1_s[g][:], in_=w1_bf[g][:])
 
         def features(g, b, before):
-            h_bf[g, b] = keep.tile([P, HALF, 4], BF16, name="h_bf", tag="h_bf%d" % g, align_bytes=64)
+            h_bf[g, b] = keep.tile([P, HALF, 4], BF16, name="h_bf", tag="h_bf%d" % b, align_bytes=64)
             for jb in range(4):
                 cols = slice(P * jb, P * (jb + 1))
                 a_ps = bank("low", [P, 4, P])
@@ -156,6 +159,8 @@ def tile_list_herbarium_expert_votes_kernel(
                     )
                 if jb == 0 and before:
                     a_sb = keep.tile([P, P, 4], F32, name="a_sb", tag="h_q%d%d" % before, align_bytes=64)
+                elif jb == 0:
+                    a_sb = keep.tile([P, P, 4], F32, name="a_sb", tag="w1_raw10", align_bytes=64)
                 else:
                     a_sb = ring.tile([P, P, 4], F32, name="a_sb", tag="a_sb", bufs=8)
                 nc.scalar.copy(out=a_sb[:], in_=a_ps[:].rearrange("p t n -> p n t"))
@@ -200,7 +205,7 @@ def tile_list_herbarium_expert_votes_kernel(
             d_ps = named_bank("high", 0, [P, HALF]) if (c, b) == (0, 1) else named_bank("low", b, [P, HALF])
             nc.tensor.matmul_mx(
                 out=d_ps[:], lhsT=w4_w[:, rows].bitcast(FP8), lhsT_scale=w4_s[:, rows],
-                rhs=v_w[b][:].bitcast(FP8), rhs_scale=v_s[b][:], start=True, stop=False,
+                rhs=v_w[b][:].bitcast(FP8), rhs_scale=v_s[b], start=True, stop=False,
             )
             for g in range(2):
                 nc.tensor.matmul_mx(
@@ -218,7 +223,7 @@ def tile_list_herbarium_expert_votes_kernel(
             e_ps = named_bank("low", 0, [P, HALF]) if (c, b) == (0, 1) else named_bank("high", b, [P, HALF])
             nc.tensor.matmul_mx(
                 out=e_ps[:], lhsT=w36_q[c][:, 2 * P : 3 * P].bitcast(FP8), lhsT_scale=w36_s[c][:, 2 * P : 3 * P],
-                rhs=v_w[b][:].bitcast(FP8), rhs_scale=v_s[b][:], start=True, stop=False,
+                rhs=v_w[b][:].bitcast(FP8), rhs_scale=v_s[b], start=True, stop=False,
             )
             for g in range(2):
                 nc.tensor.matmul_mx(
@@ -238,65 +243,78 @@ def tile_list_herbarium_expert_votes_kernel(
                 out=page[c][:].indirect(idx2[:, lo // 16 : hi // 16]), in0=votes[c][:, lo:hi], in1=wgo_sb[:, lo:hi], op=MULT
             )
 
+        def turn(c, hh):
+            z_ps = named_bank(("low", "high")[c % 2], 3 - hh, [P, 4, P])
+            for src in (x0_sb[c], page[c]):
+                for u in range(4):
+                    lo = 256 * u + P * hh
+                    nc.tensor.matmul(
+                        out=z_ps[:, u, :], lhsT=src[:, lo : lo + P], rhs=ident[:], is_transpose=True,
+                        start=(src is x0_sb[c] and u == 0), stop=(src is page[c] and u == 3),
+                    )
+            if hh == 1 and c < 2:
+                sig = keep.tile([P, 4, P], F32, name="sig", tag="votes%d" % c, align_bytes=64)
+            else:
+                sig = ring.tile([P, 4, P], F32, name="sig", tag="sig")
+            nc.scalar.activation(
+                out=sig[:].rearrange("p t q -> p q t"),
+                in_=z_ps[:].rearrange("p u (a t) -> p (u a) t", t=4),
+                func=ACT.Sigmoid,
+            )
+            return sig
+
         def finish(c):
-            last = c == 3
             y = ring.tile([P, 4, 256], F32, tag="y")
             y_ps = [named_bank(("high", "low")[c % 2], 2 + i, [P, 512]) for i in range(2)]
             for hh in range(2):
-                z_ps = named_bank(("low", "high")[c % 2], 3 - hh, [P, 4, P])
-                for src in (x0_sb[c], page[c]):
-                    for u in range(4):
-                        lo = 256 * u + P * hh
-                        nc.tensor.matmul(
-                            out=z_ps[:, u, :], lhsT=src[:, lo : lo + P], rhs=ident[:], is_transpose=True,
-                            start=(src is x0_sb[c] and u == 0), stop=(src is page[c] and u == 3),
-                        )
-                if hh == 1 and c < 2:
-                    sig = keep.tile([P, 4, P], F32, name="sig", tag="votes%d" % c, align_bytes=64)
-                elif last and hh == 0:
-                    sig = keep.tile([P, 4, P], F32, name="sig", tag="y_bf2", align_bytes=64)
-                else:
-                    sig = ring.tile([P, 4, P], F32, name="sig", tag="sig")
-                nc.scalar.activation(
-                    out=sig[:].rearrange("p t q -> p q t"),
-                    in_=z_ps[:].rearrange("p u (a t) -> p (u a) t", t=4),
-                    func=ACT.Sigmoid,
-                )
+                sig = turn(c, hh)
                 for t in range(4):
-                    if last:
-                        spot = y_ps[hh][:, P * t : P * (t + 1)]
-                    else:
-                        spot = y_ps[t // 2][:, 256 * (t % 2) + P * hh : 256 * (t % 2) + P * (hh + 1)]
+                    spot = y_ps[t // 2][:, 256 * (t % 2) + P * hh : 256 * (t % 2) + P * (hh + 1)]
                     nc.tensor.transpose(spot, sig[:, t, :], ident[:])
-                if last:
-                    cols = slice(P * hh, P * (hh + 1))
-                    nc.vector.tensor_tensor(
-                        out=y[:, :, cols], in0=y_ps[hh][:].rearrange("p (t m) -> p t m", t=4),
-                        in1=amp_sb[:, c, :].unsqueeze(2).to_broadcast([P, 4, P]), op=MULT,
-                    )
-                    (nc.scalar.copy, nc.vector.tensor_copy)[hh](
-                        out=y_bf[c][:, 512 * hh : 512 * (hh + 1)].rearrange("p (a i t) -> p a t i", i=4, t=4),
-                        in_=y[:, :, cols].rearrange("p t (a i) -> p a t i", i=4),
-                    )
-            if not last:
-                for t in range(4):
-                    nc.scalar.activation(
-                        out=y[:, t, :], in_=y_ps[t // 2][:, 256 * (t % 2) : 256 * (t % 2 + 1)], func=ACT.Copy,
-                        scale=amp_sb[:, c, t : t + 1],
-                    )
-                nc.scalar.copy(
-                    out=y_bf[c][:].rearrange("p (a i t) -> p a t i", i=4, t=4), in_=y[:].rearrange("p t (a i) -> p a t i", i=4)
+            for t in range(4):
+                nc.scalar.activation(
+                    out=y[:, t, :], in_=y_ps[t // 2][:, 256 * (t % 2) : 256 * (t % 2 + 1)], func=ACT.Copy,
+                    scale=amp_sb[:, c, t : t + 1],
                 )
+            nc.scalar.copy(
+                out=y_bf[c][:].rearrange("p (a i t) -> p a t i", i=4, t=4), in_=y[:].rearrange("p t (a i) -> p a t i", i=4)
+            )
             rows = out_0[P * c : P * (c + 1), :].rearrange("(a t) m -> a t m", t=4)
             for u in range(4):
                 nc.sync.dma_start(out=rows[:, :, 256 * u : 256 * (u + 1)], in_=y[32 * u : 32 * (u + 1)])
 
-        def store_words(c):
-            y_q = held([P, 256], U32, "y_q%d" % c)
-            nc.vector.quantize_mx(out=y_q[:].bitcast(FP8), scales=y_s[4 * c : P, :], in_=y_bf[c][:])
-            nc.sync.dma_start(
-                out=out_1[0, 32 * c : 32 * (c + 1)].rearrange("a (u m) t -> u a (m t)", u=4).bitcast(I32), in_=y_q[:].bitcast(I32)
-            )
+        def finish_last():
+            c = 3
+            z = held([P, S], F32, "z_last")
+            y = held([P, S], F32, "y_last")
+            y_q = held([P, 256], U32, "y_q_last")
+            halves = [slice(HALF * hh, HALF * (hh + 1)) for hh in range(2)]
+            for cols in halves:
+                nc.vector.tensor_tensor(out=z[:, cols], in0=page[c][:, cols], in1=x0_sb[c][:, cols], op=ADD)
+            store_planes((2, 1, 0), keep.tile([P, 3, 256], U32, name="y_q_early", tag="votes1", align_bytes=64))
+            y_ps = [named_bank("low", 2 + hh, [P, 4, P]) for hh in range(2)]
+            for hh in range(2):
+                sig = turn(c, hh)
+                for t in range(4):
+                    nc.tensor.transpose(y_ps[hh][:, t, :], sig[:, t, :], ident[:])
+            s_rows = ring.tile([P, S], F32, name="s_rows", tag="sig")
+            for cols in halves:
+                nc.scalar.activation(out=s_rows[:, cols], in_=z[:, cols], func=ACT.Sigmoid)
+            for hh in range(2):
+                nc.vector.tensor_tensor(
+                    out=y_bf[c][:, halves[hh]].rearrange("p (m t) -> p m t", t=4), in0=y_ps[hh][:].rearrange("p t m -> p m t"),
+                    in1=amp_sb[:, c, :].unsqueeze(1).to_broadcast([P, P, 4]), op=MULT,
+                )
+            words = out_1[0, 32 * c : 32 * (c + 1)].rearrange("a (u m) t -> u a (m t)", u=4).bitcast(I32)
+            for hh in range(2):
+                cols = slice(P * hh, P * (hh + 1))
+                nc.vector.quantize_mx(out=y_q[:, cols].bitcast(FP8), scales=y_s[4 * c : P, cols], in_=y_bf[c][:, halves[hh]])
+                nc.sync.dma_start(out=words[:, :, cols], in_=y_q[:, cols].bitcast(I32))
+                if hh == 0:
+                    nc.vector.tensor_scalar(out=y[:, halves[0]], in0=s_rows[:, halves[0]], scalar1=amp_last[:, 0:1], scalar2=None, op0=MULT)
+                else:
+                    nc.scalar.activation(out=y[:, halves[1]], in_=s_rows[:, halves[1]], func=ACT.Copy, scale=amp_last[:, 0:1])
+                nc.sync.dma_start(out=out_0[N - P : N, halves[hh]], in_=y[:, halves[hh]])
 
         def store_planes(tiles, y_q):
             for c in tiles:
@@ -307,17 +325,23 @@ def tile_list_herbarium_expert_votes_kernel(
                     out=words[:, 0:3, 256 * u : 256 * (u + 1)], in_=y_q[32 * u : 32 * (u + 1)].bitcast(I32)
                 )
 
-        gather(0)
+        nc.vector.tensor_copy(out=v_s_all[:], in_=tab_s[:].indirect(idx[:]))
         deal_w2(0)
-        quantise_w1(0)
-        gather(1)
         deal_w2(1)
-        quantise_w1(1)
+        cast_w1(0, 0)
+        cast_w1(0, 1)
+        quantise_w1(0)
+        gather(0, 256)
+        gather(256, 512)
+        gather(512, 1024)
+        cast_w1(1, 0)
         features(0, 0, None)
+        cast_w1(1, 1)
+        quantise_w1(1)
+        features(0, 1, (0, 0))
         quantise_w36(0, "w36_bf0")
-        features(1, 0, (0, 0))
-        features(0, 1, (1, 0))
-        features(1, 1, (0, 1))
+        features(1, 0, (0, 1))
+        features(1, 1, (1, 0))
         first_factor(0, 0)
         for c in range(4):
             vote(c, 0)
@@ -340,9 +364,7 @@ def tile_list_herbarium_expert_votes_kernel(
                 finish(c - 1)
             if c == 1:
                 quantise_w36(3, "h_bf1")
-        store_planes((2, 1, 0), keep.tile([P, 3, 256], U32, name="y_q_early", tag="votes1", align_bytes=64))
-        finish(3)
-        store_words(3)
+        finish_last()
         for u in range(4):
             nc.sync.dma_start(
                 out=out_2[0][:, 256 * u : 256 * (u + 1)].bitcast(I32), in_=y_s[32 * u : 32 * u + 16, :].bitcast(I32)

@@ -65,7 +65,7 @@ def tile_list_herbarium_expert_votes_kernel(
             for g in range(2)
         ]
         w36_first = [held([P, 4, P], F32, "w36_first%d" % s) for s in range(3)]
-        w36_rest = [held([P, 4, N - P], F32, "w36_rest%d" % s) for s in range(3)]
+        w36_rest = [keep.tile([P, 4, N - P], F32, name="w36_rest", tag="w36_rest%d" % s, align_bytes=64) for s in range(3)]
         wgo_sb = held([P, S], F32, "wgo_sb")
         x0_sb = [held([P, S], F32, "x0_sb%d" % c) for c in range(4)]
         amp_sb = held([P, 4, 4], F32, "amp_sb")
@@ -161,6 +161,8 @@ def tile_list_herbarium_expert_votes_kernel(
                     a_sb = keep.tile([P, P, 4], F32, name="a_sb", tag="h_q%d%d" % before, align_bytes=64)
                 elif jb == 0:
                     a_sb = keep.tile([P, P, 4], F32, name="a_sb", tag="w1_raw10", align_bytes=64)
+                elif (g, b, jb) == (1, 1, 3):
+                    a_sb = keep.tile([P, P, 4], F32, name="a_sb", tag="w6_bf", align_bytes=64)
                 else:
                     a_sb = ring.tile([P, P, 4], F32, name="a_sb", tag="a_sb", bufs=8)
                 nc.scalar.copy(out=a_sb[:], in_=a_ps[:].rearrange("p t n -> p n t"))
@@ -181,7 +183,8 @@ def tile_list_herbarium_expert_votes_kernel(
                 out=h_q[g][b][:].bitcast(FP8), scales=h_s[g][b][:], in_=h_bf[g, b][:].rearrange("p n t -> p (n t)")
             )
 
-        w36_q = [held([P, 3 * P], U32, "w36_q%d" % c) for c in range(4)]
+        w36_q = {}
+        e_sb = {}
         w36_s = [held([P, 3 * P], U8, "w36_s%d" % c) for c in range(4)]
         page = {}
         d_neg = {}
@@ -189,20 +192,31 @@ def tile_list_herbarium_expert_votes_kernel(
         y_bf = [keep.tile([P, 1024], BF16, name="y_bf%d" % c, tag="y_bf%d" % c, align_bytes=64) for c in range(4)]
         y_s = held([P, 256], U8, "y_s")
 
-        def quantise_w36(c, tag):
-            w36_bf = keep.tile([P, 1536], BF16, name="w36_bf", tag=tag, align_bytes=64)
+        def shared(shape, dtype, name, tag):
+            return keep.tile(shape, dtype, name=name, tag=tag, align_bytes=64)
+
+        w3_bf = {}
+        w6_bf = {}
+
+        def cast_w36(c):
+            w3_bf[c] = shared([P, 1024], BF16, "w3_bf", ("w3_bf0", "h_bf1", "d1", "d2")[c])
+            w6_bf[c] = shared([P, 512], BF16, "w6_bf", "w6_bf")
             for s in range(3):
                 raw = w36_first[s][:] if c == 0 else w36_rest[s][:, :, P * (c - 1) : P * c]
+                spot = w3_bf[c][:, 512 * s : 512 * (s + 1)] if s < 2 else w6_bf[c][:]
                 nc.scalar.copy(
-                    out=w36_bf[:, 512 * s : 512 * (s + 1)].rearrange("p (a i j) -> p a j i", i=4, j=4),
-                    in_=raw.rearrange("p j (a i) -> p a j i", i=4),
+                    out=spot.rearrange("p (a i j) -> p a j i", i=4, j=4), in_=raw.rearrange("p j (a i) -> p a j i", i=4)
                 )
-            nc.vector.quantize_mx(out=w36_q[c][:, 0:256].bitcast(FP8), scales=w36_s[c][:, 0:256], in_=w36_bf[:, 0:1024])
-            nc.vector.quantize_mx(out=w36_q[c][:, 256:384].bitcast(FP8), scales=w36_s[c][:, 256:384], in_=w36_bf[:, 1024:1536])
 
-        def first_factor(c, b):
+        def quantise_w36(c):
+            w36_q[c] = shared([P, 3 * P], U32, "w36_q", ("w36_q0", "votes0", "h_bf1", "votes3")[c])
+            nc.vector.quantize_mx(out=w36_q[c][:, 0:256].bitcast(FP8), scales=w36_s[c][:, 0:256], in_=w3_bf[c][:])
+            nc.vector.quantize_mx(out=w36_q[c][:, 256:384].bitcast(FP8), scales=w36_s[c][:, 256:384], in_=w6_bf[c][:])
+
+        def first_factor(k):
+            c, b = divmod(k, 2)
             rows = slice(P * c, P * (c + 1))
-            d_ps = named_bank("high", 0, [P, HALF]) if (c, b) == (0, 1) else named_bank("low", b, [P, HALF])
+            d_ps = named_bank("low", b, [P, HALF])
             nc.tensor.matmul_mx(
                 out=d_ps[:], lhsT=w4_w[:, rows].bitcast(FP8), lhsT_scale=w4_s[:, rows],
                 rhs=v_w[b][:].bitcast(FP8), rhs_scale=v_s[b], start=True, stop=False,
@@ -212,15 +226,13 @@ def tile_list_herbarium_expert_votes_kernel(
                     out=d_ps[:], lhsT=w36_q[c][:, P * g : P * (g + 1)].bitcast(FP8), lhsT_scale=w36_s[c][:, P * g : P * (g + 1)],
                     rhs=h_q[g][b][:].bitcast(FP8), rhs_scale=h_s[g][b][:], start=False, stop=(g == 1),
                 )
-            if c == 0:
-                d_neg[c, b] = keep.tile([P, HALF], F32, name="d_neg", tag=("h_q11", "late1")[b], align_bytes=64)
-            else:
-                d_neg[c, b] = ring.tile([P, HALF], F32, name="d_neg", tag="d_neg", bufs=4)
-            nc.scalar.activation(out=d_neg[c, b][:], in_=d_ps[:], func=ACT.Copy, scale=-1.0)
+            d_neg[k] = shared([P, HALF], F32, "d_neg", "h_q11" if k == 0 else "d%d" % k)
+            nc.scalar.activation(out=d_neg[k][:], in_=d_ps[:], func=ACT.Copy, scale=-1.0)
 
-        def vote(c, b):
+        def second_factor(k):
+            c, b = divmod(k, 2)
             rows = slice(P * c, P * (c + 1))
-            e_ps = named_bank("low", 0, [P, HALF]) if (c, b) == (0, 1) else named_bank("high", b, [P, HALF])
+            e_ps = named_bank("high", b, [P, HALF])
             nc.tensor.matmul_mx(
                 out=e_ps[:], lhsT=w36_q[c][:, 2 * P : 3 * P].bitcast(FP8), lhsT_scale=w36_s[c][:, 2 * P : 3 * P],
                 rhs=v_w[b][:].bitcast(FP8), rhs_scale=v_s[b], start=True, stop=False,
@@ -230,20 +242,47 @@ def tile_list_herbarium_expert_votes_kernel(
                     out=e_ps[:], lhsT=w5_w[:, g, 2 * P * c : 2 * P * (c + 1)].bitcast(FP4), lhsT_scale=w5_s[:, g, rows],
                     rhs=h_q[g][b][:].bitcast(FP8), rhs_scale=h_s[g][b][:], start=False, stop=(g == 1),
                 )
+            return e_ps
+
+        def weight(k):
+            return wgo_sb[:, HALF * (k % 2) : HALF * (k % 2 + 1)]
+
+        def new_votes(k):
+            votes[k] = shared([P, HALF], F32, "votes", ("votes0", "h_bf1", "d1", "votes3", "d1", "w6_bf", "d1", "w6_bf")[k])
+            return votes[k]
+
+        def vote_on_vector(k):
+            e_ps = second_factor(k)
+            nc.vector.tensor_tensor(out=new_votes(k)[:], in0=e_ps[:], in1=d_neg[k][:], op=MULT)
+
+        def weigh_on_gpsimd(k):
+            nc.gpsimd.tensor_tensor(out=d_neg[k][:], in0=d_neg[k][:], in1=weight(k), op=MULT)
+
+        def copy_second(k):
+            e_ps = second_factor(k)
+            e_sb[k] = ring.tile([P, HALF], F32, name="e_sb", tag="e_sb")
+            nc.scalar.copy(out=e_sb[k][:], in_=e_ps[:])
+
+        def vote_on_gpsimd(k):
+            nc.gpsimd.tensor_tensor(out=new_votes(k)[:], in0=e_sb[k][:], in1=d_neg[k][:], op=MULT)
+
+        def place(k):
+            c, b = divmod(k, 2)
             if b == 0:
-                votes[c] = keep.tile([P, S], F32, name="votes", tag="votes%d" % (c % 2), align_bytes=64)
-            elif c == 0:
-                votes[c] = keep.tile([P, S], F32, name="votes", tag="h_bf1", align_bytes=64)
-            nc.vector.tensor_tensor(out=votes[c][:, HALF * b : HALF * (b + 1)], in0=e_ps[:], in1=d_neg[c, b][:], op=MULT)
+                page[c] = shared([P, WINDOW], F32, "page", "d2" if c == 2 else "page%d" % c)
+            window = page[c][:].indirect(idx2[:, 32 * b : 32 * (b + 1)])
+            if k == 0:
+                nc.vector.tensor_tensor(out=window, in0=votes[k][:], in1=weight(k), op=MULT)
+            else:
+                nc.vector.tensor_copy(out=window, in_=votes[k][:])
 
-        def place(c, lo, hi):
-            if lo == 0:
-                page[c] = keep.tile([P, WINDOW], F32, name="page", tag={1: "late1", 2: "h_bf1"}.get(c, "page%d" % c), align_bytes=64)
-            nc.vector.tensor_tensor(
-                out=page[c][:].indirect(idx2[:, lo // 16 : hi // 16]), in0=votes[c][:, lo:hi], in1=wgo_sb[:, lo:hi], op=MULT
-            )
+        def prepare(k):
+            first_factor(k)
+            copy_second(k)
+            weigh_on_gpsimd(k)
+            vote_on_gpsimd(k)
 
-        def turn(c, hh):
+        def turn(c, hh, sig):
             z_ps = named_bank(("low", "high")[c % 2], 3 - hh, [P, 4, P])
             for src in (x0_sb[c], page[c]):
                 for u in range(4):
@@ -252,22 +291,19 @@ def tile_list_herbarium_expert_votes_kernel(
                         out=z_ps[:, u, :], lhsT=src[:, lo : lo + P], rhs=ident[:], is_transpose=True,
                         start=(src is x0_sb[c] and u == 0), stop=(src is page[c] and u == 3),
                     )
-            if hh == 1 and c < 2:
-                sig = keep.tile([P, 4, P], F32, name="sig", tag="votes%d" % c, align_bytes=64)
-            else:
-                sig = ring.tile([P, 4, P], F32, name="sig", tag="sig")
             nc.scalar.activation(
-                out=sig[:].rearrange("p t q -> p q t"),
+                out=sig.rearrange("p t q -> p q t"),
                 in_=z_ps[:].rearrange("p u (a t) -> p (u a) t", t=4),
                 func=ACT.Sigmoid,
             )
-            return sig
 
         def finish(c):
             y = ring.tile([P, 4, 256], F32, tag="y")
             y_ps = [named_bank(("high", "low")[c % 2], 2 + i, [P, 512]) for i in range(2)]
+            both = shared([P, 2, 4, P], F32, "sig", ("w6_bf", "w36_rest2", "sig2")[c])
             for hh in range(2):
-                sig = turn(c, hh)
+                sig = both[:, hh]
+                turn(c, hh, sig)
                 for t in range(4):
                     spot = y_ps[t // 2][:, 256 * (t % 2) + P * hh : 256 * (t % 2) + P * (hh + 1)]
                     nc.tensor.transpose(spot, sig[:, t, :], ident[:])
@@ -291,13 +327,14 @@ def tile_list_herbarium_expert_votes_kernel(
             halves = [slice(HALF * hh, HALF * (hh + 1)) for hh in range(2)]
             for cols in halves:
                 nc.vector.tensor_tensor(out=z[:, cols], in0=page[c][:, cols], in1=x0_sb[c][:, cols], op=ADD)
-            store_planes((2, 1, 0), keep.tile([P, 3, 256], U32, name="y_q_early", tag="votes1", align_bytes=64))
+            store_planes((2, 1, 0), keep.tile([P, 3, 256], U32, name="y_q_early", tag="w6_bf", align_bytes=64))
             y_ps = [named_bank("low", 2 + hh, [P, 4, P]) for hh in range(2)]
             for hh in range(2):
-                sig = turn(c, hh)
+                sig = shared([P, 4, P], F32, "sig", "sig3%d" % hh)[:]
+                turn(c, hh, sig)
                 for t in range(4):
                     nc.tensor.transpose(y_ps[hh][:, t, :], sig[:, t, :], ident[:])
-            s_rows = ring.tile([P, S], F32, name="s_rows", tag="sig")
+            s_rows = shared([P, S], F32, "s_rows", "sig30")
             for cols in halves:
                 nc.scalar.activation(out=s_rows[:, cols], in_=z[:, cols], func=ACT.Sigmoid)
             for hh in range(2):
@@ -339,31 +376,48 @@ def tile_list_herbarium_expert_votes_kernel(
         cast_w1(1, 1)
         quantise_w1(1)
         features(0, 1, (0, 0))
-        quantise_w36(0, "w36_bf0")
+        cast_w36(0)
+        quantise_w36(0)
         features(1, 0, (0, 1))
         features(1, 1, (1, 0))
-        first_factor(0, 0)
-        for c in range(4):
-            vote(c, 0)
-            if c == 0:
-                quantise_h(1, 1)
-                place(c, 0, HALF)
-                quantise_w36(1, "h_bf1")
-                first_factor(0, 1)
-                vote(c, 1)
-                place(c, HALF, S)
-            else:
-                vote(c, 1)
-                place(c, 0, S)
-            if c < 3:
-                first_factor(c + 1, 0)
-                first_factor(c + 1, 1)
-            if c == 0:
-                quantise_w36(2, "late1")
-            if c > 0:
-                finish(c - 1)
-            if c == 1:
-                quantise_w36(3, "h_bf1")
+        first_factor(0)
+        vote_on_vector(0)
+        quantise_h(1, 1)
+        place(0)
+        cast_w36(1)
+        first_factor(1)
+        e_1 = second_factor(1)
+        quantise_w36(1)
+        nc.vector.tensor_tensor(out=d_neg[1][:], in0=e_1[:], in1=d_neg[1][:], op=MULT)
+        nc.vector.tensor_tensor(out=new_votes(1)[:], in0=d_neg[1][:], in1=weight(1), op=MULT)
+        place(1)
+        cast_w36(2)
+        first_factor(2)
+        weigh_on_gpsimd(2)
+        first_factor(3)
+        weigh_on_gpsimd(3)
+        quantise_w36(2)
+        vote_on_vector(2)
+        copy_second(3)
+        vote_on_gpsimd(3)
+        place(2)
+        prepare(4)
+        place(3)
+        finish(0)
+        first_factor(5)
+        copy_second(5)
+        weigh_on_gpsimd(5)
+        cast_w36(3)
+        quantise_w36(3)
+        vote_on_gpsimd(5)
+        place(4)
+        place(5)
+        prepare(6)
+        prepare(7)
+        finish(1)
+        place(6)
+        place(7)
+        finish(2)
         finish_last()
         for u in range(4):
             nc.sync.dma_start(

@@ -113,7 +113,7 @@ def tile_list_herbarium_expert_votes_kernel(
         v_w = [held([P, HALF], U32, "v_w%d" % b) for b in range(2)]
         v_s_all = held([P, S], U8, "v_s_all")
         v_s = [v_s_all[:, HALF * b : HALF * (b + 1)] for b in range(2)]
-        w1_q = [held([P, 512], U32, "w1_q%d" % g) for g in range(2)]
+        w1_q = {}
         w1_s = [held([P, 512], U8, "w1_s%d" % g) for g in range(2)]
         w2_w = [held([P, 1024], U8, "w2_w%d" % g) for g in range(2)]
         w2_s = [held([P, 512], U8, "w2_s%d" % g) for g in range(2)]
@@ -137,16 +137,24 @@ def tile_list_herbarium_expert_votes_kernel(
 
         w1_bf = [held([P, 2048], BF16, "w1_bf%d" % g) for g in range(2)]
 
+        def round_on_gpsimd(out, in_):
+            nc.gpsimd.tensor_scalar(out=out, in0=in_, scalar1=1.0, scalar2=0.0, op0=MULT, op1=ADD)
+
         def cast_w1(g, half):
+            if g == 1:
+                dealt = w1_bf[g][:].rearrange("p (t m j) -> p m t j", t=4, j=4)
+                round_on_gpsimd(dealt[:, 64 * half : 64 * (half + 1)], w1_raw[g][half][:].rearrange("p j (m t) -> p m t j", t=4))
+                return
             dealt = w1_bf[g][:].rearrange("p (t m j) -> p m j t", t=4, j=4)
-            (nc.vector.tensor_copy if (g, half) == (1, 1) else nc.scalar.copy)(
+            nc.scalar.copy(
                 out=dealt[:, 64 * half : 64 * (half + 1)], in_=w1_raw[g][half][:].rearrange("p j (m t) -> p m j t", t=4)
             )
 
         def quantise_w1(g):
+            w1_q[g] = keep.tile([P, 512], U32, name="w1_q", tag="w1_q%d" % g, align_bytes=64)
             nc.vector.quantize_mx(out=w1_q[g][:].bitcast(FP8), scales=w1_s[g][:], in_=w1_bf[g][:])
 
-        def features(g, b, before):
+        def features(g, b, behind):
             h_bf[g, b] = keep.tile([P, HALF, 4], BF16, name="h_bf", tag="h_bf%d" % b, align_bytes=64)
             for jb in range(4):
                 cols = slice(P * jb, P * (jb + 1))
@@ -157,14 +165,10 @@ def tile_list_herbarium_expert_votes_kernel(
                         lhsT=w1_q[g][:, P * t : P * (t + 1)].bitcast(FP8), lhsT_scale=w1_s[g][:, P * t : P * (t + 1)],
                         rhs=v_w[b][:, cols].bitcast(FP8), rhs_scale=v_s[b][:, cols], start=True, stop=True,
                     )
-                if jb == 0 and before:
-                    a_sb = keep.tile([P, P, 4], F32, name="a_sb", tag="h_q%d%d" % before, align_bytes=64)
-                elif jb == 0:
-                    a_sb = keep.tile([P, P, 4], F32, name="a_sb", tag="w1_raw10", align_bytes=64)
-                elif (g, b, jb) == (1, 1, 3):
-                    a_sb = keep.tile([P, P, 4], F32, name="a_sb", tag="w6_bf", align_bytes=64)
+                if jb in behind:
+                    a_sb = keep.tile([P, P, 4], F32, name="a_sb", tag=behind[jb][0], align_bytes=64)
                 else:
-                    a_sb = ring.tile([P, P, 4], F32, name="a_sb", tag="a_sb", bufs=8)
+                    a_sb = ring.tile([P, P, 4], F32, name="a_sb", tag="a_sb", bufs=6)
                 nc.scalar.copy(out=a_sb[:], in_=a_ps[:].rearrange("p t n -> p n t"))
                 b_ps = bank("high", [P, 4, P])
                 for t in range(4):
@@ -174,8 +178,8 @@ def tile_list_herbarium_expert_votes_kernel(
                         rhs=v_w[b][:, cols].bitcast(FP8), rhs_scale=v_s[b][:, cols], start=True, stop=True,
                     )
                 nc.vector.tensor_tensor(out=h_bf[g, b][:, cols, :], in0=b_ps[:].rearrange("p t n -> p n t"), in1=a_sb[:], op=MULT)
-                if jb == 0 and before:
-                    quantise_h(*before)
+                if jb in behind and behind[jb][1]:
+                    behind[jb][1]()
 
         def quantise_h(g, b):
             h_q[g][b] = keep.tile([P, HALF], U32, name="h_q", tag="h_q%d%d" % (g, b), align_bytes=64)
@@ -195,23 +199,32 @@ def tile_list_herbarium_expert_votes_kernel(
         def shared(shape, dtype, name, tag):
             return keep.tile(shape, dtype, name=name, tag=tag, align_bytes=64)
 
+        d_last = shared([P, S], F32, "d_last", "w1_raw00")
+        e_last = held([P, S], F32, "e_last")
         w3_bf = {}
         w6_bf = {}
 
         def cast_w36(c):
-            w3_bf[c] = shared([P, 1024], BF16, "w3_bf", ("w3_bf0", "h_bf1", "d1", "d2")[c])
-            w6_bf[c] = shared([P, 512], BF16, "w6_bf", "w6_bf")
+            if c < 3:
+                both = shared([P, 1536], BF16, "w36_bf", ("w36_bf0", "a_last", "h_bf1")[c])
+                w3_bf[c], w6_bf[c] = both[:, 0:1024], both[:, 1024:1536]
+            else:
+                w3_bf[c] = shared([P, 1024], BF16, "w3_bf", "h_bf0")[:]
+                w6_bf[c] = shared([P, 512], BF16, "w6_bf", "a_last")[:]
             for s in range(3):
                 raw = w36_first[s][:] if c == 0 else w36_rest[s][:, :, P * (c - 1) : P * c]
-                spot = w3_bf[c][:, 512 * s : 512 * (s + 1)] if s < 2 else w6_bf[c][:]
+                spot = w3_bf[c][:, 512 * s : 512 * (s + 1)] if s < 2 else w6_bf[c]
+                if c == 0 and s < 2:
+                    round_on_gpsimd(spot.rearrange("p (n j) -> p n j", j=4), raw.rearrange("p j n -> p n j"))
+                    continue
                 nc.scalar.copy(
                     out=spot.rearrange("p (a i j) -> p a j i", i=4, j=4), in_=raw.rearrange("p j (a i) -> p a j i", i=4)
                 )
 
         def quantise_w36(c):
-            w36_q[c] = shared([P, 3 * P], U32, "w36_q", ("w36_q0", "votes0", "h_bf1", "votes3")[c])
-            nc.vector.quantize_mx(out=w36_q[c][:, 0:256].bitcast(FP8), scales=w36_s[c][:, 0:256], in_=w3_bf[c][:])
-            nc.vector.quantize_mx(out=w36_q[c][:, 256:384].bitcast(FP8), scales=w36_s[c][:, 256:384], in_=w6_bf[c][:])
+            w36_q[c] = shared([P, 3 * P], U32, "w36_q", ("w36_q0", "votes0", "d1", "d2")[c])
+            nc.vector.quantize_mx(out=w36_q[c][:, 0:256].bitcast(FP8), scales=w36_s[c][:, 0:256], in_=w3_bf[c])
+            nc.vector.quantize_mx(out=w36_q[c][:, 256:384].bitcast(FP8), scales=w36_s[c][:, 256:384], in_=w6_bf[c])
 
         def first_factor(k):
             c, b = divmod(k, 2)
@@ -226,13 +239,16 @@ def tile_list_herbarium_expert_votes_kernel(
                     out=d_ps[:], lhsT=w36_q[c][:, P * g : P * (g + 1)].bitcast(FP8), lhsT_scale=w36_s[c][:, P * g : P * (g + 1)],
                     rhs=h_q[g][b][:].bitcast(FP8), rhs_scale=h_s[g][b][:], start=False, stop=(g == 1),
                 )
-            d_neg[k] = shared([P, HALF], F32, "d_neg", "h_q11" if k == 0 else "d%d" % k)
-            nc.scalar.activation(out=d_neg[k][:], in_=d_ps[:], func=ACT.Copy, scale=-1.0)
+            if k < 6:
+                d_neg[k] = shared([P, HALF], F32, "d_neg", "h_q11" if k == 0 else "d%d" % k)[:]
+            else:
+                d_neg[k] = d_last[:, HALF * b : HALF * (b + 1)]
+            nc.scalar.activation(out=d_neg[k], in_=d_ps[:], func=ACT.Copy, scale=-1.0)
 
         def second_factor(k):
             c, b = divmod(k, 2)
             rows = slice(P * c, P * (c + 1))
-            e_ps = named_bank("high", b, [P, HALF])
+            e_ps = named_bank("high", 2 if k == 4 else b, [P, HALF])
             nc.tensor.matmul_mx(
                 out=e_ps[:], lhsT=w36_q[c][:, 2 * P : 3 * P].bitcast(FP8), lhsT_scale=w36_s[c][:, 2 * P : 3 * P],
                 rhs=v_w[b][:].bitcast(FP8), rhs_scale=v_s[b], start=True, stop=False,
@@ -248,33 +264,36 @@ def tile_list_herbarium_expert_votes_kernel(
             return wgo_sb[:, HALF * (k % 2) : HALF * (k % 2 + 1)]
 
         def new_votes(k):
-            votes[k] = shared([P, HALF], F32, "votes", ("votes0", "h_bf1", "d1", "votes3", "d1", "w6_bf", "d1", "w6_bf")[k])
+            votes[k] = shared([P, HALF], F32, "votes", ("votes0", "h_bf1", "votes2", "h_bf0")[k])[:] if k < 4 else d_neg[k]
             return votes[k]
 
         def vote_on_vector(k):
             e_ps = second_factor(k)
-            nc.vector.tensor_tensor(out=new_votes(k)[:], in0=e_ps[:], in1=d_neg[k][:], op=MULT)
+            nc.vector.tensor_tensor(out=new_votes(k), in0=e_ps[:], in1=d_neg[k], op=MULT)
 
         def weigh_on_gpsimd(k):
-            nc.gpsimd.tensor_tensor(out=d_neg[k][:], in0=d_neg[k][:], in1=weight(k), op=MULT)
+            plain = d_neg[k]
+            if k > 3:
+                d_neg[k] = shared([P, HALF], F32, "weighed", ("e3", "d4")[k - 4])[:]
+            nc.gpsimd.tensor_tensor(out=d_neg[k], in0=plain, in1=weight(k), op=MULT)
 
         def copy_second(k):
             e_ps = second_factor(k)
-            e_sb[k] = ring.tile([P, HALF], F32, name="e_sb", tag="e_sb")
-            nc.scalar.copy(out=e_sb[k][:], in_=e_ps[:])
+            e_sb[k] = shared([P, HALF], F32, "e_sb", "e%d" % k)[:] if k < 6 else e_last[:, HALF * (k - 6) : HALF * (k - 5)]
+            nc.scalar.copy(out=e_sb[k], in_=e_ps[:])
 
         def vote_on_gpsimd(k):
-            nc.gpsimd.tensor_tensor(out=new_votes(k)[:], in0=e_sb[k][:], in1=d_neg[k][:], op=MULT)
+            nc.gpsimd.tensor_tensor(out=new_votes(k), in0=e_sb[k], in1=d_neg[k], op=MULT)
 
         def place(k):
             c, b = divmod(k, 2)
             if b == 0:
-                page[c] = shared([P, WINDOW], F32, "page", "d2" if c == 2 else "page%d" % c)
+                page[c] = shared([P, WINDOW], F32, "page", "a_last" if c == 1 else "page%d" % c)
             window = page[c][:].indirect(idx2[:, 32 * b : 32 * (b + 1)])
             if k == 0:
-                nc.vector.tensor_tensor(out=window, in0=votes[k][:], in1=weight(k), op=MULT)
+                nc.vector.tensor_tensor(out=window, in0=votes[k], in1=weight(k), op=MULT)
             else:
-                nc.vector.tensor_copy(out=window, in_=votes[k][:])
+                nc.vector.tensor_copy(out=window, in_=votes[k])
 
         def prepare(k):
             first_factor(k)
@@ -283,7 +302,7 @@ def tile_list_herbarium_expert_votes_kernel(
             vote_on_gpsimd(k)
 
         def turn(c, hh, sig):
-            z_ps = named_bank(("low", "high")[c % 2], 3 - hh, [P, 4, P])
+            z_ps = named_bank(("low", "high")[c % 2], 3 - hh, [P, 4, P]) if c else named_bank(("low", "high")[hh], 1, [P, 4, P])
             for src in (x0_sb[c], page[c]):
                 for u in range(4):
                     lo = 256 * u + P * hh
@@ -297,16 +316,22 @@ def tile_list_herbarium_expert_votes_kernel(
                 func=ACT.Sigmoid,
             )
 
-        def finish(c):
-            y = ring.tile([P, 4, 256], F32, tag="y")
+        turned = {}
+
+        def turn_back(c):
             y_ps = [named_bank(("high", "low")[c % 2], 2 + i, [P, 512]) for i in range(2)]
-            both = shared([P, 2, 4, P], F32, "sig", ("w6_bf", "w36_rest2", "sig2")[c])
+            both = shared([P, 2, 4, P], F32, "sig", "sig%d" % (c % 2))
             for hh in range(2):
                 sig = both[:, hh]
                 turn(c, hh, sig)
                 for t in range(4):
                     spot = y_ps[t // 2][:, 256 * (t % 2) + P * hh : 256 * (t % 2) + P * (hh + 1)]
                     nc.tensor.transpose(spot, sig[:, t, :], ident[:])
+            turned[c] = y_ps
+
+        def finish(c):
+            y = ring.tile([P, 4, 256], F32, tag="y")
+            y_ps = turned[c]
             for t in range(4):
                 nc.scalar.activation(
                     out=y[:, t, :], in_=y_ps[t // 2][:, 256 * (t % 2) : 256 * (t % 2 + 1)], func=ACT.Copy,
@@ -327,7 +352,7 @@ def tile_list_herbarium_expert_votes_kernel(
             halves = [slice(HALF * hh, HALF * (hh + 1)) for hh in range(2)]
             for cols in halves:
                 nc.vector.tensor_tensor(out=z[:, cols], in0=page[c][:, cols], in1=x0_sb[c][:, cols], op=ADD)
-            store_planes((2, 1, 0), keep.tile([P, 3, 256], U32, name="y_q_early", tag="w6_bf", align_bytes=64))
+            store_planes((2, 1, 0), keep.tile([P, 3, 256], U32, name="y_q_early", tag="e5", align_bytes=64))
             y_ps = [named_bank("low", 2 + hh, [P, 4, P]) for hh in range(2)]
             for hh in range(2):
                 sig = shared([P, 4, P], F32, "sig", "sig3%d" % hh)[:]
@@ -372,14 +397,12 @@ def tile_list_herbarium_expert_votes_kernel(
         gather(256, 512)
         gather(512, 1024)
         cast_w1(1, 0)
-        features(0, 0, None)
         cast_w1(1, 1)
-        quantise_w1(1)
-        features(0, 1, (0, 0))
+        features(0, 0, {})
         cast_w36(0)
-        quantise_w36(0)
-        features(1, 0, (0, 1))
-        features(1, 1, (1, 0))
+        features(0, 1, {1: ("w1_q1", lambda: quantise_w1(1)), 2: ("h_q00", lambda: quantise_h(0, 0))})
+        features(1, 0, {0: ("h_q01", lambda: quantise_h(0, 1)), 1: ("w36_q0", lambda: quantise_w36(0))})
+        features(1, 1, {0: ("h_q10", lambda: quantise_h(1, 0)), 3: ("a_last", None)})
         first_factor(0)
         vote_on_vector(0)
         quantise_h(1, 1)
@@ -387,36 +410,41 @@ def tile_list_herbarium_expert_votes_kernel(
         cast_w36(1)
         first_factor(1)
         e_1 = second_factor(1)
-        quantise_w36(1)
-        nc.vector.tensor_tensor(out=d_neg[1][:], in0=e_1[:], in1=d_neg[1][:], op=MULT)
-        nc.vector.tensor_tensor(out=new_votes(1)[:], in0=d_neg[1][:], in1=weight(1), op=MULT)
-        place(1)
         cast_w36(2)
+        quantise_w36(1)
+        plain = shared([P, HALF], F32, "plain", "a_last")
+        nc.vector.tensor_tensor(out=plain[:], in0=e_1[:], in1=d_neg[1], op=MULT)
+        quantise_w36(2)
+        nc.vector.tensor_tensor(out=new_votes(1), in0=plain[:], in1=weight(1), op=MULT)
+        place(1)
+        cast_w36(3)
         first_factor(2)
         weigh_on_gpsimd(2)
         first_factor(3)
-        weigh_on_gpsimd(3)
-        quantise_w36(2)
-        vote_on_vector(2)
         copy_second(3)
+        weigh_on_gpsimd(3)
+        vote_on_vector(2)
+        quantise_w36(3)
         vote_on_gpsimd(3)
         place(2)
         prepare(4)
         place(3)
+        prepare(5)
+        turn_back(0)
+        first_factor(6)
+        first_factor(7)
+        weighed_last = shared([P, S], F32, "weighed_last", "e5")
+        nc.gpsimd.tensor_tensor(out=weighed_last[:], in0=d_last[:], in1=wgo_sb[:], op=MULT)
         finish(0)
-        first_factor(5)
-        copy_second(5)
-        weigh_on_gpsimd(5)
-        cast_w36(3)
-        quantise_w36(3)
-        vote_on_gpsimd(5)
+        copy_second(6)
+        copy_second(7)
         place(4)
         place(5)
-        prepare(6)
-        prepare(7)
+        turn_back(1)
         finish(1)
-        place(6)
-        place(7)
+        page[3] = held([P, WINDOW], F32, "page3")
+        nc.vector.tensor_tensor(out=page[3][:].indirect(idx2[:]), in0=weighed_last[:], in1=e_last[:], op=MULT)
+        turn_back(2)
         finish(2)
         finish_last()
         for u in range(4):

@@ -52,7 +52,7 @@ def tile_list_herbarium_expert_votes_kernel(
 
         idx = keep.tile([P, S // 16], U16, name="idx")
         idx2 = keep.tile([P, S // 16], U16, name="idx2")
-        tab_w = held([P, T], U32, "tab_w")
+        tab_w = keep.tile([P, T], U32, name="tab_w", tag="tab_w", align_bytes=64)
         tab_s = held([P, T], U8, "tab_s")
         w2_raw = held([P, 2 * H], U8, "w2_raw")
         w2_raw_s = held([P, H], U8, "w2_raw_s")
@@ -64,8 +64,8 @@ def tile_list_herbarium_expert_votes_kernel(
             [keep.tile([P, 4, 256], F32, name="w1_raw", tag="w1_raw%d%d" % (g, half), align_bytes=64) for half in range(2)]
             for g in range(2)
         ]
-        w36_first = [held([P, 4, P], F32, "w36_first%d" % s) for s in range(3)]
-        w36_rest = [keep.tile([P, 4, N - P], F32, name="w36_rest", tag="w36_rest%d" % s, align_bytes=64) for s in range(3)]
+        w36_first = [held([P, 4, 2 * P], F32, "w36_first%d" % s) for s in range(3)]
+        w36_rest = [keep.tile([P, 4, 2 * P], F32, name="w36_rest", tag="w36_rest%d" % s, align_bytes=64) for s in range(3)]
         wgo_sb = held([P, S], F32, "wgo_sb")
         x0_sb = [held([P, S], F32, "x0_sb%d" % c) for c in range(4)]
         amp_sb = held([P, 4, 4], F32, "amp_sb")
@@ -94,16 +94,15 @@ def tile_list_herbarium_expert_votes_kernel(
         w3_rows = w3.rearrange("(g p j) n -> g p j n", g=2, j=4)
         w36_rows = (w3_rows[0], w3_rows[1], w6.rearrange("(p j) n -> p j n", j=4))
         for s in range(3):
-            nc.sync.dma_start(out=w36_first[s][:], in_=w36_rows[s][:, :, 0:P])
+            nc.sync.dma_start(out=w36_first[s][:], in_=w36_rows[s][:, :, 0 : 2 * P])
         nc.sync.dma_start(out=w4_w[:].bitcast(I32), in_=w4_words[0].rearrange("p n t -> p (n t)").bitcast(I32))
         nc.sync.dma_start(out=w5_w[:].bitcast(I32), in_=w5_words.rearrange("a p b -> p a b").bitcast(I32))
         load_scale_rows(nc.sync, w4_s, w4_scales[0])
-        nc.sync.dma_start(out=w36_rest[0][:], in_=w36_rows[0][:, :, P:N])
-        load_scale_rows(nc.sync, w5_s, w5_scales.rearrange("a r n -> r a n"))
-        for s in range(1, 3):
-            nc.sync.dma_start(out=w36_rest[s][:], in_=w36_rows[s][:, :, P:N])
-        nc.sync.dma_start(out=idx2[:], in_=offs2)
         nc.sync.dma_start(out=wgo_sb[:], in_=wgo)
+        load_scale_rows(nc.sync, w5_s, w5_scales.rearrange("a r n -> r a n"))
+        nc.sync.dma_start(out=idx2[:], in_=offs2)
+        for s in range(3):
+            nc.sync.dma_start(out=w36_rest[s][:], in_=w36_rows[s][:, :, 2 * P : N])
         for c in range(4):
             nc.sync.dma_start(out=x0_sb[c][:], in_=x0[P * c : P * (c + 1), :])
         for u in range(4):
@@ -135,7 +134,7 @@ def tile_list_herbarium_expert_votes_kernel(
                 in_=w2_raw_s[:, 512 * g : 512 * (g + 1)].rearrange("p (m t) -> p t m", t=4),
             )
 
-        w1_bf = [held([P, 2048], BF16, "w1_bf%d" % g) for g in range(2)]
+        w1_bf = [keep.tile([P, 2048], BF16, name="w1_bf", tag="w1_bf%d" % g, align_bytes=64) for g in range(2)]
 
         def round_on_gpsimd(out, in_):
             nc.gpsimd.tensor_scalar(out=out, in0=in_, scalar1=1.0, scalar2=0.0, op0=MULT, op1=ADD)
@@ -154,10 +153,33 @@ def tile_list_herbarium_expert_votes_kernel(
             w1_q[g] = keep.tile([P, 512], U32, name="w1_q", tag="w1_q%d" % g, align_bytes=64)
             nc.vector.quantize_mx(out=w1_q[g][:].bitcast(FP8), scales=w1_s[g][:], in_=w1_bf[g][:])
 
-        def features(g, b, behind):
-            h_bf[g, b] = keep.tile([P, HALF, 4], BF16, name="h_bf", tag="h_bf%d" % b, align_bytes=64)
-            for jb in range(4):
-                cols = slice(P * jb, P * (jb + 1))
+        b_sb = {}
+
+        def fp4_product(g, b, half):
+            cols = slice(256 * half, 256 * (half + 1))
+            tag = {(0, 0, 1): "w1_q1", (1, 0, 1): "w36_q0", (0, 1, 0): "w36_q1", (1, 1, 1): "h_q01"}.get((g, b, half))
+            if tag:
+                b_sb[g, b, half] = keep.tile([P, 2, 256, 2], F32, name="b_sb", tag=tag, align_bytes=64)
+            else:
+                b_sb[g, b, half] = ring.tile([P, 2, 256, 2], F32, name="b_sb", tag="b_sb", bufs=3)
+            for pair in range(2):
+                b_ps = named_bank("high", 2 * pair, [P, 2, 256]) if (g, b, half) == (1, 1, 1) else bank("high", [P, 2, 256])
+                for e in range(2):
+                    t = 2 * pair + e
+                    nc.tensor.matmul_mx(
+                        out=b_ps[:, e, :],
+                        lhsT=w2_w[g][:, 2 * P * t : 2 * P * (t + 1)].bitcast(FP4), lhsT_scale=w2_s[g][:, P * t : P * (t + 1)],
+                        rhs=v_w[b][:, cols].bitcast(FP8), rhs_scale=v_s[b][:, cols], start=True, stop=True,
+                    )
+                nc.scalar.copy(out=b_sb[g, b, half][:, pair], in_=b_ps[:].rearrange("p e n -> p n e"))
+
+        def features(g, b, half):
+            if half == 0:
+                tag = {(0, 0): "h_a", (0, 1): "h_b", (1, 0): "tab_w", (1, 1): "w1_raw01"}[g, b]
+                h_bf[g, b] = keep.tile([P, HALF, 4], BF16, name="h_bf", tag=tag, align_bytes=64)
+            fp4_product(g, b, half)
+            for jb in range(2):
+                cols = slice(256 * half + P * jb, 256 * half + P * (jb + 1))
                 a_ps = bank("low", [P, 4, P])
                 for t in range(4):
                     nc.tensor.matmul_mx(
@@ -165,24 +187,15 @@ def tile_list_herbarium_expert_votes_kernel(
                         lhsT=w1_q[g][:, P * t : P * (t + 1)].bitcast(FP8), lhsT_scale=w1_s[g][:, P * t : P * (t + 1)],
                         rhs=v_w[b][:, cols].bitcast(FP8), rhs_scale=v_s[b][:, cols], start=True, stop=True,
                     )
-                if jb in behind:
-                    a_sb = keep.tile([P, P, 4], F32, name="a_sb", tag=behind[jb][0], align_bytes=64)
-                else:
-                    a_sb = ring.tile([P, P, 4], F32, name="a_sb", tag="a_sb", bufs=6)
-                nc.scalar.copy(out=a_sb[:], in_=a_ps[:].rearrange("p t n -> p n t"))
-                b_ps = bank("high", [P, 4, P])
-                for t in range(4):
-                    nc.tensor.matmul_mx(
-                        out=b_ps[:, t, :],
-                        lhsT=w2_w[g][:, 2 * P * t : 2 * P * (t + 1)].bitcast(FP4), lhsT_scale=w2_s[g][:, P * t : P * (t + 1)],
-                        rhs=v_w[b][:, cols].bitcast(FP8), rhs_scale=v_s[b][:, cols], start=True, stop=True,
-                    )
-                nc.vector.tensor_tensor(out=h_bf[g, b][:, cols, :], in0=b_ps[:].rearrange("p t n -> p n t"), in1=a_sb[:], op=MULT)
-                if jb in behind and behind[jb][1]:
-                    behind[jb][1]()
+                nc.vector.tensor_tensor(
+                    out=h_bf[g, b][:, cols, :].rearrange("p n (q e) -> p n q e", q=2),
+                    in0=a_ps[:].rearrange("p (q e) n -> p n q e", q=2),
+                    in1=b_sb[g, b, half][:, :, P * jb : P * (jb + 1), :].rearrange("p q n e -> p n q e"), op=MULT,
+                )
 
         def quantise_h(g, b):
-            h_q[g][b] = keep.tile([P, HALF], U32, name="h_q", tag="h_q%d%d" % (g, b), align_bytes=64)
+            tag = {(0, 0): "w1_bf1", (1, 0): "h_a", (0, 1): "h_q01", (1, 1): "h_q11"}[g, b]
+            h_q[g][b] = keep.tile([P, HALF], U32, name="h_q", tag=tag, align_bytes=64)
             nc.vector.quantize_mx(
                 out=h_q[g][b][:].bitcast(FP8), scales=h_s[g][b][:], in_=h_bf[g, b][:].rearrange("p n t -> p (n t)")
             )
@@ -200,21 +213,24 @@ def tile_list_herbarium_expert_votes_kernel(
             return keep.tile(shape, dtype, name=name, tag=tag, align_bytes=64)
 
         d_last = shared([P, S], F32, "d_last", "w1_raw00")
-        e_last = held([P, S], F32, "e_last")
+        e_last = shared([P, S], F32, "e_last", "w1_raw10")
         w3_bf = {}
         w6_bf = {}
 
         def cast_w36(c):
-            if c < 3:
-                both = shared([P, 1536], BF16, "w36_bf", ("w36_bf0", "a_last", "h_bf1")[c])
+            if c == 0:
+                w3_bf[c] = shared([P, 1024], BF16, "w3_bf", "h_a")[:]
+                w6_bf[c] = held([P, 512], BF16, "w6_bf0")[:]
+            elif c < 3:
+                both = shared([P, 1536], BF16, "w36_bf", ("tab_w", "d0")[c - 1])
                 w3_bf[c], w6_bf[c] = both[:, 0:1024], both[:, 1024:1536]
             else:
-                w3_bf[c] = shared([P, 1024], BF16, "w3_bf", "h_bf0")[:]
-                w6_bf[c] = shared([P, 512], BF16, "w6_bf", "a_last")[:]
+                w3_bf[c] = shared([P, 1024], BF16, "w3_bf", "w1_q1")[:]
+                w6_bf[c] = shared([P, 512], BF16, "w6_bf", "w1_q0")[:]
             for s in range(3):
-                raw = w36_first[s][:] if c == 0 else w36_rest[s][:, :, P * (c - 1) : P * c]
+                raw = (w36_first, w36_rest)[c // 2][s][:, :, P * (c % 2) : P * (c % 2 + 1)]
                 spot = w3_bf[c][:, 512 * s : 512 * (s + 1)] if s < 2 else w6_bf[c]
-                if c == 0 and s < 2:
+                if c == 0 or (c == 1 and s < 2):
                     round_on_gpsimd(spot.rearrange("p (n j) -> p n j", j=4), raw.rearrange("p j n -> p n j"))
                     continue
                 nc.scalar.copy(
@@ -222,14 +238,14 @@ def tile_list_herbarium_expert_votes_kernel(
                 )
 
         def quantise_w36(c):
-            w36_q[c] = shared([P, 3 * P], U32, "w36_q", ("w36_q0", "votes0", "d1", "d2")[c])
+            w36_q[c] = shared([P, 3 * P], U32, "w36_q", ("w36_q0", "w36_q1", "w1_q0", "tab_w")[c])
             nc.vector.quantize_mx(out=w36_q[c][:, 0:256].bitcast(FP8), scales=w36_s[c][:, 0:256], in_=w3_bf[c])
             nc.vector.quantize_mx(out=w36_q[c][:, 256:384].bitcast(FP8), scales=w36_s[c][:, 256:384], in_=w6_bf[c])
 
         def first_factor(k):
             c, b = divmod(k, 2)
             rows = slice(P * c, P * (c + 1))
-            d_ps = named_bank("low", b, [P, HALF])
+            d_ps = named_bank("high", 1, [P, HALF]) if k == 2 else bank("high", [P, HALF])
             nc.tensor.matmul_mx(
                 out=d_ps[:], lhsT=w4_w[:, rows].bitcast(FP8), lhsT_scale=w4_s[:, rows],
                 rhs=v_w[b][:].bitcast(FP8), rhs_scale=v_s[b], start=True, stop=False,
@@ -240,7 +256,7 @@ def tile_list_herbarium_expert_votes_kernel(
                     rhs=h_q[g][b][:].bitcast(FP8), rhs_scale=h_s[g][b][:], start=False, stop=(g == 1),
                 )
             if k < 6:
-                d_neg[k] = shared([P, HALF], F32, "d_neg", "h_q11" if k == 0 else "d%d" % k)[:]
+                d_neg[k] = shared([P, HALF], F32, "d_neg", {1: "w1_q1", 2: "h_b"}.get(k, "d%d" % k))[:]
             else:
                 d_neg[k] = d_last[:, HALF * b : HALF * (b + 1)]
             nc.scalar.activation(out=d_neg[k], in_=d_ps[:], func=ACT.Copy, scale=-1.0)
@@ -248,7 +264,7 @@ def tile_list_herbarium_expert_votes_kernel(
         def second_factor(k):
             c, b = divmod(k, 2)
             rows = slice(P * c, P * (c + 1))
-            e_ps = named_bank("high", 2 if k == 4 else b, [P, HALF])
+            e_ps = bank("high", [P, HALF])
             nc.tensor.matmul_mx(
                 out=e_ps[:], lhsT=w36_q[c][:, 2 * P : 3 * P].bitcast(FP8), lhsT_scale=w36_s[c][:, 2 * P : 3 * P],
                 rhs=v_w[b][:].bitcast(FP8), rhs_scale=v_s[b], start=True, stop=False,
@@ -263,19 +279,9 @@ def tile_list_herbarium_expert_votes_kernel(
         def weight(k):
             return wgo_sb[:, HALF * (k % 2) : HALF * (k % 2 + 1)]
 
-        def new_votes(k):
-            votes[k] = shared([P, HALF], F32, "votes", ("votes0", "h_bf1", "votes2", "h_bf0")[k])[:] if k < 4 else d_neg[k]
-            return votes[k]
-
-        def vote_on_vector(k):
-            e_ps = second_factor(k)
-            nc.vector.tensor_tensor(out=new_votes(k), in0=e_ps[:], in1=d_neg[k], op=MULT)
-
         def weigh_on_gpsimd(k):
-            plain = d_neg[k]
-            if k > 3:
-                d_neg[k] = shared([P, HALF], F32, "weighed", ("e3", "d4")[k - 4])[:]
-            nc.gpsimd.tensor_tensor(out=d_neg[k], in0=plain, in1=weight(k), op=MULT)
+            votes[k] = shared([P, HALF], F32, "votes", ("tab_w", "e2", "e0", "e1", "e3", "e4")[k])[:]
+            nc.gpsimd.tensor_tensor(out=votes[k], in0=d_neg[k], in1=weight(k), op=MULT)
 
         def copy_second(k):
             e_ps = second_factor(k)
@@ -283,17 +289,14 @@ def tile_list_herbarium_expert_votes_kernel(
             nc.scalar.copy(out=e_sb[k], in_=e_ps[:])
 
         def vote_on_gpsimd(k):
-            nc.gpsimd.tensor_tensor(out=new_votes(k), in0=e_sb[k], in1=d_neg[k], op=MULT)
+            nc.gpsimd.tensor_tensor(out=votes[k], in0=e_sb[k], in1=votes[k], op=MULT)
 
         def place(k):
             c, b = divmod(k, 2)
             if b == 0:
-                page[c] = shared([P, WINDOW], F32, "page", "a_last" if c == 1 else "page%d" % c)
+                page[c] = shared([P, WINDOW], F32, "page", ("w1_raw01", "d0", "page2")[c])
             window = page[c][:].indirect(idx2[:, 32 * b : 32 * (b + 1)])
-            if k == 0:
-                nc.vector.tensor_tensor(out=window, in0=votes[k], in1=weight(k), op=MULT)
-            else:
-                nc.vector.tensor_copy(out=window, in_=votes[k])
+            nc.vector.tensor_copy(out=window, in_=votes[k])
 
         def prepare(k):
             first_factor(k)
@@ -302,7 +305,7 @@ def tile_list_herbarium_expert_votes_kernel(
             vote_on_gpsimd(k)
 
         def turn(c, hh, sig):
-            z_ps = named_bank(("low", "high")[c % 2], 3 - hh, [P, 4, P]) if c else named_bank(("low", "high")[hh], 1, [P, 4, P])
+            z_ps = named_bank(*(first_free[hh] if c < 2 else ("low", 2 * (3 - c) + hh)), [P, 4, P])
             for src in (x0_sb[c], page[c]):
                 for u in range(4):
                     lo = 256 * u + P * hh
@@ -317,9 +320,10 @@ def tile_list_herbarium_expert_votes_kernel(
             )
 
         turned = {}
+        first_free = []
 
         def turn_back(c):
-            y_ps = [named_bank(("high", "low")[c % 2], 2 + i, [P, 512]) for i in range(2)]
+            y_ps = [named_bank("low", 2 * (c % 2) + i, [P, 512]) for i in range(2)]
             both = shared([P, 2, 4, P], F32, "sig", "sig%d" % (c % 2))
             for hh in range(2):
                 sig = both[:, hh]
@@ -398,48 +402,46 @@ def tile_list_herbarium_expert_votes_kernel(
         gather(512, 1024)
         cast_w1(1, 0)
         cast_w1(1, 1)
-        features(0, 0, {})
+        features(0, 0, 0)
+        features(0, 0, 1)
+        quantise_w1(1)
+        quantise_h(0, 0)
         cast_w36(0)
-        features(0, 1, {1: ("w1_q1", lambda: quantise_w1(1)), 2: ("h_q00", lambda: quantise_h(0, 0))})
-        features(1, 0, {0: ("h_q01", lambda: quantise_h(0, 1)), 1: ("w36_q0", lambda: quantise_w36(0))})
-        features(1, 1, {0: ("h_q10", lambda: quantise_h(1, 0)), 3: ("a_last", None)})
-        first_factor(0)
-        vote_on_vector(0)
-        quantise_h(1, 1)
-        place(0)
+        features(1, 0, 0)
+        features(1, 0, 1)
+        quantise_w36(0)
+        quantise_h(1, 0)
         cast_w36(1)
-        first_factor(1)
-        e_1 = second_factor(1)
-        cast_w36(2)
+        features(0, 1, 0)
         quantise_w36(1)
-        plain = shared([P, HALF], F32, "plain", "a_last")
-        nc.vector.tensor_tensor(out=plain[:], in0=e_1[:], in1=d_neg[1], op=MULT)
-        quantise_w36(2)
-        nc.vector.tensor_tensor(out=new_votes(1), in0=plain[:], in1=weight(1), op=MULT)
-        place(1)
+        features(0, 1, 1)
+        prepare(0)
+        features(1, 1, 0)
+        features(1, 1, 1)
+        taken["high"].extend([None] * 3)
+        quantise_h(0, 1)
+        quantise_h(1, 1)
+        prepare(2)
+        place(0)
+        cast_w36(2)
         cast_w36(3)
-        first_factor(2)
-        weigh_on_gpsimd(2)
-        first_factor(3)
-        copy_second(3)
-        weigh_on_gpsimd(3)
-        vote_on_vector(2)
         quantise_w36(3)
-        vote_on_gpsimd(3)
-        place(2)
-        prepare(4)
-        place(3)
-        prepare(5)
-        turn_back(0)
+        quantise_w36(2)
+        for k in (1, 3, 4, 5):
+            prepare(k)
         first_factor(6)
         first_factor(7)
         weighed_last = shared([P, S], F32, "weighed_last", "e5")
         nc.gpsimd.tensor_tensor(out=weighed_last[:], in0=d_last[:], in1=wgo_sb[:], op=MULT)
-        finish(0)
         copy_second(6)
         copy_second(7)
-        place(4)
-        place(5)
+        first_free.extend(("high", (len(taken["high"]) + hh) % 4) for hh in range(2))
+        for k in (2, 1):
+            place(k)
+        turn_back(0)
+        finish(0)
+        for k in (3, 4, 5):
+            place(k)
         turn_back(1)
         finish(1)
         page[3] = held([P, WINDOW], F32, "page3")

@@ -230,7 +230,7 @@ def tile_list_herbarium_expert_votes_kernel(
             for s in range(3):
                 raw = (w36_first, w36_rest)[c // 2][s][:, :, P * (c % 2) : P * (c % 2 + 1)]
                 spot = w3_bf[c][:, 512 * s : 512 * (s + 1)] if s < 2 else w6_bf[c]
-                if c == 0 or (c == 1 and s < 2):
+                if c < 2 and s < 2:
                     round_on_gpsimd(spot.rearrange("p (n j) -> p n j", j=4), raw.rearrange("p j n -> p n j"))
                     continue
                 nc.scalar.copy(
@@ -245,7 +245,7 @@ def tile_list_herbarium_expert_votes_kernel(
         def first_factor(k):
             c, b = divmod(k, 2)
             rows = slice(P * c, P * (c + 1))
-            d_ps = named_bank("high", 1, [P, HALF]) if k == 2 else bank("high", [P, HALF])
+            d_ps = named_bank("high", 3, [P, HALF]) if k == 2 else bank("high", [P, HALF])
             nc.tensor.matmul_mx(
                 out=d_ps[:], lhsT=w4_w[:, rows].bitcast(FP8), lhsT_scale=w4_s[:, rows],
                 rhs=v_w[b][:].bitcast(FP8), rhs_scale=v_s[b], start=True, stop=False,
@@ -280,7 +280,7 @@ def tile_list_herbarium_expert_votes_kernel(
             return wgo_sb[:, HALF * (k % 2) : HALF * (k % 2 + 1)]
 
         def weigh_on_gpsimd(k):
-            votes[k] = shared([P, HALF], F32, "votes", ("tab_w", "e2", "e0", "e1", "e3", "e4")[k])[:]
+            votes[k] = shared([P, HALF], F32, "votes", ("tab_w", "e2", "votes2", "e1", "e3", "e4")[k])[:]
             nc.gpsimd.tensor_tensor(out=votes[k], in0=d_neg[k], in1=weight(k), op=MULT)
 
         def copy_second(k):
@@ -415,11 +415,13 @@ def tile_list_herbarium_expert_votes_kernel(
         features(0, 1, 0)
         quantise_w36(1)
         features(0, 1, 1)
-        prepare(0)
+        first_factor(0)
+        weigh_on_gpsimd(0)
+        e_first = second_factor(0)
         features(1, 1, 0)
         features(1, 1, 1)
-        taken["high"].extend([None] * 3)
         quantise_h(0, 1)
+        nc.vector.tensor_tensor(out=votes[0], in0=e_first[:], in1=votes[0], op=MULT)
         quantise_h(1, 1)
         prepare(2)
         place(0)

@@ -21,6 +21,7 @@ ACT = mybir.ActivationFunctionType
 P = 128
 HALF = 512
 WINDOW = 1376
+GPSIMD_COLUMNS = 384
 
 
 def tile_list_herbarium_expert_votes_kernel(
@@ -33,26 +34,19 @@ def tile_list_herbarium_expert_votes_kernel(
         ring = ctx.enter_context(tc.tile_pool(name="ring", bufs=2))
         psum = ctx.enter_context(tc.psum_pool(name="psum", bufs=1))
 
-        def held(shape, dtype, name):
-            return keep.tile(shape, dtype, name=name, align_bytes=64)
+        def held(shape, dtype, name, tag=None):
+            return keep.tile(shape, dtype, name=name, tag=tag or name, align_bytes=64)
 
-        taken = {"low": [], "high": []}
+        def bank(number, shape):
+            return psum.tile(shape, F32, name="bank", tag="bank%d" % number)
 
-        def bank(side, shape):
-            tile = psum.tile(shape, F32, name="bank", tag="%s%d" % (side, len(taken[side]) % 4))
-            taken[side].append(tile)
-            return tile
-
-        def named_bank(side, number, shape):
-            return psum.tile(shape, F32, name="bank", tag="%s%d" % (side, number))
-
-        def load_scale_rows(queue, plane, rows):
-            for q in range(4):
-                queue.dma_start(out=plane[32 * q : 32 * q + 4].bitcast(I32), in_=rows[4 * q : 4 * q + 4].bitcast(I32))
+        def load_scale_rows(plane, rows, quadrants):
+            for q in quadrants:
+                nc.sync.dma_start(out=plane[32 * q : 32 * q + 4].bitcast(I32), in_=rows[4 * q : 4 * q + 4].bitcast(I32))
 
         idx = keep.tile([P, S // 16], U16, name="idx")
         idx2 = keep.tile([P, S // 16], U16, name="idx2")
-        tab_w = keep.tile([P, T], U32, name="tab_w", tag="tab_w", align_bytes=64)
+        tab_w = held([P, T], U32, "tab_w")
         tab_s = held([P, T], U8, "tab_s")
         w2_raw = held([P, 2 * H], U8, "w2_raw")
         w2_raw_s = held([P, H], U8, "w2_raw_s")
@@ -60,398 +54,337 @@ def tile_list_herbarium_expert_votes_kernel(
         w4_s = held([P, N], U8, "w4_s")
         w5_w = held([P, 2, 2 * N], U8, "w5_w")
         w5_s = held([P, 2, N], U8, "w5_s")
-        w1_raw = [
-            [keep.tile([P, 4, 256], F32, name="w1_raw", tag="w1_raw%d%d" % (g, half), align_bytes=64) for half in range(2)]
-            for g in range(2)
-        ]
-        w36_first = [held([P, 4, 2 * P], F32, "w36_first%d" % s) for s in range(3)]
-        w36_rest = [keep.tile([P, 4, 2 * P], F32, name="w36_rest", tag="w36_rest%d" % s, align_bytes=64) for s in range(3)]
+        w1_raw = [held([P, 4, 256], F32, "w1_raw%d" % i) for i in range(4)]
+        late_raw = [held([P, 4, N], F32, "late_raw%d" % s) for s in range(3)]
         wgo_sb = held([P, S], F32, "wgo_sb")
         x0_sb = [held([P, S], F32, "x0_sb%d" % c) for c in range(4)]
         amp_sb = held([P, 4, 4], F32, "amp_sb")
+        amp_last = held([P, 1], F32, "amp_last")
         ident = held([P, P], F32, "ident")
 
-        amp_last = held([P, 1], F32, "amp_last")
         nc.gpsimd.memset(w2_raw_s[:].bitcast(I32), 0)
         nc.gpsimd.memset(w4_s[:].bitcast(I32), 0)
         nc.gpsimd.memset(w5_s[:].rearrange("p a n -> p (a n)").bitcast(I32), 0)
         make_identity(nc, ident[:])
 
         w1_rows = w1.rearrange("(p j) c -> p j c", j=4)
+        w3_rows = w3.rearrange("(g p j) n -> g p j n", g=2, j=4)
+        late_rows = (w3_rows[0], w3_rows[1], w6.rearrange("(p j) n -> p j n", j=4))
+        w5_scale_rows = w5_scales.rearrange("a r n -> r a n")
+
+        def load_w1(i):
+            nc.sync.dma_start(out=w1_raw[i][:], in_=w1_rows[:, :, 256 * i : 256 * (i + 1)])
+
         nc.sync.dma_start(out=idx[:], in_=offs)
         for q in range(4):
             nc.sync.dma_start(
                 out=tab_s[32 * q : 32 * (q + 1)].bitcast(I32),
                 in_=tab_scales[0][4 * q : 4 * q + 4].bitcast(I32).unsqueeze(0).to_broadcast([8, 4, T // 4]),
             )
-        for half in range(2):
-            nc.sync.dma_start(out=w1_raw[0][half][:], in_=w1_rows[:, :, 256 * half : 256 * (half + 1)])
         nc.sync.dma_start(out=w2_raw[:].bitcast(I32), in_=w2_words[0].bitcast(I32))
-        load_scale_rows(nc.sync, w2_raw_s, w2_scales[0])
         nc.sync.dma_start(out=tab_w[:].bitcast(I32), in_=tab_words[0].rearrange("p n t -> p (n t)").bitcast(I32))
-        for half in range(2):
-            nc.sync.dma_start(out=w1_raw[1][half][:], in_=w1_rows[:, :, 512 + 256 * half : 512 + 256 * (half + 1)])
-        w3_rows = w3.rearrange("(g p j) n -> g p j n", g=2, j=4)
-        w36_rows = (w3_rows[0], w3_rows[1], w6.rearrange("(p j) n -> p j n", j=4))
-        for s in range(3):
-            nc.sync.dma_start(out=w36_first[s][:], in_=w36_rows[s][:, :, 0 : 2 * P])
+        load_w1(0)
+        load_scale_rows(w2_raw_s, w2_scales[0], range(4))
+        for i in range(1, 4):
+            load_w1(i)
+        nc.sync.dma_start(out=late_raw[0][:], in_=late_rows[0])
+        load_scale_rows(w4_s, w4_scales[0], (0, 1))
+        nc.sync.dma_start(out=late_raw[1][:], in_=late_rows[1])
+        load_scale_rows(w4_s, w4_scales[0], (2, 3))
+        nc.sync.dma_start(out=late_raw[2][:], in_=late_rows[2])
+        load_scale_rows(w5_s, w5_scale_rows, (0, 1))
         nc.sync.dma_start(out=w4_w[:].bitcast(I32), in_=w4_words[0].rearrange("p n t -> p (n t)").bitcast(I32))
         nc.sync.dma_start(out=w5_w[:].bitcast(I32), in_=w5_words.rearrange("a p b -> p a b").bitcast(I32))
-        load_scale_rows(nc.sync, w4_s, w4_scales[0])
+        load_scale_rows(w5_s, w5_scale_rows, (2, 3))
         nc.sync.dma_start(out=wgo_sb[:], in_=wgo)
-        load_scale_rows(nc.sync, w5_s, w5_scales.rearrange("a r n -> r a n"))
         nc.sync.dma_start(out=idx2[:], in_=offs2)
-        for s in range(3):
-            nc.sync.dma_start(out=w36_rest[s][:], in_=w36_rows[s][:, :, 2 * P : N])
         for c in range(4):
             nc.sync.dma_start(out=x0_sb[c][:], in_=x0[P * c : P * (c + 1), :])
         for u in range(4):
             nc.sync.dma_start(out=amp_sb[32 * u : 32 * (u + 1)], in_=amp.rearrange("(c a t) -> a c t", c=4, t=4))
         nc.sync.dma_start(out=amp_last[:], in_=amp[N - P : N].unsqueeze(1))
 
-        v_w = [held([P, HALF], U32, "v_w%d" % b) for b in range(2)]
         v_s_all = held([P, S], U8, "v_s_all")
         v_s = [v_s_all[:, HALF * b : HALF * (b + 1)] for b in range(2)]
-        w1_q = {}
-        w1_s = [held([P, 512], U8, "w1_s%d" % g) for g in range(2)]
-        w2_w = [held([P, 1024], U8, "w2_w%d" % g) for g in range(2)]
-        w2_s = [held([P, 512], U8, "w2_s%d" % g) for g in range(2)]
-        h_q = [[None, None], [None, None]]
-        h_bf = {}
-        h_s = [[held([P, HALF], U8, "h_s%d%d" % (g, b)) for b in range(2)] for g in range(2)]
+        v_w = {}
+        w2_w = held([P, 2 * H], U8, "w2_w")
+        w2_s = held([P, H], U8, "w2_s")
+        w1_bf, w1_q, w1_s = {}, {}, {}
+        h_bf, h_q, h_s = {}, {}, {}
+        late_bf, late_q, late_s = {}, {}, {}
 
-        def gather(lo, hi):
-            b = lo // HALF
-            nc.vector.tensor_copy(out=v_w[b][:, lo - HALF * b : hi - HALF * b], in_=tab_w[:].indirect(idx[:, lo // 16 : hi // 16]))
-
-        def deal_w2(g):
-            nc.vector.tensor_copy(
-                out=w2_w[g][:].bitcast(U16).rearrange("p (t m) -> p t m", t=4),
-                in_=w2_raw[:, 1024 * g : 1024 * (g + 1)].bitcast(U16).rearrange("p (m t) -> p t m", t=4),
-            )
-            nc.vector.tensor_copy(
-                out=w2_s[g][:].rearrange("p (t m) -> p t m", t=4),
-                in_=w2_raw_s[:, 512 * g : 512 * (g + 1)].rearrange("p (m t) -> p t m", t=4),
-            )
-
-        w1_bf = [keep.tile([P, 2048], BF16, name="w1_bf", tag="w1_bf%d" % g, align_bytes=64) for g in range(2)]
+        def gather_words(b, tag):
+            v_w[b] = held([P, HALF], U32, "v_w%d" % b, tag)
+            nc.vector.tensor_copy(out=v_w[b][:], in_=tab_w[:].indirect(idx[:, 32 * b : 32 * (b + 1)]))
 
         def round_on_gpsimd(out, in_):
             nc.gpsimd.tensor_scalar(out=out, in0=in_, scalar1=1.0, scalar2=0.0, op0=MULT, op1=ADD)
 
-        def cast_w1(g, half):
-            if g == 1:
+        def round_w1(g, lo, hi, on_gpsimd):
+            raw = w1_raw[2 * g + lo // 64][:, :, 4 * (lo % 64) : 4 * (lo % 64 + hi - lo)]
+            if on_gpsimd:
                 dealt = w1_bf[g][:].rearrange("p (t m j) -> p m t j", t=4, j=4)
-                round_on_gpsimd(dealt[:, 64 * half : 64 * (half + 1)], w1_raw[g][half][:].rearrange("p j (m t) -> p m t j", t=4))
-                return
-            dealt = w1_bf[g][:].rearrange("p (t m j) -> p m j t", t=4, j=4)
-            nc.scalar.copy(
-                out=dealt[:, 64 * half : 64 * (half + 1)], in_=w1_raw[g][half][:].rearrange("p j (m t) -> p m j t", t=4)
-            )
+                round_on_gpsimd(dealt[:, lo:hi], raw.rearrange("p j (m t) -> p m t j", t=4))
+            else:
+                dealt = w1_bf[g][:].rearrange("p (t m j) -> p m j t", t=4, j=4)
+                nc.scalar.copy(out=dealt[:, lo:hi], in_=raw.rearrange("p j (m t) -> p m j t", t=4))
+
+        def quantise(rounded, name, tag=None):
+            codes = held([P, HALF], U32, name + "_q", tag)
+            scales = held([P, HALF], U8, name + "_s")
+            nc.vector.quantize_mx(out=codes[:].bitcast(FP8), scales=scales[:], in_=rounded)
+            return codes, scales
 
         def quantise_w1(g):
-            w1_q[g] = keep.tile([P, 512], U32, name="w1_q", tag="w1_q%d" % g, align_bytes=64)
-            nc.vector.quantize_mx(out=w1_q[g][:].bitcast(FP8), scales=w1_s[g][:], in_=w1_bf[g][:])
-
-        b_sb = {}
-
-        def fp4_product(g, b, half):
-            cols = slice(256 * half, 256 * (half + 1))
-            tag = {(0, 0, 1): "w1_q1", (1, 0, 1): "w36_q0", (0, 1, 0): "w36_q1", (1, 1, 1): "h_q01"}.get((g, b, half))
-            if tag:
-                b_sb[g, b, half] = keep.tile([P, 2, 256, 2], F32, name="b_sb", tag=tag, align_bytes=64)
-            else:
-                b_sb[g, b, half] = ring.tile([P, 2, 256, 2], F32, name="b_sb", tag="b_sb", bufs=3)
-            for pair in range(2):
-                b_ps = named_bank("high", 2 * pair, [P, 2, 256]) if (g, b, half) == (1, 1, 1) else bank("high", [P, 2, 256])
-                for e in range(2):
-                    t = 2 * pair + e
-                    nc.tensor.matmul_mx(
-                        out=b_ps[:, e, :],
-                        lhsT=w2_w[g][:, 2 * P * t : 2 * P * (t + 1)].bitcast(FP4), lhsT_scale=w2_s[g][:, P * t : P * (t + 1)],
-                        rhs=v_w[b][:, cols].bitcast(FP8), rhs_scale=v_s[b][:, cols], start=True, stop=True,
-                    )
-                nc.scalar.copy(out=b_sb[g, b, half][:, pair], in_=b_ps[:].rearrange("p e n -> p n e"))
-
-        def features(g, b, half):
-            if half == 0:
-                tag = {(0, 0): "h_a", (0, 1): "h_b", (1, 0): "tab_w", (1, 1): "w1_raw01"}[g, b]
-                h_bf[g, b] = keep.tile([P, HALF, 4], BF16, name="h_bf", tag=tag, align_bytes=64)
-            fp4_product(g, b, half)
-            for jb in range(2):
-                cols = slice(256 * half + P * jb, 256 * half + P * (jb + 1))
-                a_ps = bank("low", [P, 4, P])
-                for t in range(4):
-                    nc.tensor.matmul_mx(
-                        out=a_ps[:, t, :],
-                        lhsT=w1_q[g][:, P * t : P * (t + 1)].bitcast(FP8), lhsT_scale=w1_s[g][:, P * t : P * (t + 1)],
-                        rhs=v_w[b][:, cols].bitcast(FP8), rhs_scale=v_s[b][:, cols], start=True, stop=True,
-                    )
-                nc.vector.tensor_tensor(
-                    out=h_bf[g, b][:, cols, :].rearrange("p n (q e) -> p n q e", q=2),
-                    in0=a_ps[:].rearrange("p (q e) n -> p n q e", q=2),
-                    in1=b_sb[g, b, half][:, :, P * jb : P * (jb + 1), :].rearrange("p q n e -> p n q e"), op=MULT,
-                )
+            w1_q[g], w1_s[g] = quantise(w1_bf[g][:], "w1_%d" % g)
 
         def quantise_h(g, b):
-            tag = {(0, 0): "w1_bf1", (1, 0): "h_a", (0, 1): "h_q01", (1, 1): "h_q11"}[g, b]
-            h_q[g][b] = keep.tile([P, HALF], U32, name="h_q", tag=tag, align_bytes=64)
-            nc.vector.quantize_mx(
-                out=h_q[g][b][:].bitcast(FP8), scales=h_s[g][b][:], in_=h_bf[g, b][:].rearrange("p n t -> p (n t)")
-            )
+            h_q[g, b], h_s[g, b] = quantise(h_bf[g, b][:].rearrange("p n t -> p (n t)"), "h_%d%d" % (g, b))
 
-        w36_q = {}
-        e_sb = {}
-        w36_s = [held([P, 3 * P], U8, "w36_s%d" % c) for c in range(4)]
-        page = {}
-        d_neg = {}
-        votes = {}
-        y_bf = [keep.tile([P, 1024], BF16, name="y_bf%d" % c, tag="y_bf%d" % c, align_bytes=64) for c in range(4)]
-        y_s = held([P, 256], U8, "y_s")
+        def quantise_late(s, tag=None):
+            late_q[s], late_s[s] = quantise(late_bf[s][:], "late_%d" % s, tag)
 
-        def shared(shape, dtype, name, tag):
-            return keep.tile(shape, dtype, name=name, tag=tag, align_bytes=64)
-
-        d_last = shared([P, S], F32, "d_last", "w1_raw00")
-        e_last = shared([P, S], F32, "e_last", "w1_raw10")
-        w3_bf = {}
-        w6_bf = {}
-
-        def cast_w36(c):
-            if c == 0:
-                w3_bf[c] = shared([P, 1024], BF16, "w3_bf", "h_a")[:]
-                w6_bf[c] = held([P, 512], BF16, "w6_bf0")[:]
-            elif c < 3:
-                both = shared([P, 1536], BF16, "w36_bf", ("tab_w", "d0")[c - 1])
-                w3_bf[c], w6_bf[c] = both[:, 0:1024], both[:, 1024:1536]
-            else:
-                w3_bf[c] = shared([P, 1024], BF16, "w3_bf", "w1_q1")[:]
-                w6_bf[c] = shared([P, 512], BF16, "w6_bf", "w1_q0")[:]
-            for s in range(3):
-                raw = (w36_first, w36_rest)[c // 2][s][:, :, P * (c % 2) : P * (c % 2 + 1)]
-                spot = w3_bf[c][:, 512 * s : 512 * (s + 1)] if s < 2 else w6_bf[c]
-                if c < 2 and s < 2:
-                    round_on_gpsimd(spot.rearrange("p (n j) -> p n j", j=4), raw.rearrange("p j n -> p n j"))
-                    continue
+        def round_late(s, tag, gpsimd_columns):
+            late_bf[s] = held([P, 4 * N], BF16, "late_bf%d" % s, tag)
+            if gpsimd_columns:
+                round_on_gpsimd(
+                    late_bf[s][:, 0 : 4 * gpsimd_columns].rearrange("p (n j) -> p n j", j=4),
+                    late_raw[s][:, :, 0:gpsimd_columns].rearrange("p j n -> p n j"),
+                )
+            for lo in range(gpsimd_columns, N, 256):
+                hi = min(lo + 256, N)
                 nc.scalar.copy(
-                    out=spot.rearrange("p (a i j) -> p a j i", i=4, j=4), in_=raw.rearrange("p j (a i) -> p a j i", i=4)
+                    out=late_bf[s][:, 4 * lo : 4 * hi].rearrange("p (a i j) -> p a j i", i=4, j=4),
+                    in_=late_raw[s][:, :, lo:hi].rearrange("p j (a i) -> p a j i", i=4),
                 )
 
-        def quantise_w36(c):
-            w36_q[c] = shared([P, 3 * P], U32, "w36_q", ("w36_q0", "w36_q1", "w1_q0", "tab_w")[c])
-            nc.vector.quantize_mx(out=w36_q[c][:, 0:256].bitcast(FP8), scales=w36_s[c][:, 0:256], in_=w3_bf[c])
-            nc.vector.quantize_mx(out=w36_q[c][:, 256:384].bitcast(FP8), scales=w36_s[c][:, 256:384], in_=w6_bf[c])
+        def features(g, b, tag, b_tag):
+            h_bf[g, b] = held([P, HALF, 4], BF16, "h_bf", tag)
+            b_both = held([P, 2, 2, 256, 2], F32, "b_sb", b_tag)
+            for half in range(2):
+                step = 4 * b + 2 * g + half
+                cols = slice(256 * half, 256 * (half + 1))
+                b_sb = b_both[:, half]
+                for pair in range(2):
+                    b_ps = bank(3 + (2 * step + pair) % 3, [P, 2, 256])
+                    for e in range(2):
+                        lo = HALF * g + P * (2 * pair + e)
+                        nc.tensor.matmul_mx(
+                            out=b_ps[:, e, :],
+                            lhsT=w2_w[:, 2 * lo : 2 * (lo + P)].bitcast(FP4), lhsT_scale=w2_s[:, lo : lo + P],
+                            rhs=v_w[b][:, cols].bitcast(FP8), rhs_scale=v_s[b][:, cols], start=True, stop=True,
+                        )
+                    nc.scalar.copy(out=b_sb[:, pair], in_=b_ps[:].rearrange("p e n -> p n e"))
+                for jb in range(2):
+                    cols = slice(256 * half + P * jb, 256 * half + P * (jb + 1))
+                    a_ps = bank((2 * step + jb) % 3, [P, 4, P])
+                    for t in range(4):
+                        nc.tensor.matmul_mx(
+                            out=a_ps[:, t, :],
+                            lhsT=w1_q[g][:, P * t : P * (t + 1)].bitcast(FP8), lhsT_scale=w1_s[g][:, P * t : P * (t + 1)],
+                            rhs=v_w[b][:, cols].bitcast(FP8), rhs_scale=v_s[b][:, cols], start=True, stop=True,
+                        )
+                    nc.vector.tensor_tensor(
+                        out=h_bf[g, b][:, cols, :].rearrange("p n (q e) -> p n q e", q=2),
+                        in0=a_ps[:].rearrange("p (q e) n -> p n q e", q=2),
+                        in1=b_sb[:, :, P * jb : P * (jb + 1), :].rearrange("p q n e -> p n q e"), op=MULT,
+                    )
 
-        def first_factor(k):
+        d_neg, e_sb, votes, page = {}, {}, {}, {}
+
+        def first_sum(k, number):
             c, b = divmod(k, 2)
             rows = slice(P * c, P * (c + 1))
-            d_ps = named_bank("high", 3, [P, HALF]) if k == 2 else bank("high", [P, HALF])
+            d_ps = bank(number, [P, HALF])
             nc.tensor.matmul_mx(
                 out=d_ps[:], lhsT=w4_w[:, rows].bitcast(FP8), lhsT_scale=w4_s[:, rows],
                 rhs=v_w[b][:].bitcast(FP8), rhs_scale=v_s[b], start=True, stop=False,
             )
             for g in range(2):
                 nc.tensor.matmul_mx(
-                    out=d_ps[:], lhsT=w36_q[c][:, P * g : P * (g + 1)].bitcast(FP8), lhsT_scale=w36_s[c][:, P * g : P * (g + 1)],
-                    rhs=h_q[g][b][:].bitcast(FP8), rhs_scale=h_s[g][b][:], start=False, stop=(g == 1),
+                    out=d_ps[:], lhsT=late_q[g][:, rows].bitcast(FP8), lhsT_scale=late_s[g][:, rows],
+                    rhs=h_q[g, b][:].bitcast(FP8), rhs_scale=h_s[g, b][:], start=False, stop=(g == 1),
                 )
-            if k < 6:
-                d_neg[k] = shared([P, HALF], F32, "d_neg", {1: "w1_q1", 2: "h_b"}.get(k, "d%d" % k))[:]
-            else:
-                d_neg[k] = d_last[:, HALF * b : HALF * (b + 1)]
             nc.scalar.activation(out=d_neg[k], in_=d_ps[:], func=ACT.Copy, scale=-1.0)
 
-        def second_factor(k):
+        def second_sum(k, number):
             c, b = divmod(k, 2)
             rows = slice(P * c, P * (c + 1))
-            e_ps = bank("high", [P, HALF])
+            e_ps = bank(number, [P, HALF])
             nc.tensor.matmul_mx(
-                out=e_ps[:], lhsT=w36_q[c][:, 2 * P : 3 * P].bitcast(FP8), lhsT_scale=w36_s[c][:, 2 * P : 3 * P],
+                out=e_ps[:], lhsT=late_q[2][:, rows].bitcast(FP8), lhsT_scale=late_s[2][:, rows],
                 rhs=v_w[b][:].bitcast(FP8), rhs_scale=v_s[b], start=True, stop=False,
             )
             for g in range(2):
                 nc.tensor.matmul_mx(
                     out=e_ps[:], lhsT=w5_w[:, g, 2 * P * c : 2 * P * (c + 1)].bitcast(FP4), lhsT_scale=w5_s[:, g, rows],
-                    rhs=h_q[g][b][:].bitcast(FP8), rhs_scale=h_s[g][b][:], start=False, stop=(g == 1),
+                    rhs=h_q[g, b][:].bitcast(FP8), rhs_scale=h_s[g, b][:], start=False, stop=(g == 1),
                 )
             return e_ps
 
-        def weight(k):
-            return wgo_sb[:, HALF * (k % 2) : HALF * (k % 2 + 1)]
-
-        def weigh_on_gpsimd(k):
-            votes[k] = shared([P, HALF], F32, "votes", ("tab_w", "e2", "votes2", "e1", "e3", "e4")[k])[:]
-            nc.gpsimd.tensor_tensor(out=votes[k], in0=d_neg[k], in1=weight(k), op=MULT)
-
-        def copy_second(k):
-            e_ps = second_factor(k)
-            e_sb[k] = shared([P, HALF], F32, "e_sb", "e%d" % k)[:] if k < 6 else e_last[:, HALF * (k - 6) : HALF * (k - 5)]
-            nc.scalar.copy(out=e_sb[k], in_=e_ps[:])
-
-        def vote_on_gpsimd(k):
-            nc.gpsimd.tensor_tensor(out=votes[k], in0=e_sb[k], in1=votes[k], op=MULT)
+        def weigh(k, tag):
+            votes[k] = held([P, HALF], F32, "votes", tag)[:]
+            nc.gpsimd.tensor_tensor(out=votes[k], in0=d_neg[k], in1=wgo_sb[:, HALF * (k % 2) : HALF * (k % 2 + 1)], op=MULT)
 
         def place(k):
             c, b = divmod(k, 2)
             if b == 0:
-                page[c] = shared([P, WINDOW], F32, "page", ("w1_raw01", "d0", "page2")[c])
-            window = page[c][:].indirect(idx2[:, 32 * b : 32 * (b + 1)])
-            nc.vector.tensor_copy(out=window, in_=votes[k])
+                page[c] = held([P, WINDOW], F32, "page", ("w1_raw0", "page1", "w1_raw2")[c])
+            nc.vector.tensor_copy(out=page[c][:].indirect(idx2[:, 32 * b : 32 * (b + 1)]), in_=votes[k])
 
-        def prepare(k):
-            first_factor(k)
-            copy_second(k)
-            weigh_on_gpsimd(k)
-            vote_on_gpsimd(k)
-
-        def turn(c, hh, sig):
-            z_ps = named_bank(*(first_free[hh] if c < 2 else ("low", 2 * (3 - c) + hh)), [P, 4, P])
+        def turn(c, z_banks, y_spot, sig):
+            z_ps = [bank(number, [P, 4, P]) for number in z_banks]
             for src in (x0_sb[c], page[c]):
-                for u in range(4):
-                    lo = 256 * u + P * hh
-                    nc.tensor.matmul(
-                        out=z_ps[:, u, :], lhsT=src[:, lo : lo + P], rhs=ident[:], is_transpose=True,
-                        start=(src is x0_sb[c] and u == 0), stop=(src is page[c] and u == 3),
-                    )
-            nc.scalar.activation(
-                out=sig.rearrange("p t q -> p q t"),
-                in_=z_ps[:].rearrange("p u (a t) -> p (u a) t", t=4),
-                func=ACT.Sigmoid,
-            )
-
-        turned = {}
-        first_free = []
-
-        def turn_back(c):
-            y_ps = [named_bank("low", 2 * (c % 2) + i, [P, 512]) for i in range(2)]
-            both = shared([P, 2, 4, P], F32, "sig", "sig%d" % (c % 2))
+                for hh in range(2):
+                    for u in range(4):
+                        lo = 256 * u + P * hh
+                        nc.tensor.matmul(
+                            out=z_ps[hh][:, u, :], lhsT=src[:, lo : lo + P], rhs=ident[:], is_transpose=True,
+                            start=(src is x0_sb[c] and u == 0), stop=(src is page[c] and u == 3),
+                        )
             for hh in range(2):
-                sig = both[:, hh]
-                turn(c, hh, sig)
+                nc.scalar.activation(
+                    out=sig[hh].rearrange("p t q -> p q t"),
+                    in_=z_ps[hh][:].rearrange("p u (a t) -> p (u a) t", t=4),
+                    func=ACT.Sigmoid,
+                )
+            for hh in range(2):
                 for t in range(4):
-                    spot = y_ps[t // 2][:, 256 * (t % 2) + P * hh : 256 * (t % 2) + P * (hh + 1)]
-                    nc.tensor.transpose(spot, sig[:, t, :], ident[:])
-            turned[c] = y_ps
+                    nc.tensor.transpose(y_spot(hh, t), sig[hh][:, t, :], ident[:])
+
+        y_bf = held([P, 3, S], BF16, "y_bf")
+        y_s = held([P, 256], U8, "y_s")
+        turn_banks = ((4, 5), (0, 1))
 
         def finish(c):
+            y_ps = [bank(number, [P, HALF]) for number in turn_banks[(c + 1) % 2]]
+            both = held([P, 2, 4, P], F32, "sig", "sig%d" % (c % 2))
+            turn(
+                c, turn_banks[c % 2],
+                lambda hh, t: y_ps[t // 2][:, 256 * (t % 2) + P * hh : 256 * (t % 2) + P * (hh + 1)],
+                [both[:, hh] for hh in range(2)],
+            )
             y = ring.tile([P, 4, 256], F32, tag="y")
-            y_ps = turned[c]
             for t in range(4):
                 nc.scalar.activation(
                     out=y[:, t, :], in_=y_ps[t // 2][:, 256 * (t % 2) : 256 * (t % 2 + 1)], func=ACT.Copy,
                     scale=amp_sb[:, c, t : t + 1],
                 )
             nc.scalar.copy(
-                out=y_bf[c][:].rearrange("p (a i t) -> p a t i", i=4, t=4), in_=y[:].rearrange("p t (a i) -> p a t i", i=4)
+                out=y_bf[:, c, :].rearrange("p (a i t) -> p a t i", i=4, t=4), in_=y[:].rearrange("p t (a i) -> p a t i", i=4)
             )
             rows = out_0[P * c : P * (c + 1), :].rearrange("(a t) m -> a t m", t=4)
             for u in range(4):
                 nc.sync.dma_start(out=rows[:, :, 256 * u : 256 * (u + 1)], in_=y[32 * u : 32 * (u + 1)])
 
-        def finish_last():
-            c = 3
-            z = held([P, S], F32, "z_last")
-            y = held([P, S], F32, "y_last")
-            y_q = held([P, 256], U32, "y_q_last")
-            halves = [slice(HALF * hh, HALF * (hh + 1)) for hh in range(2)]
-            for cols in halves:
-                nc.vector.tensor_tensor(out=z[:, cols], in0=page[c][:, cols], in1=x0_sb[c][:, cols], op=ADD)
-            store_planes((2, 1, 0), keep.tile([P, 3, 256], U32, name="y_q_early", tag="e5", align_bytes=64))
-            y_ps = [named_bank("low", 2 + hh, [P, 4, P]) for hh in range(2)]
-            for hh in range(2):
-                sig = shared([P, 4, P], F32, "sig", "sig3%d" % hh)[:]
-                turn(c, hh, sig)
-                for t in range(4):
-                    nc.tensor.transpose(y_ps[hh][:, t, :], sig[:, t, :], ident[:])
-            s_rows = shared([P, S], F32, "s_rows", "sig30")
-            for cols in halves:
-                nc.scalar.activation(out=s_rows[:, cols], in_=z[:, cols], func=ACT.Sigmoid)
-            for hh in range(2):
-                nc.vector.tensor_tensor(
-                    out=y_bf[c][:, halves[hh]].rearrange("p (m t) -> p m t", t=4), in0=y_ps[hh][:].rearrange("p t m -> p m t"),
-                    in1=amp_sb[:, c, :].unsqueeze(1).to_broadcast([P, P, 4]), op=MULT,
-                )
-            words = out_1[0, 32 * c : 32 * (c + 1)].rearrange("a (u m) t -> u a (m t)", u=4).bitcast(I32)
-            for hh in range(2):
-                cols = slice(P * hh, P * (hh + 1))
-                nc.vector.quantize_mx(out=y_q[:, cols].bitcast(FP8), scales=y_s[4 * c : P, cols], in_=y_bf[c][:, halves[hh]])
-                nc.sync.dma_start(out=words[:, :, cols], in_=y_q[:, cols].bitcast(I32))
-                if hh == 0:
-                    nc.vector.tensor_scalar(out=y[:, halves[0]], in0=s_rows[:, halves[0]], scalar1=amp_last[:, 0:1], scalar2=None, op0=MULT)
-                else:
-                    nc.scalar.activation(out=y[:, halves[1]], in_=s_rows[:, halves[1]], func=ACT.Copy, scale=amp_last[:, 0:1])
-                nc.sync.dma_start(out=out_0[N - P : N, halves[hh]], in_=y[:, halves[hh]])
-
-        def store_planes(tiles, y_q):
-            for c in tiles:
-                nc.vector.quantize_mx(out=y_q[:, c, :].bitcast(FP8), scales=y_s[4 * c : P, :], in_=y_bf[c][:])
+        def store_early_planes():
+            y_q = held([P, 3, 256], U32, "y_q_early", "tab_w")
+            for c in range(3):
+                nc.vector.quantize_mx(out=y_q[:, c, :].bitcast(FP8), scales=y_s[4 * c : P, :], in_=y_bf[:, c, :])
             words = out_1[0].rearrange("(c a) m t -> a c (m t)", c=4).bitcast(I32)
             for u in range(4):
                 nc.sync.dma_start(
                     out=words[:, 0:3, 256 * u : 256 * (u + 1)], in_=y_q[32 * u : 32 * (u + 1)].bitcast(I32)
                 )
 
+        def finish_last():
+            c = 3
+            halves = [slice(HALF * hh, HALF * (hh + 1)) for hh in range(2)]
+            z = held([P, S], F32, "z_last", "y_bf")
+            y = held([P, S], F32, "y_last")
+            y_last_bf = held([P, S], BF16, "y_last_bf")
+            y_q = held([P, 256], U32, "y_q_last")
+            for cols in halves:
+                nc.vector.tensor_tensor(out=z[:, cols], in0=page[c][:, cols], in1=x0_sb[c][:, cols], op=ADD)
+            y_ps = [bank(number, [P, 4, P]) for number in turn_banks[(c + 1) % 2]]
+            sig = [held([P, 4, P], F32, "sig", "sig3%d" % hh)[:] for hh in range(2)]
+            turn(c, turn_banks[c % 2], lambda hh, t: y_ps[hh][:, t, :], sig)
+            s_rows = held([P, S], F32, "s_rows", "sig30")
+            for cols in halves:
+                nc.scalar.activation(out=s_rows[:, cols], in_=z[:, cols], func=ACT.Sigmoid)
+            for hh in range(2):
+                nc.vector.tensor_tensor(
+                    out=y_last_bf[:, halves[hh]].rearrange("p (m t) -> p m t", t=4), in0=y_ps[hh][:].rearrange("p t m -> p m t"),
+                    in1=amp_sb[:, c, :].unsqueeze(1).to_broadcast([P, P, 4]), op=MULT,
+                )
+            words = out_1[0, 32 * c : 32 * (c + 1)].rearrange("a (u m) t -> u a (m t)", u=4).bitcast(I32)
+            for hh in range(2):
+                cols = slice(P * hh, P * (hh + 1))
+                nc.vector.quantize_mx(out=y_q[:, cols].bitcast(FP8), scales=y_s[4 * c : P, cols], in_=y_last_bf[:, halves[hh]])
+                nc.sync.dma_start(out=words[:, :, cols], in_=y_q[:, cols].bitcast(I32))
+                if hh == 0:
+                    nc.vector.tensor_scalar(out=y[:, halves[0]], in0=s_rows[:, halves[0]], scalar1=amp_last[:, 0:1], scalar2=None, op0=MULT)
+                else:
+                    nc.scalar.activation(out=y[:, halves[1]], in_=s_rows[:, halves[1]], func=ACT.Copy, scale=amp_last[:, 0:1])
+                nc.sync.dma_start(out=out_0[N - P : N, halves[hh]], in_=y[:, halves[hh]])
+            for u in range(4):
+                nc.sync.dma_start(
+                    out=out_2[0][:, 256 * u : 256 * (u + 1)].bitcast(I32), in_=y_s[32 * u : 32 * u + 16, :].bitcast(I32)
+                )
+
         nc.vector.tensor_copy(out=v_s_all[:], in_=tab_s[:].indirect(idx[:]))
-        deal_w2(0)
-        deal_w2(1)
-        cast_w1(0, 0)
-        cast_w1(0, 1)
+        nc.vector.tensor_copy(
+            out=w2_w[:].bitcast(U16).rearrange("p (g t m) -> p g t m", g=2, t=4),
+            in_=w2_raw[:].bitcast(U16).rearrange("p (g m t) -> p g t m", g=2, t=4),
+        )
+        gather_words(0, None)
+        nc.vector.tensor_copy(
+            out=w2_s[:].rearrange("p (g t m) -> p g t m", g=2, t=4),
+            in_=w2_raw_s[:].rearrange("p (g m t) -> p g t m", g=2, t=4),
+        )
+        gather_words(1, "w2_raw_s")
+        w1_bf[0] = held([P, 4 * HALF], BF16, "w1_bf")
+        round_w1(0, 0, 64, False)
+        round_w1(0, 64, 96, False)
+        round_w1(0, 96, 128, True)
         quantise_w1(0)
-        gather(0, 256)
-        gather(256, 512)
-        gather(512, 1024)
-        cast_w1(1, 0)
-        cast_w1(1, 1)
-        features(0, 0, 0)
-        features(0, 0, 1)
+        w1_bf[1] = held([P, 4 * HALF], BF16, "w1_bf")
+        round_w1(1, 0, 64, True)
+        round_w1(1, 64, 128, True)
+
+        features(0, 0, "rounded_a", "w1_raw1")
         quantise_w1(1)
         quantise_h(0, 0)
-        cast_w36(0)
-        features(1, 0, 0)
-        features(1, 0, 1)
-        quantise_w36(0)
+        round_late(0, "rounded_a", GPSIMD_COLUMNS)
+        features(1, 0, "rounded_b", "b_sb0")
+        round_late(1, None, 0)
+        quantise_late(0)
         quantise_h(1, 0)
-        cast_w36(1)
-        features(0, 1, 0)
-        quantise_w36(1)
-        features(0, 1, 1)
-        first_factor(0)
-        weigh_on_gpsimd(0)
-        e_first = second_factor(0)
-        features(1, 1, 0)
-        features(1, 1, 1)
+        round_late(2, "rounded_b", GPSIMD_COLUMNS)
+        features(0, 1, "rounded_c", "w1_raw1")
+        quantise_late(1, "w1_raw1")
         quantise_h(0, 1)
+        quantise_late(2)
+
+        last = held([P, 2, S], F32, "last", "tab_w")
+        for k in range(8):
+            d_neg[k] = held([P, HALF], F32, "d%d" % k)[:] if k < 6 else last[:, 0, HALF * (k - 6) : HALF * (k - 5)]
+        for k in range(1, 8):
+            e_sb[k] = held([P, HALF], F32, "e%d" % k)[:] if k < 6 else last[:, 1, HALF * (k - 6) : HALF * (k - 5)]
+        first_sum(0, 6)
+        e_first = second_sum(0, 7)
+        weigh(0, "rounded_b")
+        features(1, 1, "rounded_a", "b_sb0")
         nc.vector.tensor_tensor(out=votes[0], in0=e_first[:], in1=votes[0], op=MULT)
         quantise_h(1, 1)
-        prepare(2)
         place(0)
-        cast_w36(2)
-        cast_w36(3)
-        quantise_w36(3)
-        quantise_w36(2)
-        for k in (1, 3, 4, 5):
-            prepare(k)
-        first_factor(6)
-        first_factor(7)
-        weighed_last = shared([P, S], F32, "weighed_last", "e5")
-        nc.gpsimd.tensor_tensor(out=weighed_last[:], in0=d_last[:], in1=wgo_sb[:], op=MULT)
-        copy_second(6)
-        copy_second(7)
-        first_free.extend(("high", (len(taken["high"]) + hh) % 4) for hh in range(2))
-        for k in (2, 1):
+
+        order = (2, 1, 4, 3, 5, 6, 7)
+        sum_banks = (4, 5, 3, 6)
+        for i, k in enumerate(order):
+            first_sum(k, sum_banks[2 * i % 4])
+            nc.scalar.copy(out=e_sb[k], in_=second_sum(k, sum_banks[(2 * i + 1) % 4])[:])
+        freed = "rounded_a"
+        for k in order[:5]:
+            weigh(k, freed)
+            nc.gpsimd.tensor_tensor(out=votes[k], in0=e_sb[k], in1=votes[k], op=MULT)
+            freed = "e%d" % k
             place(k)
-        turn_back(0)
-        finish(0)
-        for k in (3, 4, 5):
-            place(k)
-        turn_back(1)
-        finish(1)
-        page[3] = held([P, WINDOW], F32, "page3")
-        nc.vector.tensor_tensor(out=page[3][:].indirect(idx2[:]), in0=weighed_last[:], in1=e_last[:], op=MULT)
-        turn_back(2)
-        finish(2)
+        weighed_last = held([P, S], F32, "weighed_last", freed)
+        nc.gpsimd.tensor_tensor(out=weighed_last[:], in0=last[:, 0, :], in1=wgo_sb[:], op=MULT)
+        page[3] = held([P, WINDOW], F32, "page", "w1_raw3")
+        nc.vector.tensor_tensor(out=page[3][:].indirect(idx2[:]), in0=weighed_last[:], in1=last[:, 1, :], op=MULT)
+        for c in range(3):
+            finish(c)
+        store_early_planes()
         finish_last()
-        for u in range(4):
-            nc.sync.dma_start(
-                out=out_2[0][:, 256 * u : 256 * (u + 1)].bitcast(I32), in_=y_s[32 * u : 32 * u + 16, :].bitcast(I32)
-            )

@@ -21,7 +21,7 @@ ACT = mybir.ActivationFunctionType
 P = 128
 HALF = 512
 WINDOW = 1376
-GPSIMD_COLUMNS = 384
+GPSIMD_COLUMNS = 512
 
 
 def tile_list_herbarium_expert_votes_kernel(
@@ -32,9 +32,12 @@ def tile_list_herbarium_expert_votes_kernel(
     with ExitStack() as ctx:
         keep = ctx.enter_context(tc.tile_pool(name="keep", bufs=1))
         ring = ctx.enter_context(tc.tile_pool(name="ring", bufs=2))
+        chain = ctx.enter_context(tc.tile_pool(name="chain", bufs=1))
         psum = ctx.enter_context(tc.psum_pool(name="psum", bufs=1))
 
         def held(shape, dtype, name, tag=None):
+            if isinstance(tag, int):
+                return chain.tile(shape, dtype, name=name, tag=name, align_bytes=64, offset=1024 * tag)
             return keep.tile(shape, dtype, name=name, tag=tag or name, align_bytes=64)
 
         def bank(number, shape):
@@ -55,7 +58,7 @@ def tile_list_herbarium_expert_votes_kernel(
         w5_w = held([P, 2, 2 * N], U8, "w5_w")
         w5_s = held([P, 2, N], U8, "w5_s")
         w1_raw = [held([P, 4, 256], F32, "w1_raw%d" % i) for i in range(4)]
-        late_raw = [held([P, 4, N], F32, "late_raw%d" % s) for s in range(3)]
+        late_raw = [held([P, 4, N], F32, "late_raw%d" % s, (14, None, 22)[s]) for s in range(3)]
         wgo_sb = held([P, S], F32, "wgo_sb")
         x0_sb = [held([P, S], F32, "x0_sb%d" % c) for c in range(4)]
         amp_sb = held([P, 4, 4], F32, "amp_sb")
@@ -138,8 +141,8 @@ def tile_list_herbarium_expert_votes_kernel(
         def quantise_w1(g):
             w1_q[g], w1_s[g] = quantise(w1_bf[g][:], "w1_%d" % g)
 
-        def quantise_h(g, b):
-            h_q[g, b], h_s[g, b] = quantise(h_bf[g, b][:].rearrange("p n t -> p (n t)"), "h_%d%d" % (g, b))
+        def quantise_h(g, b, tag=None):
+            h_q[g, b], h_s[g, b] = quantise(h_bf[g, b][:].rearrange("p n t -> p (n t)"), "h_%d%d" % (g, b), tag)
 
         def quantise_late(s, tag=None):
             late_q[s], late_s[s] = quantise(late_bf[s][:], "late_%d" % s, tag)
@@ -158,10 +161,14 @@ def tile_list_herbarium_expert_votes_kernel(
                     in_=late_raw[s][:, :, lo:hi].rearrange("p j (a i) -> p a j i", i=4),
                 )
 
-        def features(g, b, tag, b_tag):
-            h_bf[g, b] = held([P, HALF, 4], BF16, "h_bf", tag)
-            b_both = held([P, 2, 2, 256, 2], F32, "b_sb", b_tag)
-            for half in range(2):
+        b_held = {}
+
+        def features(g, b, tag, b_tag, halves=(0, 1), last_bank=None):
+            if 0 in halves:
+                h_bf[g, b] = held([P, HALF, 4], BF16, "h_bf%d%d" % (g, b), tag)
+                b_held[g, b] = held([P, 2, 2, 256, 2], F32, "b_sb", b_tag)
+            b_both = b_held[g, b]
+            for half in halves:
                 step = 4 * b + 2 * g + half
                 cols = slice(256 * half, 256 * (half + 1))
                 b_sb = b_both[:, half]
@@ -177,7 +184,7 @@ def tile_list_herbarium_expert_votes_kernel(
                     nc.scalar.copy(out=b_sb[:, pair], in_=b_ps[:].rearrange("p e n -> p n e"))
                 for jb in range(2):
                     cols = slice(256 * half + P * jb, 256 * half + P * (jb + 1))
-                    a_ps = bank((2 * step + jb) % 3, [P, 4, P])
+                    a_ps = bank(last_bank if last_bank and jb == 1 else (2 * step + jb) % 3, [P, 4, P])
                     for t in range(4):
                         nc.tensor.matmul_mx(
                             out=a_ps[:, t, :],
@@ -223,7 +230,7 @@ def tile_list_herbarium_expert_votes_kernel(
             return e_ps
 
         def weigh(k, tag):
-            votes[k] = held([P, HALF], F32, "votes", tag)[:]
+            votes[k] = held([P, HALF], F32, "votes%d" % k, tag)[:]
             nc.gpsimd.tensor_tensor(out=votes[k], in0=d_neg[k], in1=wgo_sb[:, HALF * (k % 2) : HALF * (k % 2 + 1)], op=MULT)
 
         def place(k):
@@ -290,12 +297,13 @@ def tile_list_herbarium_expert_votes_kernel(
         def finish_last():
             c = 3
             halves = [slice(HALF * hh, HALF * (hh + 1)) for hh in range(2)]
-            z = held([P, S], F32, "z_last", "y_bf")
+            z = held([P, S], F32, "z_last", "late_raw1")
             y = held([P, S], F32, "y_last")
             y_last_bf = held([P, S], BF16, "y_last_bf")
             y_q = held([P, 256], U32, "y_q_last")
             for cols in halves:
                 nc.vector.tensor_tensor(out=z[:, cols], in0=page[c][:, cols], in1=x0_sb[c][:, cols], op=ADD)
+            store_early_planes()
             y_ps = [bank(number, [P, 4, P]) for number in turn_banks[(c + 1) % 2]]
             sig = [held([P, 4, P], F32, "sig", "sig3%d" % hh)[:] for hh in range(2)]
             turn(c, turn_banks[c % 2], lambda hh, t: y_ps[hh][:, t, :], sig)
@@ -333,38 +341,39 @@ def tile_list_herbarium_expert_votes_kernel(
             in_=w2_raw_s[:].rearrange("p (g m t) -> p g t m", g=2, t=4),
         )
         gather_words(1, "w2_raw_s")
-        w1_bf[0] = held([P, 4 * HALF], BF16, "w1_bf")
+        w1_bf[0] = held([P, 4 * HALF], BF16, "w1_bf0", 0)
         round_w1(0, 0, 64, False)
         round_w1(0, 64, 96, False)
         round_w1(0, 96, 128, True)
         quantise_w1(0)
-        w1_bf[1] = held([P, 4 * HALF], BF16, "w1_bf")
+        w1_bf[1] = held([P, 4 * HALF], BF16, "w1_bf1", 2)
         round_w1(1, 0, 64, True)
         round_w1(1, 64, 128, True)
 
-        features(0, 0, "rounded_a", "w1_raw1")
+        features(0, 0, 6, "w1_raw1")
         quantise_w1(1)
-        quantise_h(0, 0)
-        round_late(0, "rounded_a", GPSIMD_COLUMNS)
-        features(1, 0, "rounded_b", "b_sb0")
-        round_late(1, None, 0)
+        quantise_h(0, 0, "w1_raw3")
+        round_late(0, 4, GPSIMD_COLUMNS)
+        features(1, 0, 10, "b_sb0")
         quantise_late(0)
-        quantise_h(1, 0)
-        round_late(2, "rounded_b", GPSIMD_COLUMNS)
-        features(0, 1, "rounded_c", "w1_raw1")
-        quantise_late(1, "w1_raw1")
-        quantise_h(0, 1)
+        quantise_h(1, 0, 14)
+        features(0, 1, 16, "w1_raw1")
+        round_late(1, None, 0)
+        round_late(2, 7, GPSIMD_COLUMNS)
+        quantise_late(1, 22)
         quantise_late(2)
+        quantise_h(0, 1, 24)
 
         last = held([P, 2, S], F32, "last", "tab_w")
         for k in range(8):
             d_neg[k] = held([P, HALF], F32, "d%d" % k)[:] if k < 6 else last[:, 0, HALF * (k - 6) : HALF * (k - 5)]
         for k in range(1, 8):
             e_sb[k] = held([P, HALF], F32, "e%d" % k)[:] if k < 6 else last[:, 1, HALF * (k - 6) : HALF * (k - 5)]
+        features(1, 1, 26, "late_raw1", (0,))
         first_sum(0, 6)
         e_first = second_sum(0, 7)
-        weigh(0, "rounded_b")
-        features(1, 1, "rounded_a", "b_sb0")
+        weigh(0, None)
+        features(1, 1, 26, "late_raw1", (1,), 6)
         nc.vector.tensor_tensor(out=votes[0], in0=e_first[:], in1=votes[0], op=MULT)
         quantise_h(1, 1)
         place(0)
@@ -374,7 +383,7 @@ def tile_list_herbarium_expert_votes_kernel(
         for i, k in enumerate(order):
             first_sum(k, sum_banks[2 * i % 4])
             nc.scalar.copy(out=e_sb[k], in_=second_sum(k, sum_banks[(2 * i + 1) % 4])[:])
-        freed = "rounded_a"
+        freed = 26
         for k in order[:5]:
             weigh(k, freed)
             nc.gpsimd.tensor_tensor(out=votes[k], in0=e_sb[k], in1=votes[k], op=MULT)
@@ -386,5 +395,4 @@ def tile_list_herbarium_expert_votes_kernel(
         nc.vector.tensor_tensor(out=page[3][:].indirect(idx2[:]), in0=weighed_last[:], in1=last[:, 1, :], op=MULT)
         for c in range(3):
             finish(c)
-        store_early_planes()
         finish_last()

@@ -21,7 +21,6 @@ ACT = mybir.ActivationFunctionType
 P = 128
 HALF = 512
 WINDOW = 1376
-GPSIMD_COLUMNS = 512
 
 
 def tile_list_herbarium_expert_votes_kernel(
@@ -37,7 +36,7 @@ def tile_list_herbarium_expert_votes_kernel(
 
         def held(shape, dtype, name, tag=None):
             if isinstance(tag, int):
-                return chain.tile(shape, dtype, name=name, tag=name, align_bytes=64, offset=1024 * tag)
+                return chain.tile(shape, dtype, name=name, tag=name, align_bytes=64, offset=512 * tag)
             return keep.tile(shape, dtype, name=name, tag=tag or name, align_bytes=64)
 
         def bank(number, shape):
@@ -57,8 +56,11 @@ def tile_list_herbarium_expert_votes_kernel(
         w4_s = held([P, N], U8, "w4_s")
         w5_w = held([P, 2, 2 * N], U8, "w5_w")
         w5_s = held([P, 2, N], U8, "w5_s")
-        w1_raw = [held([P, 4, 256], F32, "w1_raw%d" % i) for i in range(4)]
-        late_raw = [held([P, 4, N], F32, "late_raw%d" % s, (14, None, 22)[s]) for s in range(3)]
+        w1_raw = [held([P, 4, 256], F32, "w1_raw%d" % i, 104 if i == 1 else None) for i in range(4)]
+        first_pair = held([P, 2, 4, 256], F32, "first_pair", 32)
+        first_raw = [first_pair[:, 0], first_pair[:, 1], held([P, 4, 256], F32, "first_raw2", 52)[:]]
+        rest_pair = held([P, 2, 4, 256], F32, "rest_pair")
+        rest_raw = [rest_pair[:, 0], rest_pair[:, 1], held([P, 4, 256], F32, "rest_raw2", 88)[:]]
         wgo_sb = held([P, S], F32, "wgo_sb")
         x0_sb = [held([P, S], F32, "x0_sb%d" % c) for c in range(4)]
         amp_sb = held([P, 4, 4], F32, "amp_sb")
@@ -90,15 +92,17 @@ def tile_list_herbarium_expert_votes_kernel(
         load_scale_rows(w2_raw_s, w2_scales[0], range(4))
         for i in range(1, 4):
             load_w1(i)
-        nc.sync.dma_start(out=late_raw[0][:], in_=late_rows[0])
+        nc.sync.dma_start(out=first_raw[0], in_=late_rows[0][:, :, 0:256])
         load_scale_rows(w4_s, w4_scales[0], (0, 1))
-        nc.sync.dma_start(out=late_raw[1][:], in_=late_rows[1])
+        nc.sync.dma_start(out=first_raw[1], in_=late_rows[1][:, :, 0:256])
         load_scale_rows(w4_s, w4_scales[0], (2, 3))
-        nc.sync.dma_start(out=late_raw[2][:], in_=late_rows[2])
+        nc.sync.dma_start(out=first_raw[2], in_=late_rows[2][:, :, 0:256])
         load_scale_rows(w5_s, w5_scale_rows, (0, 1))
         nc.sync.dma_start(out=w4_w[:].bitcast(I32), in_=w4_words[0].rearrange("p n t -> p (n t)").bitcast(I32))
         nc.sync.dma_start(out=w5_w[:].bitcast(I32), in_=w5_words.rearrange("a p b -> p a b").bitcast(I32))
         load_scale_rows(w5_s, w5_scale_rows, (2, 3))
+        for s in range(3):
+            nc.sync.dma_start(out=rest_raw[s], in_=late_rows[s][:, :, 256:N])
         nc.sync.dma_start(out=wgo_sb[:], in_=wgo)
         nc.sync.dma_start(out=idx2[:], in_=offs2)
         for c in range(4):
@@ -114,7 +118,7 @@ def tile_list_herbarium_expert_votes_kernel(
         w2_s = held([P, H], U8, "w2_s")
         w1_bf, w1_q, w1_s = {}, {}, {}
         h_bf, h_q, h_s = {}, {}, {}
-        late_bf, late_q, late_s = {}, {}, {}
+        late_q, late_s = {}, [held([P, 768], U8, "late_s%d" % part) for part in range(2)]
 
         def gather_words(b, tag):
             v_w[b] = held([P, HALF], U32, "v_w%d" % b, tag)
@@ -136,7 +140,7 @@ def tile_list_herbarium_expert_votes_kernel(
             codes = held([P, HALF], U32, name + "_q", tag)
             scales = held([P, HALF], U8, name + "_s")
             nc.vector.quantize_mx(out=codes[:].bitcast(FP8), scales=scales[:], in_=rounded)
-            return codes, scales
+            return codes[:], scales[:]
 
         def quantise_w1(g):
             w1_q[g], w1_s[g] = quantise(w1_bf[g][:], "w1_%d" % g)
@@ -144,36 +148,30 @@ def tile_list_herbarium_expert_votes_kernel(
         def quantise_h(g, b, tag=None):
             h_q[g, b], h_s[g, b] = quantise(h_bf[g, b][:].rearrange("p n t -> p (n t)"), "h_%d%d" % (g, b), tag)
 
-        def quantise_late(s, tag=None):
-            late_q[s], late_s[s] = quantise(late_bf[s][:], "late_%d" % s, tag)
-
-        def round_late(s, tag, gpsimd_columns):
-            late_bf[s] = held([P, 4 * N], BF16, "late_bf%d" % s, tag)
-            if gpsimd_columns:
-                round_on_gpsimd(
-                    late_bf[s][:, 0 : 4 * gpsimd_columns].rearrange("p (n j) -> p n j", j=4),
-                    late_raw[s][:, :, 0:gpsimd_columns].rearrange("p j n -> p n j"),
-                )
-            for lo in range(gpsimd_columns, N, 256):
-                hi = min(lo + 256, N)
+        def round_late(rounded, raw, on_gpsimd):
+            if on_gpsimd:
+                round_on_gpsimd(rounded.rearrange("p (n j) -> p n j", j=4), raw.rearrange("p j n -> p n j"))
+            else:
                 nc.scalar.copy(
-                    out=late_bf[s][:, 4 * lo : 4 * hi].rearrange("p (a i j) -> p a j i", i=4, j=4),
-                    in_=late_raw[s][:, :, lo:hi].rearrange("p j (a i) -> p a j i", i=4),
+                    out=rounded.rearrange("p (a i j) -> p a j i", i=4, j=4), in_=raw.rearrange("p j (a i) -> p a j i", i=4)
                 )
 
-        b_held = {}
+        def quantise_late(part, lo, hi, rounded):
+            nc.vector.quantize_mx(out=late_q[part][:, lo:hi].bitcast(FP8), scales=late_s[part][:, lo:hi], in_=rounded)
 
-        def features(g, b, tag, b_tag, halves=(0, 1), last_bank=None):
-            if 0 in halves:
-                h_bf[g, b] = held([P, HALF, 4], BF16, "h_bf%d%d" % (g, b), tag)
-                b_held[g, b] = held([P, 2, 2, 256, 2], F32, "b_sb", b_tag)
-            b_both = b_held[g, b]
+        def late_weight(s, c):
+            cols = slice(256 * s + P * (c % 2), 256 * s + P * (c % 2 + 1))
+            return late_q[c // 2][:, cols].bitcast(FP8), late_s[c // 2][:, cols]
+
+        b_sb = {}
+
+        def fp4_products(g, b, tags, halves=(0, 1)):
             for half in halves:
+                b_sb[g, b, half] = held([P, 2, 256, 2], F32, "b_sb%d%d%d" % (g, b, half), tags[half])
                 step = 4 * b + 2 * g + half
                 cols = slice(256 * half, 256 * (half + 1))
-                b_sb = b_both[:, half]
                 for pair in range(2):
-                    b_ps = bank(3 + (2 * step + pair) % 3, [P, 2, 256])
+                    b_ps = bank((3, 4, 5, 3, 4, 6, 7, 5, 3, 4, 6, 7, 5, 3, 6, 4)[2 * step + pair], [P, 2, 256])
                     for e in range(2):
                         lo = HALF * g + P * (2 * pair + e)
                         nc.tensor.matmul_mx(
@@ -181,21 +179,26 @@ def tile_list_herbarium_expert_votes_kernel(
                             lhsT=w2_w[:, 2 * lo : 2 * (lo + P)].bitcast(FP4), lhsT_scale=w2_s[:, lo : lo + P],
                             rhs=v_w[b][:, cols].bitcast(FP8), rhs_scale=v_s[b][:, cols], start=True, stop=True,
                         )
-                    nc.scalar.copy(out=b_sb[:, pair], in_=b_ps[:].rearrange("p e n -> p n e"))
-                for jb in range(2):
-                    cols = slice(256 * half + P * jb, 256 * half + P * (jb + 1))
-                    a_ps = bank(last_bank if last_bank and jb == 1 else (2 * step + jb) % 3, [P, 4, P])
-                    for t in range(4):
-                        nc.tensor.matmul_mx(
-                            out=a_ps[:, t, :],
-                            lhsT=w1_q[g][:, P * t : P * (t + 1)].bitcast(FP8), lhsT_scale=w1_s[g][:, P * t : P * (t + 1)],
-                            rhs=v_w[b][:, cols].bitcast(FP8), rhs_scale=v_s[b][:, cols], start=True, stop=True,
-                        )
-                    nc.vector.tensor_tensor(
-                        out=h_bf[g, b][:, cols, :].rearrange("p n (q e) -> p n q e", q=2),
-                        in0=a_ps[:].rearrange("p (q e) n -> p n q e", q=2),
-                        in1=b_sb[:, :, P * jb : P * (jb + 1), :].rearrange("p q n e -> p n q e"), op=MULT,
+                    nc.scalar.copy(out=b_sb[g, b, half][:, pair], in_=b_ps[:].rearrange("p e n -> p n e"))
+
+        def features(g, b, tag, pieces=range(4), last_bank=None):
+            if 0 in pieces:
+                h_bf[g, b] = held([P, HALF, 4], BF16, "h_bf%d%d" % (g, b), tag)
+            for piece in pieces:
+                half, jb = divmod(piece, 2)
+                cols = slice(P * piece, P * (piece + 1))
+                a_ps = bank(last_bank or {0: 6, 1: 7}.get(8 * b + 4 * g + piece, (8 * b + 4 * g + piece) % 3), [P, 4, P])
+                for t in range(4):
+                    nc.tensor.matmul_mx(
+                        out=a_ps[:, t, :],
+                        lhsT=w1_q[g][:, P * t : P * (t + 1)].bitcast(FP8), lhsT_scale=w1_s[g][:, P * t : P * (t + 1)],
+                        rhs=v_w[b][:, cols].bitcast(FP8), rhs_scale=v_s[b][:, cols], start=True, stop=True,
                     )
+                nc.vector.tensor_tensor(
+                    out=h_bf[g, b][:, cols, :].rearrange("p n (q e) -> p n q e", q=2),
+                    in0=a_ps[:].rearrange("p (q e) n -> p n q e", q=2),
+                    in1=b_sb[g, b, half][:, :, P * jb : P * (jb + 1), :].rearrange("p q n e -> p n q e"), op=MULT,
+                )
 
         d_neg, e_sb, votes, page = {}, {}, {}, {}
 
@@ -209,8 +212,8 @@ def tile_list_herbarium_expert_votes_kernel(
             )
             for g in range(2):
                 nc.tensor.matmul_mx(
-                    out=d_ps[:], lhsT=late_q[g][:, rows].bitcast(FP8), lhsT_scale=late_s[g][:, rows],
-                    rhs=h_q[g, b][:].bitcast(FP8), rhs_scale=h_s[g, b][:], start=False, stop=(g == 1),
+                    out=d_ps[:], lhsT=late_weight(g, c)[0], lhsT_scale=late_weight(g, c)[1],
+                    rhs=h_q[g, b].bitcast(FP8), rhs_scale=h_s[g, b], start=False, stop=(g == 1),
                 )
             nc.scalar.activation(out=d_neg[k], in_=d_ps[:], func=ACT.Copy, scale=-1.0)
 
@@ -219,13 +222,13 @@ def tile_list_herbarium_expert_votes_kernel(
             rows = slice(P * c, P * (c + 1))
             e_ps = bank(number, [P, HALF])
             nc.tensor.matmul_mx(
-                out=e_ps[:], lhsT=late_q[2][:, rows].bitcast(FP8), lhsT_scale=late_s[2][:, rows],
+                out=e_ps[:], lhsT=late_weight(2, c)[0], lhsT_scale=late_weight(2, c)[1],
                 rhs=v_w[b][:].bitcast(FP8), rhs_scale=v_s[b], start=True, stop=False,
             )
             for g in range(2):
                 nc.tensor.matmul_mx(
                     out=e_ps[:], lhsT=w5_w[:, g, 2 * P * c : 2 * P * (c + 1)].bitcast(FP4), lhsT_scale=w5_s[:, g, rows],
-                    rhs=h_q[g, b][:].bitcast(FP8), rhs_scale=h_s[g, b][:], start=False, stop=(g == 1),
+                    rhs=h_q[g, b].bitcast(FP8), rhs_scale=h_s[g, b], start=False, stop=(g == 1),
                 )
             return e_ps
 
@@ -236,7 +239,7 @@ def tile_list_herbarium_expert_votes_kernel(
         def place(k):
             c, b = divmod(k, 2)
             if b == 0:
-                page[c] = held([P, WINDOW], F32, "page", ("w1_raw0", "page1", "w1_raw2")[c])
+                page[c] = held([P, WINDOW], F32, "page%d" % c, (78, "w1_raw0", "w1_raw2")[c])
             nc.vector.tensor_copy(out=page[c][:].indirect(idx2[:, 32 * b : 32 * (b + 1)]), in_=votes[k])
 
         def turn(c, z_banks, y_spot, sig):
@@ -261,7 +264,7 @@ def tile_list_herbarium_expert_votes_kernel(
 
         y_bf = held([P, 3, S], BF16, "y_bf")
         y_s = held([P, 256], U8, "y_s")
-        turn_banks = ((4, 5), (0, 1))
+        turn_banks = ((7, 5), (0, 1))
 
         def finish(c):
             y_ps = [bank(number, [P, HALF]) for number in turn_banks[(c + 1) % 2]]
@@ -297,7 +300,7 @@ def tile_list_herbarium_expert_votes_kernel(
         def finish_last():
             c = 3
             halves = [slice(HALF * hh, HALF * (hh + 1)) for hh in range(2)]
-            z = held([P, S], F32, "z_last", "late_raw1")
+            z = held([P, S], F32, "z_last")
             y = held([P, S], F32, "y_last")
             y_last_bf = held([P, S], BF16, "y_last_bf")
             y_q = held([P, 256], U32, "y_q_last")
@@ -346,48 +349,62 @@ def tile_list_herbarium_expert_votes_kernel(
         round_w1(0, 64, 96, False)
         round_w1(0, 96, 128, True)
         quantise_w1(0)
-        w1_bf[1] = held([P, 4 * HALF], BF16, "w1_bf1", 2)
+        w1_bf[1] = held([P, 4 * HALF], BF16, "w1_bf1", 4)
         round_w1(1, 0, 64, True)
         round_w1(1, 64, 128, True)
 
-        features(0, 0, 6, "w1_raw1")
+        for half in range(2):
+            fp4_products(0, 0, (100, 108), (half,))
+            features(0, 0, 12, (2 * half, 2 * half + 1))
+        fp4_products(1, 0, (None, None))
         quantise_w1(1)
         quantise_h(0, 0, "w1_raw3")
-        round_late(0, 4, GPSIMD_COLUMNS)
-        features(1, 0, 10, "b_sb0")
-        quantise_late(0)
-        quantise_h(1, 0, 14)
-        features(0, 1, 16, "w1_raw1")
-        round_late(1, None, 0)
-        round_late(2, 7, GPSIMD_COLUMNS)
-        quantise_late(1, 22)
-        quantise_late(2)
-        quantise_h(0, 1, 24)
-
-        last = held([P, 2, S], F32, "last", "tab_w")
-        for k in range(8):
-            d_neg[k] = held([P, HALF], F32, "d%d" % k)[:] if k < 6 else last[:, 0, HALF * (k - 6) : HALF * (k - 5)]
-        for k in range(1, 8):
-            e_sb[k] = held([P, HALF], F32, "e%d" % k)[:] if k < 6 else last[:, 1, HALF * (k - 6) : HALF * (k - 5)]
-        features(1, 1, 26, "late_raw1", (0,))
-        first_sum(0, 6)
-        e_first = second_sum(0, 7)
-        weigh(0, None)
-        features(1, 1, 26, "late_raw1", (1,), 6)
+        first_w3 = held([P, 2048], BF16, "first_w3", 11)
+        round_late(first_w3[:, 0:1024], first_raw[0], True)
+        round_late(first_w3[:, 1024:2048], first_raw[1], False)
+        features(1, 0, 20)
+        fp4_products(0, 1, (100, 44))
+        late_q[0] = held([P, 768], U32, "late_q0")
+        quantise_late(0, 0, 512, first_w3[:])
+        quantise_h(1, 0, 32)
+        first_w6 = held([P, 1024], BF16, "first_w6", 18)
+        round_late(first_w6[:], first_raw[2], True)
+        features(0, 1, 36)
+        d_neg[0] = held([P, HALF], F32, "d0")[:]
+        first_sum(0, 7)
+        fp4_products(1, 1, ("b_sb100", "b_sb101"))
+        quantise_late(0, 512, 768, first_w6[:])
+        quantise_h(0, 1, 52)
+        weigh(0, 36)
+        features(1, 1, 56, range(3))
+        features(1, 1, 56, (3,), 5)
+        e_first = second_sum(0, 6)
+        rest_bf = held([P, 3072], BF16, "rest_bf", 64)
+        for s in range(3):
+            round_late(rest_bf[:, 1024 * s : 1024 * (s + 1)], rest_raw[s], False)
         nc.vector.tensor_tensor(out=votes[0], in0=e_first[:], in1=votes[0], op=MULT)
         quantise_h(1, 1)
+        late_q[1] = held([P, 768], U32, "late_q1", "d0")
+        quantise_late(1, 0, 512, rest_bf[:, 0:2048])
+        quantise_late(1, 512, 768, rest_bf[:, 2048:3072])
         place(0)
 
+        last = held([P, 2, S], F32, "last", "tab_w")
         order = (2, 1, 4, 3, 5, 6, 7)
-        sum_banks = (4, 5, 3, 6)
         for i, k in enumerate(order):
-            first_sum(k, sum_banks[2 * i % 4])
-            nc.scalar.copy(out=e_sb[k], in_=second_sum(k, sum_banks[(2 * i + 1) % 4])[:])
-        freed = 26
+            if k < 6:
+                d_neg[k] = held([P, HALF], F32, "d%d" % k, {2: 89}.get(k))[:]
+                e_sb[k] = held([P, HALF], F32, "e%d" % k, {2: 93}.get(k))[:]
+            else:
+                d_neg[k], e_sb[k] = (last[:, i, HALF * (k - 6) : HALF * (k - 5)] for i in range(2))
+            d_bank, e_bank = ((4, 3), (7, 5))[max(i - 1, 0) % 2]
+            first_sum(k, d_bank)
+            nc.scalar.copy(out=e_sb[k], in_=second_sum(k, e_bank)[:])
+        freed = 62
         for k in order[:5]:
             weigh(k, freed)
             nc.gpsimd.tensor_tensor(out=votes[k], in0=e_sb[k], in1=votes[k], op=MULT)
-            freed = "e%d" % k
+            freed = {2: 93}.get(k, "e%d" % k)
             place(k)
         weighed_last = held([P, S], F32, "weighed_last", freed)
         nc.gpsimd.tensor_tensor(out=weighed_last[:], in0=last[:, 0, :], in1=wgo_sb[:], op=MULT)

@@ -56,7 +56,7 @@ def tile_list_herbarium_expert_votes_kernel(
         w4_s = held([P, N], U8, "w4_s")
         w5_w = held([P, 2, 2 * N], U8, "w5_w")
         w5_s = held([P, 2, N], U8, "w5_s")
-        w1_raw = [held([P, 4, 256], F32, "w1_raw%d" % i, 104 if i == 1 else None) for i in range(4)]
+        w1_raw = [held([P, 4, 256], F32, "w1_raw%d" % i, {1: 104, 3: 120}.get(i)) for i in range(4)]
         first_pair = held([P, 2, 4, 256], F32, "first_pair", 32)
         first_raw = [first_pair[:, 0], first_pair[:, 1], held([P, 4, 256], F32, "first_raw2", 52)[:]]
         rest_pair = held([P, 2, 4, 256], F32, "rest_pair")
@@ -304,9 +304,9 @@ def tile_list_herbarium_expert_votes_kernel(
             y = held([P, S], F32, "y_last")
             y_last_bf = held([P, S], BF16, "y_last_bf")
             y_q = held([P, 256], U32, "y_q_last")
+            store_early_planes()
             for cols in halves:
                 nc.vector.tensor_tensor(out=z[:, cols], in0=page[c][:, cols], in1=x0_sb[c][:, cols], op=ADD)
-            store_early_planes()
             y_ps = [bank(number, [P, 4, P]) for number in turn_banks[(c + 1) % 2]]
             sig = [held([P, 4, P], F32, "sig", "sig3%d" % hh)[:] for hh in range(2)]
             turn(c, turn_banks[c % 2], lambda hh, t: y_ps[hh][:, t, :], sig)
@@ -346,19 +346,20 @@ def tile_list_herbarium_expert_votes_kernel(
         gather_words(1, "w2_raw_s")
         w1_bf[0] = held([P, 4 * HALF], BF16, "w1_bf0", 0)
         round_w1(0, 0, 64, False)
-        round_w1(0, 64, 96, False)
-        round_w1(0, 96, 128, True)
+        round_w1(0, 64, 104, False)
+        round_w1(0, 104, 128, True)
         quantise_w1(0)
         w1_bf[1] = held([P, 4 * HALF], BF16, "w1_bf1", 4)
         round_w1(1, 0, 64, True)
-        round_w1(1, 64, 128, True)
+        round_w1(1, 64, 96, True)
+        round_w1(1, 96, 128, False)
 
         for half in range(2):
             fp4_products(0, 0, (100, 108), (half,))
             features(0, 0, 12, (2 * half, 2 * half + 1))
-        fp4_products(1, 0, (None, None))
+        fp4_products(1, 0, (124, None))
         quantise_w1(1)
-        quantise_h(0, 0, "w1_raw3")
+        quantise_h(0, 0, 120)
         first_w3 = held([P, 2048], BF16, "first_w3", 11)
         round_late(first_w3[:, 0:1024], first_raw[0], True)
         round_late(first_w3[:, 1024:2048], first_raw[1], False)
@@ -372,7 +373,7 @@ def tile_list_herbarium_expert_votes_kernel(
         features(0, 1, 36)
         d_neg[0] = held([P, HALF], F32, "d0")[:]
         first_sum(0, 7)
-        fp4_products(1, 1, ("b_sb100", "b_sb101"))
+        fp4_products(1, 1, (124, "b_sb101"))
         quantise_late(0, 512, 768, first_w6[:])
         quantise_h(0, 1, 52)
         weigh(0, 36)
@@ -408,7 +409,7 @@ def tile_list_herbarium_expert_votes_kernel(
             place(k)
         weighed_last = held([P, S], F32, "weighed_last", freed)
         nc.gpsimd.tensor_tensor(out=weighed_last[:], in0=last[:, 0, :], in1=wgo_sb[:], op=MULT)
-        page[3] = held([P, WINDOW], F32, "page", "w1_raw3")
+        page[3] = held([P, WINDOW], F32, "page3")
         nc.vector.tensor_tensor(out=page[3][:].indirect(idx2[:]), in0=weighed_last[:], in1=last[:, 1, :], op=MULT)
         for c in range(3):
             finish(c)

@@ -30,7 +30,6 @@ def tile_list_herbarium_expert_votes_kernel(
     nc = tc.nc
     with ExitStack() as ctx:
         keep = ctx.enter_context(tc.tile_pool(name="keep", bufs=1))
-        ring = ctx.enter_context(tc.tile_pool(name="ring", bufs=2))
         chain = ctx.enter_context(tc.tile_pool(name="chain", bufs=1))
         psum = ctx.enter_context(tc.psum_pool(name="psum", bufs=1))
 
@@ -262,33 +261,31 @@ def tile_list_herbarium_expert_votes_kernel(
                 for t in range(4):
                     nc.tensor.transpose(y_spot(hh, t), sig[hh][:, t, :], ident[:])
 
-        y_bf = held([P, 3, S], BF16, "y_bf")
         y_s = held([P, 256], U8, "y_s")
-        turn_banks = ((7, 5), (0, 1))
+        z_banks = ((4, 3), (7, 5))
+        y_banks = ((0, 1), (2, 6))
 
         def finish(c):
-            y_ps = [bank(number, [P, HALF]) for number in turn_banks[(c + 1) % 2]]
+            y_ps = [bank(number, [P, HALF]) for number in y_banks[c % 2]]
             both = held([P, 2, 4, P], F32, "sig", "sig%d" % (c % 2))
             turn(
-                c, turn_banks[c % 2],
+                c, z_banks[c % 2],
                 lambda hh, t: y_ps[t // 2][:, 256 * (t % 2) + P * hh : 256 * (t % 2) + P * (hh + 1)],
                 [both[:, hh] for hh in range(2)],
             )
-            y = ring.tile([P, 4, 256], F32, tag="y")
+            y = held([P, 4, 256], F32, "y%d" % c)
             for t in range(4):
                 nc.scalar.activation(
                     out=y[:, t, :], in_=y_ps[t // 2][:, 256 * (t % 2) : 256 * (t % 2 + 1)], func=ACT.Copy,
                     scale=amp_sb[:, c, t : t + 1],
                 )
-            nc.scalar.copy(
-                out=y_bf[:, c, :].rearrange("p (a i t) -> p a t i", i=4, t=4), in_=y[:].rearrange("p t (a i) -> p a t i", i=4)
-            )
+            round_on_gpsimd(y_bf[:, c, :].rearrange("p (m t) -> p m t", t=4), y[:].rearrange("p t m -> p m t"))
             rows = out_0[P * c : P * (c + 1), :].rearrange("(a t) m -> a t m", t=4)
             for u in range(4):
                 nc.sync.dma_start(out=rows[:, :, 256 * u : 256 * (u + 1)], in_=y[32 * u : 32 * (u + 1)])
 
         def store_early_planes():
-            y_q = held([P, 3, 256], U32, "y_q_early", "tab_w")
+            y_q = held([P, 3, 256], U32, "y_q_early", "e5")
             for c in range(3):
                 nc.vector.quantize_mx(out=y_q[:, c, :].bitcast(FP8), scales=y_s[4 * c : P, :], in_=y_bf[:, c, :])
             words = out_1[0].rearrange("(c a) m t -> a c (m t)", c=4).bitcast(I32)
@@ -307,9 +304,9 @@ def tile_list_herbarium_expert_votes_kernel(
             store_early_planes()
             for cols in halves:
                 nc.vector.tensor_tensor(out=z[:, cols], in0=page[c][:, cols], in1=x0_sb[c][:, cols], op=ADD)
-            y_ps = [bank(number, [P, 4, P]) for number in turn_banks[(c + 1) % 2]]
+            y_ps = [bank(number, [P, 4, P]) for number in y_banks[c % 2]]
             sig = [held([P, 4, P], F32, "sig", "sig3%d" % hh)[:] for hh in range(2)]
-            turn(c, turn_banks[c % 2], lambda hh, t: y_ps[hh][:, t, :], sig)
+            turn(c, z_banks[c % 2], lambda hh, t: y_ps[hh][:, t, :], sig)
             s_rows = held([P, S], F32, "s_rows", "sig30")
             for cols in halves:
                 nc.scalar.activation(out=s_rows[:, cols], in_=z[:, cols], func=ACT.Sigmoid)
@@ -410,7 +407,9 @@ def tile_list_herbarium_expert_votes_kernel(
         weighed_last = held([P, S], F32, "weighed_last", freed)
         nc.gpsimd.tensor_tensor(out=weighed_last[:], in0=last[:, 0, :], in1=wgo_sb[:], op=MULT)
         page[3] = held([P, WINDOW], F32, "page3")
-        nc.vector.tensor_tensor(out=page[3][:].indirect(idx2[:]), in0=weighed_last[:], in1=last[:, 1, :], op=MULT)
+        nc.gpsimd.tensor_tensor(out=weighed_last[:], in0=last[:, 1, :], in1=weighed_last[:], op=MULT)
+        nc.vector.tensor_copy(out=page[3][:].indirect(idx2[:]), in_=weighed_last[:])
+        y_bf = held([P, 3, S], BF16, "y_bf", "tab_w")
         for c in range(3):
             finish(c)
         finish_last()

@@ -58,7 +58,7 @@ def tile_list_herbarium_expert_votes_kernel(
         w1_raw = [held([P, 4, 256], F32, "w1_raw%d" % i, {1: 104, 3: 120}.get(i)) for i in range(4)]
         first_pair = held([P, 2, 4, 256], F32, "first_pair", 32)
         first_raw = [first_pair[:, 0], first_pair[:, 1], held([P, 4, 256], F32, "first_raw2", 52)[:]]
-        rest_pair = held([P, 2, 4, 256], F32, "rest_pair")
+        rest_pair = held([P, 2, 4, 256], F32, "rest_pair", 136)
         rest_raw = [rest_pair[:, 0], rest_pair[:, 1], held([P, 4, 256], F32, "rest_raw2", 88)[:]]
         wgo_sb = held([P, S], F32, "wgo_sb")
         x0_sb = [held([P, S], F32, "x0_sb%d" % c) for c in range(4)]
@@ -66,6 +66,7 @@ def tile_list_herbarium_expert_votes_kernel(
         amp_last = held([P, 1], F32, "amp_last")
         ident = held([P, P], F32, "ident")
 
+        nc.gpsimd.memset(tab_s[:].bitcast(I32), 0)
         nc.gpsimd.memset(w2_raw_s[:].bitcast(I32), 0)
         nc.gpsimd.memset(w4_s[:].bitcast(I32), 0)
         nc.gpsimd.memset(w5_s[:].rearrange("p a n -> p (a n)").bitcast(I32), 0)
@@ -80,14 +81,10 @@ def tile_list_herbarium_expert_votes_kernel(
             nc.sync.dma_start(out=w1_raw[i][:], in_=w1_rows[:, :, 256 * i : 256 * (i + 1)])
 
         nc.sync.dma_start(out=idx[:], in_=offs)
-        for q in range(4):
-            nc.sync.dma_start(
-                out=tab_s[32 * q : 32 * (q + 1)].bitcast(I32),
-                in_=tab_scales[0][4 * q : 4 * q + 4].bitcast(I32).unsqueeze(0).to_broadcast([8, 4, T // 4]),
-            )
-        nc.sync.dma_start(out=w2_raw[:].bitcast(I32), in_=w2_words[0].bitcast(I32))
-        nc.sync.dma_start(out=tab_w[:].bitcast(I32), in_=tab_words[0].rearrange("p n t -> p (n t)").bitcast(I32))
         load_w1(0)
+        load_scale_rows(tab_s, tab_scales[0], range(4))
+        nc.sync.dma_start(out=tab_w[:].bitcast(I32), in_=tab_words[0].rearrange("p n t -> p (n t)").bitcast(I32))
+        nc.sync.dma_start(out=w2_raw[:].bitcast(I32), in_=w2_words[0].bitcast(I32))
         load_scale_rows(w2_raw_s, w2_scales[0], range(4))
         for i in range(1, 4):
             load_w1(i)
@@ -100,10 +97,10 @@ def tile_list_herbarium_expert_votes_kernel(
         nc.sync.dma_start(out=w4_w[:].bitcast(I32), in_=w4_words[0].rearrange("p n t -> p (n t)").bitcast(I32))
         nc.sync.dma_start(out=w5_w[:].bitcast(I32), in_=w5_words.rearrange("a p b -> p a b").bitcast(I32))
         load_scale_rows(w5_s, w5_scale_rows, (2, 3))
-        for s in range(3):
-            nc.sync.dma_start(out=rest_raw[s], in_=late_rows[s][:, :, 256:N])
         nc.sync.dma_start(out=wgo_sb[:], in_=wgo)
         nc.sync.dma_start(out=idx2[:], in_=offs2)
+        for s in (2, 0, 1):
+            nc.sync.dma_start(out=rest_raw[s], in_=late_rows[s][:, :, 256:N])
         for c in range(4):
             nc.sync.dma_start(out=x0_sb[c][:], in_=x0[P * c : P * (c + 1), :])
         for u in range(4):
@@ -119,9 +116,19 @@ def tile_list_herbarium_expert_votes_kernel(
         h_bf, h_q, h_s = {}, {}, {}
         late_q, late_s = {}, [held([P, 768], U8, "late_s%d" % part) for part in range(2)]
 
-        def gather_words(b, tag):
-            v_w[b] = held([P, HALF], U32, "v_w%d" % b, tag)
-            nc.vector.tensor_copy(out=v_w[b][:], in_=tab_w[:].indirect(idx[:, 32 * b : 32 * (b + 1)]))
+        def gather_words(first, count, tag):
+            words = held([P, 256 * count], U32, "v_w%d" % first, tag)
+            nc.vector.tensor_copy(out=words[:], in_=tab_w[:].indirect(idx[:, 16 * first : 16 * (first + count)]))
+            for i in range(count):
+                v_w[first + i] = words[:, 256 * i : 256 * (i + 1)]
+
+        def table_passes(out, codes, scales, b):
+            for half in range(2):
+                cols = slice(256 * half, 256 * (half + 1))
+                nc.tensor.matmul_mx(
+                    out=out[:, cols], lhsT=codes, lhsT_scale=scales,
+                    rhs=v_w[2 * b + half].bitcast(FP8), rhs_scale=v_s[b][:, cols], start=(half == 0), stop=False,
+                )
 
         def round_on_gpsimd(out, in_):
             nc.gpsimd.tensor_scalar(out=out, in0=in_, scalar1=1.0, scalar2=0.0, op0=MULT, op1=ADD)
@@ -176,9 +183,22 @@ def tile_list_herbarium_expert_votes_kernel(
                         nc.tensor.matmul_mx(
                             out=b_ps[:, e, :],
                             lhsT=w2_w[:, 2 * lo : 2 * (lo + P)].bitcast(FP4), lhsT_scale=w2_s[:, lo : lo + P],
-                            rhs=v_w[b][:, cols].bitcast(FP8), rhs_scale=v_s[b][:, cols], start=True, stop=True,
+                            rhs=v_w[2 * b + half].bitcast(FP8), rhs_scale=v_s[b][:, cols], start=True, stop=True,
                         )
                     nc.scalar.copy(out=b_sb[g, b, half][:, pair], in_=b_ps[:].rearrange("p e n -> p n e"))
+
+        def first_fp4_products():
+            b_sb[0, 0, 0] = held([P, 2, 256, 2], F32, "b_sb000", 97)
+            for jb in range(2):
+                cols = slice(P * jb, P * (jb + 1))
+                b_ps = bank(3 + jb, [P, 4, P])
+                for t in range(4):
+                    nc.tensor.matmul_mx(
+                        out=b_ps[:, t, :],
+                        lhsT=w2_w[:, 2 * P * t : 2 * P * (t + 1)].bitcast(FP4), lhsT_scale=w2_s[:, P * t : P * (t + 1)],
+                        rhs=v_w[0][:, cols].bitcast(FP8), rhs_scale=v_s[0][:, cols], start=True, stop=True,
+                    )
+                nc.scalar.copy(out=b_sb[0, 0, 0][:, :, cols, :], in_=b_ps[:].rearrange("p (q e) n -> p q n e", q=2))
 
         def features(g, b, tag, pieces=range(4), last_bank=None):
             if 0 in pieces:
@@ -191,7 +211,7 @@ def tile_list_herbarium_expert_votes_kernel(
                     nc.tensor.matmul_mx(
                         out=a_ps[:, t, :],
                         lhsT=w1_q[g][:, P * t : P * (t + 1)].bitcast(FP8), lhsT_scale=w1_s[g][:, P * t : P * (t + 1)],
-                        rhs=v_w[b][:, cols].bitcast(FP8), rhs_scale=v_s[b][:, cols], start=True, stop=True,
+                        rhs=v_w[2 * b + half][:, P * jb : P * (jb + 1)].bitcast(FP8), rhs_scale=v_s[b][:, cols], start=True, stop=True,
                     )
                 nc.vector.tensor_tensor(
                     out=h_bf[g, b][:, cols, :].rearrange("p n (q e) -> p n q e", q=2),
@@ -205,10 +225,7 @@ def tile_list_herbarium_expert_votes_kernel(
             c, b = divmod(k, 2)
             rows = slice(P * c, P * (c + 1))
             d_ps = bank(number, [P, HALF])
-            nc.tensor.matmul_mx(
-                out=d_ps[:], lhsT=w4_w[:, rows].bitcast(FP8), lhsT_scale=w4_s[:, rows],
-                rhs=v_w[b][:].bitcast(FP8), rhs_scale=v_s[b], start=True, stop=False,
-            )
+            table_passes(d_ps, w4_w[:, rows].bitcast(FP8), w4_s[:, rows], b)
             for g in range(2):
                 nc.tensor.matmul_mx(
                     out=d_ps[:], lhsT=late_weight(g, c)[0], lhsT_scale=late_weight(g, c)[1],
@@ -220,10 +237,7 @@ def tile_list_herbarium_expert_votes_kernel(
             c, b = divmod(k, 2)
             rows = slice(P * c, P * (c + 1))
             e_ps = bank(number, [P, HALF])
-            nc.tensor.matmul_mx(
-                out=e_ps[:], lhsT=late_weight(2, c)[0], lhsT_scale=late_weight(2, c)[1],
-                rhs=v_w[b][:].bitcast(FP8), rhs_scale=v_s[b], start=True, stop=False,
-            )
+            table_passes(e_ps, *late_weight(2, c), b)
             for g in range(2):
                 nc.tensor.matmul_mx(
                     out=e_ps[:], lhsT=w5_w[:, g, 2 * P * c : 2 * P * (c + 1)].bitcast(FP4), lhsT_scale=w5_s[:, g, rows],
@@ -238,7 +252,7 @@ def tile_list_herbarium_expert_votes_kernel(
         def place(k):
             c, b = divmod(k, 2)
             if b == 0:
-                page[c] = held([P, WINDOW], F32, "page%d" % c, (78, "w1_raw0", "w1_raw2")[c])
+                page[c] = held([P, WINDOW], F32, "page%d" % c, ("w1_raw0", 150, "w1_raw2")[c])
             nc.vector.tensor_copy(out=page[c][:].indirect(idx2[:, 32 * b : 32 * (b + 1)]), in_=votes[k])
 
         def turn(c, z_banks, y_spot, sig):
@@ -262,14 +276,13 @@ def tile_list_herbarium_expert_votes_kernel(
                     nc.tensor.transpose(y_spot(hh, t), sig[hh][:, t, :], ident[:])
 
         y_s = held([P, 256], U8, "y_s")
-        z_banks = ((4, 3), (7, 5))
-        y_banks = ((0, 1), (2, 6))
+        pairs = ((0, 1), (7, 5), (2, 6), (4, 3))
 
         def finish(c):
-            y_ps = [bank(number, [P, HALF]) for number in y_banks[c % 2]]
+            y_ps = [bank(number, [P, HALF]) for number in pairs[c + 1]]
             both = held([P, 2, 4, P], F32, "sig", "sig%d" % (c % 2))
             turn(
-                c, z_banks[c % 2],
+                c, pairs[c],
                 lambda hh, t: y_ps[t // 2][:, 256 * (t % 2) + P * hh : 256 * (t % 2) + P * (hh + 1)],
                 [both[:, hh] for hh in range(2)],
             )
@@ -279,13 +292,13 @@ def tile_list_herbarium_expert_votes_kernel(
                     out=y[:, t, :], in_=y_ps[t // 2][:, 256 * (t % 2) : 256 * (t % 2 + 1)], func=ACT.Copy,
                     scale=amp_sb[:, c, t : t + 1],
                 )
-            round_on_gpsimd(y_bf[:, c, :].rearrange("p (m t) -> p m t", t=4), y[:].rearrange("p t m -> p m t"))
+            round_late(y_bf[:, c, :], y[:], False)
             rows = out_0[P * c : P * (c + 1), :].rearrange("(a t) m -> a t m", t=4)
             for u in range(4):
                 nc.sync.dma_start(out=rows[:, :, 256 * u : 256 * (u + 1)], in_=y[32 * u : 32 * (u + 1)])
 
         def store_early_planes():
-            y_q = held([P, 3, 256], U32, "y_q_early", "e5")
+            y_q = held([P, 3, 256], U32, "y_q_early", "tab_w")
             for c in range(3):
                 nc.vector.quantize_mx(out=y_q[:, c, :].bitcast(FP8), scales=y_s[4 * c : P, :], in_=y_bf[:, c, :])
             words = out_1[0].rearrange("(c a) m t -> a c (m t)", c=4).bitcast(I32)
@@ -304,9 +317,9 @@ def tile_list_herbarium_expert_votes_kernel(
             store_early_planes()
             for cols in halves:
                 nc.vector.tensor_tensor(out=z[:, cols], in0=page[c][:, cols], in1=x0_sb[c][:, cols], op=ADD)
-            y_ps = [bank(number, [P, 4, P]) for number in y_banks[c % 2]]
+            y_ps = [bank(number, [P, 4, P]) for number in pairs[0]]
             sig = [held([P, 4, P], F32, "sig", "sig3%d" % hh)[:] for hh in range(2)]
-            turn(c, z_banks[c % 2], lambda hh, t: y_ps[hh][:, t, :], sig)
+            turn(c, pairs[c], lambda hh, t: y_ps[hh][:, t, :], sig)
             s_rows = held([P, S], F32, "s_rows", "sig30")
             for cols in halves:
                 nc.scalar.activation(out=s_rows[:, cols], in_=z[:, cols], func=ACT.Sigmoid)
@@ -331,29 +344,31 @@ def tile_list_herbarium_expert_votes_kernel(
                 )
 
         nc.vector.tensor_copy(out=v_s_all[:], in_=tab_s[:].indirect(idx[:]))
-        nc.vector.tensor_copy(
+        nc.scalar.copy(
             out=w2_w[:].bitcast(U16).rearrange("p (g t m) -> p g t m", g=2, t=4),
             in_=w2_raw[:].bitcast(U16).rearrange("p (g m t) -> p g t m", g=2, t=4),
         )
-        gather_words(0, None)
+        gather_words(0, 1, None)
         nc.vector.tensor_copy(
             out=w2_s[:].rearrange("p (g t m) -> p g t m", g=2, t=4),
             in_=w2_raw_s[:].rearrange("p (g m t) -> p g t m", g=2, t=4),
         )
-        gather_words(1, "w2_raw_s")
+        gather_words(1, 2, "w2_raw_s")
         w1_bf[0] = held([P, 4 * HALF], BF16, "w1_bf0", 0)
         round_w1(0, 0, 64, False)
         round_w1(0, 64, 104, False)
         round_w1(0, 104, 128, True)
         quantise_w1(0)
+        gather_words(3, 1, 105)
         w1_bf[1] = held([P, 4 * HALF], BF16, "w1_bf1", 4)
         round_w1(1, 0, 64, True)
         round_w1(1, 64, 96, True)
         round_w1(1, 96, 128, False)
 
-        for half in range(2):
-            fp4_products(0, 0, (100, 108), (half,))
-            features(0, 0, 12, (2 * half, 2 * half + 1))
+        first_fp4_products()
+        features(0, 0, 12, (0, 1))
+        fp4_products(0, 0, (None, 111), (1,))
+        features(0, 0, 12, (2, 3))
         fp4_products(1, 0, (124, None))
         quantise_w1(1)
         quantise_h(0, 0, 120)
@@ -361,7 +376,7 @@ def tile_list_herbarium_expert_votes_kernel(
         round_late(first_w3[:, 0:1024], first_raw[0], True)
         round_late(first_w3[:, 1024:2048], first_raw[1], False)
         features(1, 0, 20)
-        fp4_products(0, 1, (100, 44))
+        fp4_products(0, 1, (97, 44))
         late_q[0] = held([P, 768], U32, "late_q0")
         quantise_late(0, 0, 512, first_w3[:])
         quantise_h(1, 0, 32)
@@ -377,39 +392,51 @@ def tile_list_herbarium_expert_votes_kernel(
         features(1, 1, 56, range(3))
         features(1, 1, 56, (3,), 5)
         e_first = second_sum(0, 6)
-        rest_bf = held([P, 3072], BF16, "rest_bf", 64)
-        for s in range(3):
-            round_late(rest_bf[:, 1024 * s : 1024 * (s + 1)], rest_raw[s], False)
         nc.vector.tensor_tensor(out=votes[0], in0=e_first[:], in1=votes[0], op=MULT)
         quantise_h(1, 1)
-        late_q[1] = held([P, 768], U32, "late_q1", "d0")
-        quantise_late(1, 0, 512, rest_bf[:, 0:2048])
-        quantise_late(1, 512, 768, rest_bf[:, 2048:3072])
         place(0)
 
-        last = held([P, 2, S], F32, "last", "tab_w")
-        order = (2, 1, 4, 3, 5, 6, 7)
-        for i, k in enumerate(order):
-            if k < 6:
-                d_neg[k] = held([P, HALF], F32, "d%d" % k, {2: 89}.get(k))[:]
-                e_sb[k] = held([P, HALF], F32, "e%d" % k, {2: 93}.get(k))[:]
-            else:
-                d_neg[k], e_sb[k] = (last[:, i, HALF * (k - 6) : HALF * (k - 5)] for i in range(2))
-            d_bank, e_bank = ((4, 3), (7, 5))[max(i - 1, 0) % 2]
+        def sums(k, d_bank, e_bank):
             first_sum(k, d_bank)
             nc.scalar.copy(out=e_sb[k], in_=second_sum(k, e_bank)[:])
-        freed = 62
-        for k in order[:5]:
-            weigh(k, freed)
+
+        def vote(k, tag):
+            weigh(k, tag)
             nc.gpsimd.tensor_tensor(out=votes[k], in0=e_sb[k], in1=votes[k], op=MULT)
-            freed = {2: 93}.get(k, "e%d" % k)
             place(k)
-        weighed_last = held([P, S], F32, "weighed_last", freed)
+
+        for k in range(1, 6):
+            d_neg[k] = held([P, HALF], F32, "d%d" % k, {1: 142}.get(k))[:]
+            e_sb[k] = held([P, HALF], F32, "e%d" % k, {2: 124, 1: 146}.get(k))[:]
+        sums(2, 4, 3)
+        rest_w6 = held([P, 1024], BF16, "rest_w6", 48)
+        round_late(rest_w6[:], rest_raw[2], False)
+        rest_w3 = held([P, 2048], BF16, "rest_w3", 128)
+        for s in range(2):
+            round_late(rest_w3[:, 1024 * s : 1024 * (s + 1)], rest_raw[s], False)
+        late_q[1] = held([P, 768], U32, "late_q1", 136)
+        quantise_late(1, 512, 768, rest_w6[:])
+        quantise_late(1, 0, 512, rest_w3[:])
+        sums(1, 7, 5)
+        sums(3, 7, 5)
+        sums(4, 4, 3)
+        sums(5, 7, 5)
+        last = held([P, 2, S], F32, "last", "tab_w")
+        for k in (6, 7):
+            d_neg[k], e_sb[k] = (last[:, i, HALF * (k - 6) : HALF * (k - 5)] for i in range(2))
+        sums(6, 4, 3)
+        vote(2, 62)
+        vote(1, 126)
+        y_bf = held([P, 3, S], BF16, "y_bf")
+        finish(0)
+        sums(7, 2, 6)
+        vote(3, 146)
+        vote(4, "e3")
+        vote(5, "e4")
+        weighed_last = held([P, S], F32, "weighed_last", "e5")
         nc.gpsimd.tensor_tensor(out=weighed_last[:], in0=last[:, 0, :], in1=wgo_sb[:], op=MULT)
         page[3] = held([P, WINDOW], F32, "page3")
-        nc.gpsimd.tensor_tensor(out=weighed_last[:], in0=last[:, 1, :], in1=weighed_last[:], op=MULT)
-        nc.vector.tensor_copy(out=page[3][:].indirect(idx2[:]), in_=weighed_last[:])
-        y_bf = held([P, 3, S], BF16, "y_bf", "tab_w")
-        for c in range(3):
-            finish(c)
+        nc.vector.tensor_tensor(out=page[3][:].indirect(idx2[:]), in0=weighed_last[:], in1=last[:, 1, :], op=MULT)
+        finish(1)
+        finish(2)
         finish_last()

@@ -66,7 +66,6 @@ def tile_list_herbarium_expert_votes_kernel(
         amp_last = held([P, 1], F32, "amp_last")
         ident = held([P, P], F32, "ident")
 
-        nc.gpsimd.memset(tab_s[:].bitcast(I32), 0)
         nc.gpsimd.memset(w2_raw_s[:].bitcast(I32), 0)
         nc.gpsimd.memset(w4_s[:].bitcast(I32), 0)
         nc.gpsimd.memset(w5_s[:].rearrange("p a n -> p (a n)").bitcast(I32), 0)
@@ -81,12 +80,15 @@ def tile_list_herbarium_expert_votes_kernel(
             nc.sync.dma_start(out=w1_raw[i][:], in_=w1_rows[:, :, 256 * i : 256 * (i + 1)])
 
         nc.sync.dma_start(out=idx[:], in_=offs)
-        load_w1(0)
-        load_scale_rows(tab_s, tab_scales[0], range(4))
+        for q in range(4):
+            nc.sync.dma_start(
+                out=tab_s[32 * q : 32 * (q + 1)].bitcast(I32),
+                in_=tab_scales[0][4 * q : 4 * q + 4].bitcast(I32).unsqueeze(0).to_broadcast([8, 4, T // 4]),
+            )
         nc.sync.dma_start(out=tab_w[:].bitcast(I32), in_=tab_words[0].rearrange("p n t -> p (n t)").bitcast(I32))
-        nc.sync.dma_start(out=w2_raw[:].bitcast(I32), in_=w2_words[0].bitcast(I32))
         load_scale_rows(w2_raw_s, w2_scales[0], range(4))
-        for i in range(1, 4):
+        nc.sync.dma_start(out=w2_raw[:].bitcast(I32), in_=w2_words[0].bitcast(I32))
+        for i in range(4):
             load_w1(i)
         nc.sync.dma_start(out=first_raw[0], in_=late_rows[0][:, :, 0:256])
         load_scale_rows(w4_s, w4_scales[0], (0, 1))
@@ -133,14 +135,14 @@ def tile_list_herbarium_expert_votes_kernel(
         def round_on_gpsimd(out, in_):
             nc.gpsimd.tensor_scalar(out=out, in0=in_, scalar1=1.0, scalar2=0.0, op0=MULT, op1=ADD)
 
-        def round_w1(g, lo, hi, on_gpsimd):
+        def round_w1(g, lo, hi, on_gpsimd, copy=nc.scalar.copy):
             raw = w1_raw[2 * g + lo // 64][:, :, 4 * (lo % 64) : 4 * (lo % 64 + hi - lo)]
             if on_gpsimd:
                 dealt = w1_bf[g][:].rearrange("p (t m j) -> p m t j", t=4, j=4)
                 round_on_gpsimd(dealt[:, lo:hi], raw.rearrange("p j (m t) -> p m t j", t=4))
             else:
                 dealt = w1_bf[g][:].rearrange("p (t m j) -> p m j t", t=4, j=4)
-                nc.scalar.copy(out=dealt[:, lo:hi], in_=raw.rearrange("p j (m t) -> p m j t", t=4))
+                copy(out=dealt[:, lo:hi], in_=raw.rearrange("p j (m t) -> p m j t", t=4))
 
         def quantise(rounded, name, tag=None):
             codes = held([P, HALF], U32, name + "_q", tag)
@@ -267,8 +269,8 @@ def tile_list_herbarium_expert_votes_kernel(
                         )
             for hh in range(2):
                 nc.scalar.activation(
-                    out=sig[hh].rearrange("p t q -> p q t"),
-                    in_=z_ps[hh][:].rearrange("p u (a t) -> p (u a) t", t=4),
+                    out=sig[hh],
+                    in_=z_ps[hh][:].rearrange("p u (a t) -> p t (u a)", t=4),
                     func=ACT.Sigmoid,
                 )
             for hh in range(2):
@@ -344,10 +346,11 @@ def tile_list_herbarium_expert_votes_kernel(
                 )
 
         nc.vector.tensor_copy(out=v_s_all[:], in_=tab_s[:].indirect(idx[:]))
-        nc.scalar.copy(
-            out=w2_w[:].bitcast(U16).rearrange("p (g t m) -> p g t m", g=2, t=4),
-            in_=w2_raw[:].bitcast(U16).rearrange("p (g m t) -> p g t m", g=2, t=4),
-        )
+        for g in range(2):
+            nc.scalar.copy(
+                out=w2_w[:].bitcast(U16).rearrange("p (g t m) -> p g t m", g=2, t=4)[:, g],
+                in_=w2_raw[:].bitcast(U16).rearrange("p (g m t) -> p g t m", g=2, t=4)[:, g],
+            )
         gather_words(0, 1, None)
         nc.vector.tensor_copy(
             out=w2_s[:].rearrange("p (g t m) -> p g t m", g=2, t=4),
@@ -355,9 +358,10 @@ def tile_list_herbarium_expert_votes_kernel(
         )
         gather_words(1, 2, "w2_raw_s")
         w1_bf[0] = held([P, 4 * HALF], BF16, "w1_bf0", 0)
-        round_w1(0, 0, 64, False)
-        round_w1(0, 64, 104, False)
-        round_w1(0, 104, 128, True)
+        round_w1(0, 0, 40, False)
+        round_w1(0, 40, 64, True)
+        round_w1(0, 64, 84, False)
+        round_w1(0, 84, 128, False, nc.vector.tensor_copy)
         quantise_w1(0)
         gather_words(3, 1, 105)
         w1_bf[1] = held([P, 4 * HALF], BF16, "w1_bf1", 4)

@@ -58,7 +58,7 @@ def tile_list_herbarium_expert_votes_kernel(
         w1_raw = [held([P, 4, 256], F32, "w1_raw%d" % i, {1: 104, 3: 120}.get(i)) for i in range(4)]
         first_pair = held([P, 2, 4, 256], F32, "first_pair", 32)
         first_raw = [first_pair[:, 0], first_pair[:, 1], held([P, 4, 256], F32, "first_raw2", 52)[:]]
-        rest_pair = held([P, 2, 4, 256], F32, "rest_pair", 136)
+        rest_pair = held([P, 2, 4, 256], F32, "rest_pair")
         rest_raw = [rest_pair[:, 0], rest_pair[:, 1], held([P, 4, 256], F32, "rest_raw2", 88)[:]]
         wgo_sb = held([P, S], F32, "wgo_sb")
         x0_sb = [held([P, S], F32, "x0_sb%d" % c) for c in range(4)]
@@ -99,10 +99,10 @@ def tile_list_herbarium_expert_votes_kernel(
         nc.sync.dma_start(out=w4_w[:].bitcast(I32), in_=w4_words[0].rearrange("p n t -> p (n t)").bitcast(I32))
         nc.sync.dma_start(out=w5_w[:].bitcast(I32), in_=w5_words.rearrange("a p b -> p a b").bitcast(I32))
         load_scale_rows(w5_s, w5_scale_rows, (2, 3))
+        for s in range(3):
+            nc.sync.dma_start(out=rest_raw[s], in_=late_rows[s][:, :, 256:N])
         nc.sync.dma_start(out=wgo_sb[:], in_=wgo)
         nc.sync.dma_start(out=idx2[:], in_=offs2)
-        for s in (2, 0, 1):
-            nc.sync.dma_start(out=rest_raw[s], in_=late_rows[s][:, :, 256:N])
         for c in range(4):
             nc.sync.dma_start(out=x0_sb[c][:], in_=x0[P * c : P * (c + 1), :])
         for u in range(4):
@@ -254,7 +254,7 @@ def tile_list_herbarium_expert_votes_kernel(
         def place(k):
             c, b = divmod(k, 2)
             if b == 0:
-                page[c] = held([P, WINDOW], F32, "page%d" % c, ("w1_raw0", 150, "w1_raw2")[c])
+                page[c] = held([P, WINDOW], F32, "page%d" % c, (78, "w1_raw0", "w1_raw2")[c])
             nc.vector.tensor_copy(out=page[c][:].indirect(idx2[:, 32 * b : 32 * (b + 1)]), in_=votes[k])
 
         def turn(c, z_banks, y_spot, sig):
@@ -278,13 +278,14 @@ def tile_list_herbarium_expert_votes_kernel(
                     nc.tensor.transpose(y_spot(hh, t), sig[hh][:, t, :], ident[:])
 
         y_s = held([P, 256], U8, "y_s")
-        pairs = ((0, 1), (7, 5), (2, 6), (4, 3))
+        z_banks = ((4, 3), (7, 5))
+        y_banks = ((0, 1), (2, 6))
 
         def finish(c):
-            y_ps = [bank(number, [P, HALF]) for number in pairs[c + 1]]
+            y_ps = [bank(number, [P, HALF]) for number in y_banks[c % 2]]
             both = held([P, 2, 4, P], F32, "sig", "sig%d" % (c % 2))
             turn(
-                c, pairs[c],
+                c, z_banks[c % 2],
                 lambda hh, t: y_ps[t // 2][:, 256 * (t % 2) + P * hh : 256 * (t % 2) + P * (hh + 1)],
                 [both[:, hh] for hh in range(2)],
             )
@@ -294,13 +295,13 @@ def tile_list_herbarium_expert_votes_kernel(
                     out=y[:, t, :], in_=y_ps[t // 2][:, 256 * (t % 2) : 256 * (t % 2 + 1)], func=ACT.Copy,
                     scale=amp_sb[:, c, t : t + 1],
                 )
-            round_late(y_bf[:, c, :], y[:], False)
+            round_on_gpsimd(y_bf[:, c, :].rearrange("p (m t) -> p m t", t=4), y[:].rearrange("p t m -> p m t"))
             rows = out_0[P * c : P * (c + 1), :].rearrange("(a t) m -> a t m", t=4)
             for u in range(4):
                 nc.sync.dma_start(out=rows[:, :, 256 * u : 256 * (u + 1)], in_=y[32 * u : 32 * (u + 1)])
 
         def store_early_planes():
-            y_q = held([P, 3, 256], U32, "y_q_early", "tab_w")
+            y_q = held([P, 3, 256], U32, "y_q_early", "e5")
             for c in range(3):
                 nc.vector.quantize_mx(out=y_q[:, c, :].bitcast(FP8), scales=y_s[4 * c : P, :], in_=y_bf[:, c, :])
             words = out_1[0].rearrange("(c a) m t -> a c (m t)", c=4).bitcast(I32)
@@ -319,10 +320,10 @@ def tile_list_herbarium_expert_votes_kernel(
             store_early_planes()
             for cols in halves:
                 nc.vector.tensor_tensor(out=z[:, cols], in0=page[c][:, cols], in1=x0_sb[c][:, cols], op=ADD)
-            y_ps = [bank(number, [P, 4, P]) for number in pairs[0]]
+            y_ps = [bank(number, [P, 4, P]) for number in y_banks[c % 2]]
             sig = [held([P, 4, P], F32, "sig", "sig3%d" % hh)[:] for hh in range(2)]
-            turn(c, pairs[c], lambda hh, t: y_ps[hh][:, t, :], sig)
-            s_rows = held([P, S], F32, "s_rows", "sig30")
+            turn(c, z_banks[c % 2], lambda hh, t: y_ps[hh][:, t, :], sig)
+            s_rows = held([P, S], F32, "s_rows", "page3")
             for cols in halves:
                 nc.scalar.activation(out=s_rows[:, cols], in_=z[:, cols], func=ACT.Sigmoid)
             for hh in range(2):
@@ -396,51 +397,47 @@ def tile_list_herbarium_expert_votes_kernel(
         features(1, 1, 56, range(3))
         features(1, 1, 56, (3,), 5)
         e_first = second_sum(0, 6)
+        rest_bf = held([P, 3072], BF16, "rest_bf", 64)
+        for s in range(3):
+            round_late(rest_bf[:, 1024 * s : 1024 * (s + 1)], rest_raw[s], False)
         nc.vector.tensor_tensor(out=votes[0], in0=e_first[:], in1=votes[0], op=MULT)
         quantise_h(1, 1)
+        late_q[1] = held([P, 768], U32, "late_q1", "d0")
+        quantise_late(1, 0, 512, rest_bf[:, 0:2048])
+        quantise_late(1, 512, 768, rest_bf[:, 2048:3072])
         place(0)
 
-        def sums(k, d_bank, e_bank):
+        last = held([P, 2, S], F32, "last", "tab_w")
+        d_pair = held([P, 2, HALF], F32, "d_pair")
+        order = (2, 1, 4, 3, 5, 6, 7)
+        for i, k in enumerate(order):
+            if k < 6:
+                d_neg[k] = d_pair[:, k // 5] if k in (3, 5) else held([P, HALF], F32, "d%d" % k, {2: 89}.get(k))[:]
+                e_sb[k] = held([P, HALF], F32, "e%d" % k, {2: 93}.get(k))[:]
+            else:
+                d_neg[k], e_sb[k] = (last[:, i, HALF * (k - 6) : HALF * (k - 5)] for i in range(2))
+            d_bank, e_bank = ((4, 3), (7, 5))[max(i - 1, 0) % 2]
             first_sum(k, d_bank)
             nc.scalar.copy(out=e_sb[k], in_=second_sum(k, e_bank)[:])
-
-        def vote(k, tag):
-            weigh(k, tag)
+        freed = 62
+        for k in order[:5]:
+            if k == 3:
+                pair = held([P, 2, HALF], F32, "votes_pair", freed)
+                nc.gpsimd.tensor_tensor(
+                    out=pair[:], in0=d_pair[:], in1=wgo_sb[:, HALF:S].unsqueeze(1).to_broadcast([P, 2, HALF]), op=MULT
+                )
+                votes[3], votes[5] = pair[:, 0], pair[:, 1]
+            elif k != 5:
+                weigh(k, freed)
             nc.gpsimd.tensor_tensor(out=votes[k], in0=e_sb[k], in1=votes[k], op=MULT)
+            freed = {2: 93}.get(k, "e%d" % k)
             place(k)
-
-        for k in range(1, 6):
-            d_neg[k] = held([P, HALF], F32, "d%d" % k, {1: 142}.get(k))[:]
-            e_sb[k] = held([P, HALF], F32, "e%d" % k, {2: 124, 1: 146}.get(k))[:]
-        sums(2, 4, 3)
-        rest_w6 = held([P, 1024], BF16, "rest_w6", 48)
-        round_late(rest_w6[:], rest_raw[2], False)
-        rest_w3 = held([P, 2048], BF16, "rest_w3", 128)
-        for s in range(2):
-            round_late(rest_w3[:, 1024 * s : 1024 * (s + 1)], rest_raw[s], False)
-        late_q[1] = held([P, 768], U32, "late_q1", 136)
-        quantise_late(1, 512, 768, rest_w6[:])
-        quantise_late(1, 0, 512, rest_w3[:])
-        sums(1, 7, 5)
-        sums(3, 7, 5)
-        sums(4, 4, 3)
-        sums(5, 7, 5)
-        last = held([P, 2, S], F32, "last", "tab_w")
-        for k in (6, 7):
-            d_neg[k], e_sb[k] = (last[:, i, HALF * (k - 6) : HALF * (k - 5)] for i in range(2))
-        sums(6, 4, 3)
-        vote(2, 62)
-        vote(1, 126)
-        y_bf = held([P, 3, S], BF16, "y_bf")
-        finish(0)
-        sums(7, 2, 6)
-        vote(3, 146)
-        vote(4, "e3")
-        vote(5, "e4")
-        weighed_last = held([P, S], F32, "weighed_last", "e5")
+        weighed_last = held([P, S], F32, "weighed_last", freed)
         nc.gpsimd.tensor_tensor(out=weighed_last[:], in0=last[:, 0, :], in1=wgo_sb[:], op=MULT)
         page[3] = held([P, WINDOW], F32, "page3")
-        nc.vector.tensor_tensor(out=page[3][:].indirect(idx2[:]), in0=weighed_last[:], in1=last[:, 1, :], op=MULT)
-        finish(1)
-        finish(2)
+        nc.gpsimd.tensor_tensor(out=weighed_last[:], in0=last[:, 1, :], in1=weighed_last[:], op=MULT)
+        nc.vector.tensor_copy(out=page[3][:].indirect(idx2[:]), in_=weighed_last[:])
+        y_bf = held([P, 3, S], BF16, "y_bf", "tab_w")
+        for c in range(3):
+            finish(c)
         finish_last()

@@ -337,7 +337,9 @@ def tile_list_herbarium_expert_votes_kernel(
                 nc.vector.quantize_mx(out=y_q[:, cols].bitcast(FP8), scales=y_s[4 * c : P, cols], in_=y_last_bf[:, halves[hh]])
                 nc.sync.dma_start(out=words[:, :, cols], in_=y_q[:, cols].bitcast(I32))
                 if hh == 0:
-                    nc.vector.tensor_scalar(out=y[:, halves[0]], in0=s_rows[:, halves[0]], scalar1=amp_last[:, 0:1], scalar2=None, op0=MULT)
+                    nc.gpsimd.tensor_scalar(
+                        out=y[:, halves[0]], in0=s_rows[:, halves[0]], scalar1=amp_last[:, 0:1], scalar2=0.0, op0=MULT, op1=ADD
+                    )
                 else:
                     nc.scalar.activation(out=y[:, halves[1]], in_=s_rows[:, halves[1]], func=ACT.Copy, scale=amp_last[:, 0:1])
                 nc.sync.dma_start(out=out_0[N - P : N, halves[hh]], in_=y[:, halves[hh]])

@@ -314,18 +314,25 @@ def tile_list_herbarium_expert_votes_kernel(
             c = 3
             halves = [slice(HALF * hh, HALF * (hh + 1)) for hh in range(2)]
             z = held([P, S], F32, "z_last")
-            y = held([P, S], F32, "y_last")
             y_last_bf = held([P, S], BF16, "y_last_bf")
             y_q = held([P, 256], U32, "y_q_last")
-            store_early_planes()
-            for cols in halves:
+            early = [slice(0, 256), slice(256, HALF)]
+            for cols in early + halves[1:]:
                 nc.vector.tensor_tensor(out=z[:, cols], in0=page[c][:, cols], in1=x0_sb[c][:, cols], op=ADD)
+            store_early_planes()
+            s_rows = [held([P, HALF], F32, "s_rows0", "sig0")]
+            for cols in early:
+                nc.scalar.activation(out=s_rows[0][:, cols], in_=z[:, cols], func=ACT.Sigmoid)
             y_ps = [bank(number, [P, 4, P]) for number in y_banks[c % 2]]
             sig = [held([P, 4, P], F32, "sig", "sig3%d" % hh)[:] for hh in range(2)]
             turn(c, z_banks[c % 2], lambda hh, t: y_ps[hh][:, t, :], sig)
-            s_rows = held([P, S], F32, "s_rows", "page3")
-            for cols in halves:
-                nc.scalar.activation(out=s_rows[:, cols], in_=z[:, cols], func=ACT.Sigmoid)
+            s_rows.append(held([P, HALF], F32, "s_rows1", "page3"))
+            nc.scalar.activation(out=s_rows[1][:], in_=z[:, halves[1]], func=ACT.Sigmoid)
+            y = [held([P, HALF], F32, "y_last0", "tab_w"), held([P, HALF], F32, "y_last1")]
+            nc.gpsimd.tensor_scalar(out=y[0][:], in0=s_rows[0][:], scalar1=amp_last[:, 0:1], scalar2=0.0, op0=MULT, op1=ADD)
+            nc.scalar.activation(out=y[1][:], in_=s_rows[1][:], func=ACT.Copy, scale=amp_last[:, 0:1])
+            for hh in range(2):
+                nc.sync.dma_start(out=out_0[N - P : N, halves[hh]], in_=y[hh][:])
             for hh in range(2):
                 nc.vector.tensor_tensor(
                     out=y_last_bf[:, halves[hh]].rearrange("p (m t) -> p m t", t=4), in0=y_ps[hh][:].rearrange("p t m -> p m t"),
@@ -336,13 +343,6 @@ def tile_list_herbarium_expert_votes_kernel(
                 cols = slice(P * hh, P * (hh + 1))
                 nc.vector.quantize_mx(out=y_q[:, cols].bitcast(FP8), scales=y_s[4 * c : P, cols], in_=y_last_bf[:, halves[hh]])
                 nc.sync.dma_start(out=words[:, :, cols], in_=y_q[:, cols].bitcast(I32))
-                if hh == 0:
-                    nc.gpsimd.tensor_scalar(
-                        out=y[:, halves[0]], in0=s_rows[:, halves[0]], scalar1=amp_last[:, 0:1], scalar2=0.0, op0=MULT, op1=ADD
-                    )
-                else:
-                    nc.scalar.activation(out=y[:, halves[1]], in_=s_rows[:, halves[1]], func=ACT.Copy, scale=amp_last[:, 0:1])
-                nc.sync.dma_start(out=out_0[N - P : N, halves[hh]], in_=y[:, halves[hh]])
             for u in range(4):
                 nc.sync.dma_start(
                     out=out_2[0][:, 256 * u : 256 * (u + 1)].bitcast(I32), in_=y_s[32 * u : 32 * u + 16, :].bitcast(I32)

@@ -21,6 +21,7 @@ ACT = mybir.ActivationFunctionType
 P = 128
 HALF = 512
 WINDOW = 1376
+QUADRANTS = (0, 2, 1, 3)
 
 
 def tile_list_herbarium_expert_votes_kernel(
@@ -55,7 +56,7 @@ def tile_list_herbarium_expert_votes_kernel(
         w4_s = held([P, N], U8, "w4_s")
         w5_w = held([P, 2, 2 * N], U8, "w5_w")
         w5_s = held([P, 2, N], U8, "w5_s")
-        w1_raw = [held([P, 4, 256], F32, "w1_raw%d" % i, {1: 104, 3: 120}.get(i)) for i in range(4)]
+        w1_raw = [held([P, 4, 256], F32, "w1_raw%d" % i, {1: 104, 2: 128, 3: 120}.get(i)) for i in range(4)]
         first_pair = held([P, 2, 4, 256], F32, "first_pair", 32)
         first_raw = [first_pair[:, 0], first_pair[:, 1], held([P, 4, 256], F32, "first_raw2", 52)[:]]
         rest_pair = held([P, 2, 4, 256], F32, "rest_pair")
@@ -254,7 +255,7 @@ def tile_list_herbarium_expert_votes_kernel(
         def place(k):
             c, b = divmod(k, 2)
             if b == 0:
-                page[c] = held([P, WINDOW], F32, "page%d" % c, (78, "w1_raw0", "w1_raw2")[c])
+                page[c] = held([P, WINDOW], F32, "page%d" % c, (78, "w1_raw0", 128)[c])
             nc.vector.tensor_copy(out=page[c][:].indirect(idx2[:, 32 * b : 32 * (b + 1)]), in_=votes[k])
 
         def turn(c, z_banks, y_spot, sig):
@@ -297,7 +298,7 @@ def tile_list_herbarium_expert_votes_kernel(
                 )
             round_on_gpsimd(y_bf[:, c, :].rearrange("p (m t) -> p m t", t=4), y[:].rearrange("p t m -> p m t"))
             rows = out_0[P * c : P * (c + 1), :].rearrange("(a t) m -> a t m", t=4)
-            for u in range(4):
+            for u in QUADRANTS:
                 nc.sync.dma_start(out=rows[:, :, 256 * u : 256 * (u + 1)], in_=y[32 * u : 32 * (u + 1)])
 
         def store_early_planes():
@@ -305,7 +306,7 @@ def tile_list_herbarium_expert_votes_kernel(
             for c in range(3):
                 nc.vector.quantize_mx(out=y_q[:, c, :].bitcast(FP8), scales=y_s[4 * c : P, :], in_=y_bf[:, c, :])
             words = out_1[0].rearrange("(c a) m t -> a c (m t)", c=4).bitcast(I32)
-            for u in range(4):
+            for u in QUADRANTS:
                 nc.sync.dma_start(
                     out=words[:, 0:3, 256 * u : 256 * (u + 1)], in_=y_q[32 * u : 32 * (u + 1)].bitcast(I32)
                 )
@@ -343,7 +344,7 @@ def tile_list_herbarium_expert_votes_kernel(
                 cols = slice(P * hh, P * (hh + 1))
                 nc.vector.quantize_mx(out=y_q[:, cols].bitcast(FP8), scales=y_s[4 * c : P, cols], in_=y_last_bf[:, halves[hh]])
                 nc.sync.dma_start(out=words[:, :, cols], in_=y_q[:, cols].bitcast(I32))
-            for u in range(4):
+            for u in QUADRANTS:
                 nc.sync.dma_start(
                     out=out_2[0][:, 256 * u : 256 * (u + 1)].bitcast(I32), in_=y_s[32 * u : 32 * u + 16, :].bitcast(I32)
                 )
@@ -368,15 +369,15 @@ def tile_list_herbarium_expert_votes_kernel(
         quantise_w1(0)
         gather_words(3, 1, 105)
         w1_bf[1] = held([P, 4 * HALF], BF16, "w1_bf1", 4)
-        round_w1(1, 0, 64, True)
-        round_w1(1, 64, 96, True)
-        round_w1(1, 96, 128, False)
+        round_w1(1, 0, 32, False)
+        round_w1(1, 32, 64, True)
+        round_w1(1, 64, 128, True)
 
         first_fp4_products()
         features(0, 0, 12, (0, 1))
         fp4_products(0, 0, (None, 111), (1,))
         features(0, 0, 12, (2, 3))
-        fp4_products(1, 0, (124, None))
+        fp4_products(1, 0, (132, None))
         quantise_w1(1)
         quantise_h(0, 0, 120)
         first_w3 = held([P, 2048], BF16, "first_w3", 11)
@@ -392,7 +393,7 @@ def tile_list_herbarium_expert_votes_kernel(
         features(0, 1, 36)
         d_neg[0] = held([P, HALF], F32, "d0")[:]
         first_sum(0, 7)
-        fp4_products(1, 1, (124, "b_sb101"))
+        fp4_products(1, 1, (132, "b_sb101"))
         quantise_late(0, 512, 768, first_w6[:])
         quantise_h(0, 1, 52)
         weigh(0, 36)

@@ -360,18 +360,19 @@ def tile_list_herbarium_expert_votes_kernel(
             out=w2_s[:].rearrange("p (g t m) -> p g t m", g=2, t=4),
             in_=w2_raw_s[:].rearrange("p (g m t) -> p g t m", g=2, t=4),
         )
-        gather_words(1, 2, "w2_raw_s")
+        gather_words(1, 1, "w2_raw_s")
         w1_bf[0] = held([P, 4 * HALF], BF16, "w1_bf0", 0)
         round_w1(0, 0, 40, False)
-        round_w1(0, 40, 64, True)
+        round_w1(0, 40, 64, False, nc.vector.tensor_copy)
         round_w1(0, 64, 84, False)
         round_w1(0, 84, 128, False, nc.vector.tensor_copy)
         quantise_w1(0)
-        gather_words(3, 1, 105)
+        gather_words(2, 2, 105)
         w1_bf[1] = held([P, 4 * HALF], BF16, "w1_bf1", 4)
         round_w1(1, 0, 32, False)
         round_w1(1, 32, 64, True)
-        round_w1(1, 64, 128, True)
+        round_w1(1, 64, 104, True)
+        round_w1(1, 104, 128, False)
 
         first_fp4_products()
         features(0, 0, 12, (0, 1))

@@ -21,6 +21,7 @@ ACT = mybir.ActivationFunctionType
 P = 128
 HALF = 512
 WINDOW = 1376
+W1_CUTS = (0, 256, 512, 864, 1024)
 QUADRANTS = (0, 2, 1, 3)
 
 
@@ -56,7 +57,7 @@ def tile_list_herbarium_expert_votes_kernel(
         w4_s = held([P, N], U8, "w4_s")
         w5_w = held([P, 2, 2 * N], U8, "w5_w")
         w5_s = held([P, 2, N], U8, "w5_s")
-        w1_raw = [held([P, 4, 256], F32, "w1_raw%d" % i, {1: 104, 2: 128, 3: 120}.get(i)) for i in range(4)]
+        w1_raw = [held([P, 4, W1_CUTS[i + 1] - W1_CUTS[i]], F32, "w1_raw%d" % i, (147, 104, 125, 120)[i]) for i in range(4)]
         first_pair = held([P, 2, 4, 256], F32, "first_pair", 32)
         first_raw = [first_pair[:, 0], first_pair[:, 1], held([P, 4, 256], F32, "first_raw2", 52)[:]]
         rest_pair = held([P, 2, 4, 256], F32, "rest_pair")
@@ -78,7 +79,7 @@ def tile_list_herbarium_expert_votes_kernel(
         w5_scale_rows = w5_scales.rearrange("a r n -> r a n")
 
         def load_w1(i):
-            nc.sync.dma_start(out=w1_raw[i][:], in_=w1_rows[:, :, 256 * i : 256 * (i + 1)])
+            nc.sync.dma_start(out=w1_raw[i][:], in_=w1_rows[:, :, W1_CUTS[i] : W1_CUTS[i + 1]])
 
         nc.sync.dma_start(out=idx[:], in_=offs)
         for q in range(4):
@@ -137,7 +138,8 @@ def tile_list_herbarium_expert_votes_kernel(
             nc.gpsimd.tensor_scalar(out=out, in0=in_, scalar1=1.0, scalar2=0.0, op0=MULT, op1=ADD)
 
         def round_w1(g, lo, hi, on_gpsimd, copy=nc.scalar.copy):
-            raw = w1_raw[2 * g + lo // 64][:, :, 4 * (lo % 64) : 4 * (lo % 64 + hi - lo)]
+            i = max(load for load in range(4) if W1_CUTS[load] <= HALF * g + 4 * lo)
+            raw = w1_raw[i][:, :, HALF * g + 4 * lo - W1_CUTS[i] : HALF * g + 4 * hi - W1_CUTS[i]]
             if on_gpsimd:
                 dealt = w1_bf[g][:].rearrange("p (t m j) -> p m t j", t=4, j=4)
                 round_on_gpsimd(dealt[:, lo:hi], raw.rearrange("p j (m t) -> p m t j", t=4))
@@ -153,6 +155,13 @@ def tile_list_herbarium_expert_votes_kernel(
 
         def quantise_w1(g):
             w1_q[g], w1_s[g] = quantise(w1_bf[g][:], "w1_%d" % g)
+
+        def quantise_w1_load(i):
+            for t in range(4):
+                lo = P * t + 64 * i
+                nc.vector.quantize_mx(
+                    out=w1_q[0][:, lo : lo + 64].bitcast(FP8), scales=w1_s[0][:, lo : lo + 64], in_=w1_bf[0][:, 4 * lo : 4 * (lo + 64)]
+                )
 
         def quantise_h(g, b, tag=None):
             h_q[g, b], h_s[g, b] = quantise(h_bf[g, b][:].rearrange("p n t -> p (n t)"), "h_%d%d" % (g, b), tag)
@@ -172,7 +181,7 @@ def tile_list_herbarium_expert_votes_kernel(
             cols = slice(256 * s + P * (c % 2), 256 * s + P * (c % 2 + 1))
             return late_q[c // 2][:, cols].bitcast(FP8), late_s[c // 2][:, cols]
 
-        b_sb = {}
+        b_sb, b_first = {}, {}
 
         def fp4_products(g, b, tags, halves=(0, 1)):
             for half in halves:
@@ -180,7 +189,7 @@ def tile_list_herbarium_expert_votes_kernel(
                 step = 4 * b + 2 * g + half
                 cols = slice(256 * half, 256 * (half + 1))
                 for pair in range(2):
-                    b_ps = bank((3, 4, 5, 3, 4, 6, 7, 5, 3, 4, 6, 7, 5, 3, 6, 4)[2 * step + pair], [P, 2, 256])
+                    b_ps = bank((3, 4, 5, 6, 3, 4, 7, 5, 3, 4, 6, 7, 5, 3, 6, 4)[2 * step + pair], [P, 2, 256])
                     for e in range(2):
                         lo = HALF * g + P * (2 * pair + e)
                         nc.tensor.matmul_mx(
@@ -191,8 +200,8 @@ def tile_list_herbarium_expert_votes_kernel(
                     nc.scalar.copy(out=b_sb[g, b, half][:, pair], in_=b_ps[:].rearrange("p e n -> p n e"))
 
         def first_fp4_products():
-            b_sb[0, 0, 0] = held([P, 2, 256, 2], F32, "b_sb000", 97)
             for jb in range(2):
+                b_first[jb] = held([P, P, 4], F32, "b_first%d" % jb, (148, 101)[jb])
                 cols = slice(P * jb, P * (jb + 1))
                 b_ps = bank(3 + jb, [P, 4, P])
                 for t in range(4):
@@ -201,7 +210,7 @@ def tile_list_herbarium_expert_votes_kernel(
                         lhsT=w2_w[:, 2 * P * t : 2 * P * (t + 1)].bitcast(FP4), lhsT_scale=w2_s[:, P * t : P * (t + 1)],
                         rhs=v_w[0][:, cols].bitcast(FP8), rhs_scale=v_s[0][:, cols], start=True, stop=True,
                     )
-                nc.scalar.copy(out=b_sb[0, 0, 0][:, :, cols, :], in_=b_ps[:].rearrange("p (q e) n -> p q n e", q=2))
+                nc.scalar.copy(out=b_first[jb][:], in_=b_ps[:].rearrange("p t n -> p n t"))
 
         def features(g, b, tag, pieces=range(4), last_bank=None):
             if 0 in pieces:
@@ -209,17 +218,21 @@ def tile_list_herbarium_expert_votes_kernel(
             for piece in pieces:
                 half, jb = divmod(piece, 2)
                 cols = slice(P * piece, P * (piece + 1))
-                a_ps = bank(last_bank or {0: 6, 1: 7}.get(8 * b + 4 * g + piece, (8 * b + 4 * g + piece) % 3), [P, 4, P])
+                a_ps = bank(last_bank or {0: 7}.get(8 * b + 4 * g + piece, (8 * b + 4 * g + piece) % 3), [P, 4, P])
                 for t in range(4):
                     nc.tensor.matmul_mx(
                         out=a_ps[:, t, :],
                         lhsT=w1_q[g][:, P * t : P * (t + 1)].bitcast(FP8), lhsT_scale=w1_s[g][:, P * t : P * (t + 1)],
                         rhs=v_w[2 * b + half][:, P * jb : P * (jb + 1)].bitcast(FP8), rhs_scale=v_s[b][:, cols], start=True, stop=True,
                     )
+                if (g, b, half) == (0, 0, 0):
+                    b_piece = b_first[jb][:].rearrange("p n (q e) -> p n q e", q=2)
+                else:
+                    b_piece = b_sb[g, b, half][:, :, P * jb : P * (jb + 1), :].rearrange("p q n e -> p n q e")
                 nc.vector.tensor_tensor(
                     out=h_bf[g, b][:, cols, :].rearrange("p n (q e) -> p n q e", q=2),
                     in0=a_ps[:].rearrange("p (q e) n -> p n q e", q=2),
-                    in1=b_sb[g, b, half][:, :, P * jb : P * (jb + 1), :].rearrange("p q n e -> p n q e"), op=MULT,
+                    in1=b_piece, op=MULT,
                 )
 
         d_neg, e_sb, votes, page = {}, {}, {}, {}
@@ -255,7 +268,7 @@ def tile_list_herbarium_expert_votes_kernel(
         def place(k):
             c, b = divmod(k, 2)
             if b == 0:
-                page[c] = held([P, WINDOW], F32, "page%d" % c, (78, "w1_raw0", 128)[c])
+                page[c] = held([P, WINDOW], F32, "page%d" % c, (78, 147, 128)[c])
             nc.vector.tensor_copy(out=page[c][:].indirect(idx2[:, 32 * b : 32 * (b + 1)]), in_=votes[k])
 
         def turn(c, z_banks, y_spot, sig):
@@ -364,19 +377,20 @@ def tile_list_herbarium_expert_votes_kernel(
         w1_bf[0] = held([P, 4 * HALF], BF16, "w1_bf0", 0)
         round_w1(0, 0, 40, False)
         round_w1(0, 40, 64, False, nc.vector.tensor_copy)
+        w1_q[0], w1_s[0] = held([P, HALF], U32, "w1_0_q")[:], held([P, HALF], U8, "w1_0_s")[:]
+        quantise_w1_load(0)
         round_w1(0, 64, 84, False)
         round_w1(0, 84, 128, False, nc.vector.tensor_copy)
-        quantise_w1(0)
+        quantise_w1_load(1)
         gather_words(2, 2, 105)
         w1_bf[1] = held([P, 4 * HALF], BF16, "w1_bf1", 4)
-        round_w1(1, 0, 32, False)
-        round_w1(1, 32, 64, True)
-        round_w1(1, 64, 104, True)
-        round_w1(1, 104, 128, False)
+        round_w1(1, 56, 88, True)
+        round_w1(1, 88, 128, True)
 
         first_fp4_products()
         features(0, 0, 12, (0, 1))
         fp4_products(0, 0, (None, 111), (1,))
+        round_w1(1, 0, 56, False)
         features(0, 0, 12, (2, 3))
         fp4_products(1, 0, (132, None))
         quantise_w1(1)

@@ -58,8 +58,7 @@ def tile_list_herbarium_expert_votes_kernel(
         w5_w = held([P, 2, 2 * N], U8, "w5_w")
         w5_s = held([P, 2, N], U8, "w5_s")
         w1_raw = [held([P, 4, W1_CUTS[i + 1] - W1_CUTS[i]], F32, "w1_raw%d" % i, (147, 104, 125, 120)[i]) for i in range(4)]
-        first_pair = held([P, 2, 4, 256], F32, "first_pair", 32)
-        first_raw = [first_pair[:, 0], first_pair[:, 1], held([P, 4, 256], F32, "first_raw2", 52)[:]]
+        first_raw = [held([P, 4, 256], F32, "first_raw%d" % s, (32, 165, 52)[s])[:] for s in range(3)]
         rest_pair = held([P, 2, 4, 256], F32, "rest_pair")
         rest_raw = [rest_pair[:, 0], rest_pair[:, 1], held([P, 4, 256], F32, "rest_raw2", 88)[:]]
         wgo_sb = held([P, S], F32, "wgo_sb")
@@ -296,28 +295,30 @@ def tile_list_herbarium_expert_votes_kernel(
         y_banks = ((0, 1), (2, 6))
 
         def finish(c):
-            y_ps = [bank(number, [P, HALF]) for number in y_banks[c % 2]]
+            y_ps = [bank(number, [P, 4, P]) for number in y_banks[c % 2]]
             both = held([P, 2, 4, P], F32, "sig", "sig%d" % (c % 2))
-            turn(
-                c, z_banks[c % 2],
-                lambda hh, t: y_ps[t // 2][:, 256 * (t % 2) + P * hh : 256 * (t % 2) + P * (hh + 1)],
-                [both[:, hh] for hh in range(2)],
-            )
+            turn(c, z_banks[c % 2], lambda hh, t: y_ps[hh][:, t, :], [both[:, hh] for hh in range(2)])
             y = held([P, 4, 256], F32, "y%d" % c)
-            for t in range(4):
-                nc.scalar.activation(
-                    out=y[:, t, :], in_=y_ps[t // 2][:, 256 * (t % 2) : 256 * (t % 2 + 1)], func=ACT.Copy,
-                    scale=amp_sb[:, c, t : t + 1],
-                )
-            round_on_gpsimd(y_bf[:, c, :].rearrange("p (m t) -> p m t", t=4), y[:].rearrange("p t m -> p m t"))
+            for hh in range(2):
+                cols = slice(P * hh, P * (hh + 1))
+                for t in range(4):
+                    nc.scalar.activation(out=y[:, t, cols], in_=y_ps[hh][:, t, :], func=ACT.Copy, scale=amp_sb[:, c, t : t + 1])
+                if c == 2:
+                    round_on_gpsimd(
+                        y_bf[c][:, HALF * hh : HALF * (hh + 1)].rearrange("p (m t) -> p m t", t=4), y[:, :, cols].rearrange("p t m -> p m t")
+                    )
+            if c == 1:
+                round_on_gpsimd(y_bf[c].rearrange("p (m t) -> p m t", t=4), y[:].rearrange("p t m -> p m t"))
+            if c == 0:
+                nc.scalar.copy(out=y_bf[c].rearrange("p (a i t) -> p a t i", i=4, t=4), in_=y[:].rearrange("p t (a i) -> p a t i", i=4))
             rows = out_0[P * c : P * (c + 1), :].rearrange("(a t) m -> a t m", t=4)
             for u in QUADRANTS:
                 nc.sync.dma_start(out=rows[:, :, 256 * u : 256 * (u + 1)], in_=y[32 * u : 32 * (u + 1)])
 
         def store_early_planes():
-            y_q = held([P, 3, 256], U32, "y_q_early", "e5")
+            y_q = held([P, 3, 256], U32, "y_q_early", 8)
             for c in range(3):
-                nc.vector.quantize_mx(out=y_q[:, c, :].bitcast(FP8), scales=y_s[4 * c : P, :], in_=y_bf[:, c, :])
+                nc.vector.quantize_mx(out=y_q[:, c, :].bitcast(FP8), scales=y_s[4 * c : P, :], in_=y_bf[c])
             words = out_1[0].rearrange("(c a) m t -> a c (m t)", c=4).bitcast(I32)
             for u in QUADRANTS:
                 nc.sync.dma_start(
@@ -342,7 +343,7 @@ def tile_list_herbarium_expert_votes_kernel(
             turn(c, z_banks[c % 2], lambda hh, t: y_ps[hh][:, t, :], sig)
             s_rows.append(held([P, HALF], F32, "s_rows1", "page3"))
             nc.scalar.activation(out=s_rows[1][:], in_=z[:, halves[1]], func=ACT.Sigmoid)
-            y = [held([P, HALF], F32, "y_last0", "tab_w"), held([P, HALF], F32, "y_last1")]
+            y = [held([P, HALF], F32, "y_last0", 0), held([P, HALF], F32, "y_last1")]
             nc.gpsimd.tensor_scalar(out=y[0][:], in0=s_rows[0][:], scalar1=amp_last[:, 0:1], scalar2=0.0, op0=MULT, op1=ADD)
             nc.scalar.activation(out=y[1][:], in_=s_rows[1][:], func=ACT.Copy, scale=amp_last[:, 0:1])
             for hh in range(2):
@@ -384,22 +385,22 @@ def tile_list_herbarium_expert_votes_kernel(
         quantise_w1_load(1)
         gather_words(2, 2, 105)
         w1_bf[1] = held([P, 4 * HALF], BF16, "w1_bf1", 4)
-        round_w1(1, 56, 88, True)
+        round_w1(1, 72, 88, True)
         round_w1(1, 88, 128, True)
 
         first_fp4_products()
         features(0, 0, 12, (0, 1))
         fp4_products(0, 0, (None, 111), (1,))
-        round_w1(1, 0, 56, False)
+        round_w1(1, 0, 72, False)
         features(0, 0, 12, (2, 3))
-        fp4_products(1, 0, (132, None))
+        fp4_products(1, 0, (133, 125))
         quantise_w1(1)
         quantise_h(0, 0, 120)
         first_w3 = held([P, 2048], BF16, "first_w3", 11)
         round_late(first_w3[:, 0:1024], first_raw[0], True)
         round_late(first_w3[:, 1024:2048], first_raw[1], False)
         features(1, 0, 20)
-        fp4_products(0, 1, (97, 44))
+        fp4_products(0, 1, (158, 172))
         late_q[0] = held([P, 768], U32, "late_q0")
         quantise_late(0, 0, 512, first_w3[:])
         quantise_h(1, 0, 32)
@@ -408,7 +409,7 @@ def tile_list_herbarium_expert_votes_kernel(
         features(0, 1, 36)
         d_neg[0] = held([P, HALF], F32, "d0")[:]
         first_sum(0, 7)
-        fp4_products(1, 1, (132, "b_sb101"))
+        fp4_products(1, 1, (133, 125))
         quantise_late(0, 512, 768, first_w6[:])
         quantise_h(0, 1, 52)
         weigh(0, 36)
@@ -425,7 +426,7 @@ def tile_list_herbarium_expert_votes_kernel(
         quantise_late(1, 512, 768, rest_bf[:, 2048:3072])
         place(0)
 
-        last = held([P, 2, S], F32, "last", "tab_w")
+        last = held([P, 2, S], F32, "last", 0)
         d_pair = held([P, 2, HALF], F32, "d_pair")
         order = (2, 1, 4, 3, 5, 6, 7)
         for i, k in enumerate(order):
@@ -455,7 +456,8 @@ def tile_list_herbarium_expert_votes_kernel(
         page[3] = held([P, WINDOW], F32, "page3")
         nc.gpsimd.tensor_tensor(out=weighed_last[:], in0=last[:, 1, :], in1=weighed_last[:], op=MULT)
         nc.vector.tensor_copy(out=page[3][:].indirect(idx2[:]), in_=weighed_last[:])
-        y_bf = held([P, 3, S], BF16, "y_bf", "tab_w")
+        y_late = held([P, 2, S], BF16, "y_late", 0)
+        y_bf = [held([P, S], BF16, "y_bf0")[:], y_late[:, 0], y_late[:, 1]]
         for c in range(3):
             finish(c)
         finish_last()

from contextlib import ExitStack

import concourse.mybir as mybir
from concourse.masks import make_identity

K, T, S, H, N = 512, 2048, 1024, 1024, 512
FLOPS = 2 * S * (2 * K * H + 2 * H * N + 2 * K * N)

F32 = mybir.dt.float32
BF16 = mybir.dt.bfloat16
I32 = mybir.dt.int32
U32 = mybir.dt.uint32
U16 = mybir.dt.uint16
U8 = mybir.dt.uint8
FP8 = mybir.dt.float8_e4m3fn_x4
FP4 = mybir.dt.float4_e2m1fn_x4
MULT = mybir.AluOpType.mult
ADD = mybir.AluOpType.add
ACT = mybir.ActivationFunctionType

P = 128
HALF = 512
WINDOW = 1376
W1_CUTS = (0, 256, 512, 864, 1024)
QUADRANTS = (0, 2, 1, 3)


def tile_list_herbarium_expert_votes_kernel(
    tc, tab_words, tab_scales, offs, offs2, w1, w2_words, w2_scales, w3, w4_words, w4_scales,
    w5_words, w5_scales, w6, wgo, x0, amp, out_0, out_1, out_2,
):
    nc = tc.nc
    with ExitStack() as ctx:
        keep = ctx.enter_context(tc.tile_pool(name="keep", bufs=1))
        chain = ctx.enter_context(tc.tile_pool(name="chain", bufs=1))
        psum = ctx.enter_context(tc.psum_pool(name="psum", bufs=1))

        def held(shape, dtype, name, tag=None):
            if isinstance(tag, int):
                return chain.tile(shape, dtype, name=name, tag=name, align_bytes=64, offset=512 * tag)
            return keep.tile(shape, dtype, name=name, tag=tag or name, align_bytes=64)

        def bank(number, shape):
            return psum.tile(shape, F32, name="bank", tag="bank%d" % number)

        def load_scale_rows(plane, rows, quadrants):
            for q in quadrants:
                nc.sync.dma_start(out=plane[32 * q : 32 * q + 4].bitcast(I32), in_=rows[4 * q : 4 * q + 4].bitcast(I32))

        idx = keep.tile([P, S // 16], U16, name="idx")
        idx2 = keep.tile([P, S // 16], U16, name="idx2")
        tab_w = held([P, T], U32, "tab_w")
        tab_s = held([P, T], U8, "tab_s")
        w2_raw = held([P, 2 * H], U8, "w2_raw")
        w2_raw_s = held([P, H], U8, "w2_raw_s")
        w4_w = held([P, N], U32, "w4_w")
        w4_s = held([P, N], U8, "w4_s")
        w5_w = held([P, 2, 2 * N], U8, "w5_w")
        w5_s = held([P, 2, N], U8, "w5_s")
        w1_raw = [held([P, 4, W1_CUTS[i + 1] - W1_CUTS[i]], F32, "w1_raw%d" % i, (147, 104, 125, 120)[i]) for i in range(4)]
        first_raw = [held([P, 4, 256], F32, "first_raw%d" % s, (32, 165, 52)[s])[:] for s in range(3)]
        rest_pair = held([P, 2, 4, 256], F32, "rest_pair")
        rest_raw = [rest_pair[:, 0], rest_pair[:, 1], held([P, 4, 256], F32, "rest_raw2", 88)[:]]
        wgo_sb = held([P, S], F32, "wgo_sb")
        x0_sb = [held([P, S], F32, "x0_sb%d" % c) for c in range(4)]
        amp_sb = held([P, 4, 4], F32, "amp_sb")
        amp_last = held([P, 1], F32, "amp_last")
        ident = held([P, P], F32, "ident")

        nc.gpsimd.memset(w2_raw_s[:].bitcast(I32), 0)
        nc.gpsimd.memset(w4_s[:].bitcast(I32), 0)
        nc.gpsimd.memset(w5_s[:].rearrange("p a n -> p (a n)").bitcast(I32), 0)
        make_identity(nc, ident[:])

        w1_rows = w1.rearrange("(p j) c -> p j c", j=4)
        w3_rows = w3.rearrange("(g p j) n -> g p j n", g=2, j=4)
        late_rows = (w3_rows[0], w3_rows[1], w6.rearrange("(p j) n -> p j n", j=4))
        w5_scale_rows = w5_scales.rearrange("a r n -> r a n")

        def load_w1(i):
            nc.sync.dma_start(out=w1_raw[i][:], in_=w1_rows[:, :, W1_CUTS[i] : W1_CUTS[i + 1]])

        nc.sync.dma_start(out=idx[:], in_=offs)
        for q in range(4):
            nc.sync.dma_start(
                out=tab_s[32 * q : 32 * (q + 1)].bitcast(I32),
                in_=tab_scales[0][4 * q : 4 * q + 4].bitcast(I32).unsqueeze(0).to_broadcast([8, 4, T // 4]),
            )
        nc.sync.dma_start(out=tab_w[:].bitcast(I32), in_=tab_words[0].rearrange("p n t -> p (n t)").bitcast(I32))
        load_scale_rows(w2_raw_s, w2_scales[0], range(4))
        nc.sync.dma_start(out=w2_raw[:].bitcast(I32), in_=w2_words[0].bitcast(I32))
        for i in range(4):
            load_w1(i)
        nc.sync.dma_start(out=first_raw[0], in_=late_rows[0][:, :, 0:256])
        load_scale_rows(w4_s, w4_scales[0], (0, 1))
        nc.sync.dma_start(out=first_raw[1], in_=late_rows[1][:, :, 0:256])
        load_scale_rows(w4_s, w4_scales[0], (2, 3))
        nc.sync.dma_start(out=first_raw[2], in_=late_rows[2][:, :, 0:256])
        load_scale_rows(w5_s, w5_scale_rows, (0, 1))
        nc.sync.dma_start(out=w4_w[:].bitcast(I32), in_=w4_words[0].rearrange("p n t -> p (n t)").bitcast(I32))
        nc.sync.dma_start(out=w5_w[:].bitcast(I32), in_=w5_words.rearrange("a p b -> p a b").bitcast(I32))
        load_scale_rows(w5_s, w5_scale_rows, (2, 3))
        for s in range(3):
            nc.sync.dma_start(out=rest_raw[s], in_=late_rows[s][:, :, 256:N])
        nc.sync.dma_start(out=wgo_sb[:], in_=wgo)
        nc.sync.dma_start(out=idx2[:], in_=offs2)
        for c in range(4):
            nc.sync.dma_start(out=x0_sb[c][:], in_=x0[P * c : P * (c + 1), :])
        for u in range(4):
            nc.sync.dma_start(out=amp_sb[32 * u : 32 * (u + 1)], in_=amp.rearrange("(c a t) -> a c t", c=4, t=4))
        nc.sync.dma_start(out=amp_last[:], in_=amp[N - P : N].unsqueeze(1))

        v_s_all = held([P, S], U8, "v_s_all")
        v_s = [v_s_all[:, HALF * b : HALF * (b + 1)] for b in range(2)]
        v_w = {}
        w2_w = held([P, 2 * H], U8, "w2_w")
        w2_s = held([P, H], U8, "w2_s")
        w1_bf, w1_q, w1_s = {}, {}, {}
        h_bf, h_q, h_s = {}, {}, {}
        late_q, late_s = {}, [held([P, 768], U8, "late_s%d" % part) for part in range(2)]

        def gather_words(first, count, tag):
            words = held([P, 256 * count], U32, "v_w%d" % first, tag)
            nc.vector.tensor_copy(out=words[:], in_=tab_w[:].indirect(idx[:, 16 * first : 16 * (first + count)]))
            for i in range(count):
                v_w[first + i] = words[:, 256 * i : 256 * (i + 1)]

        def table_passes(out, codes, scales, b):
            for half in range(2):
                cols = slice(256 * half, 256 * (half + 1))
                nc.tensor.matmul_mx(
                    out=out[:, cols], lhsT=codes, lhsT_scale=scales,
                    rhs=v_w[2 * b + half].bitcast(FP8), rhs_scale=v_s[b][:, cols], start=(half == 0), stop=False,
                )

        def round_on_gpsimd(out, in_):
            nc.gpsimd.tensor_scalar(out=out, in0=in_, scalar1=1.0, scalar2=0.0, op0=MULT, op1=ADD)

        def round_w1(g, lo, hi, on_gpsimd, copy=nc.scalar.copy):
            i = max(load for load in range(4) if W1_CUTS[load] <= HALF * g + 4 * lo)
            raw = w1_raw[i][:, :, HALF * g + 4 * lo - W1_CUTS[i] : HALF * g + 4 * hi - W1_CUTS[i]]
            if on_gpsimd:
                dealt = w1_bf[g][:].rearrange("p (t m j) -> p m t j", t=4, j=4)
                round_on_gpsimd(dealt[:, lo:hi], raw.rearrange("p j (m t) -> p m t j", t=4))
            else:
                dealt = w1_bf[g][:].rearrange("p (t m j) -> p m j t", t=4, j=4)
                copy(out=dealt[:, lo:hi], in_=raw.rearrange("p j (m t) -> p m j t", t=4))

        def quantise(rounded, name, tag=None):
            codes = held([P, HALF], U32, name + "_q", tag)
            scales = held([P, HALF], U8, name + "_s")
            nc.vector.quantize_mx(out=codes[:].bitcast(FP8), scales=scales[:], in_=rounded)
            return codes[:], scales[:]

        def quantise_w1(g):
            w1_q[g], w1_s[g] = quantise(w1_bf[g][:], "w1_%d" % g)

        def quantise_w1_load(i):
            for t in range(4):
                lo = P * t + 64 * i
                nc.vector.quantize_mx(
                    out=w1_q[0][:, lo : lo + 64].bitcast(FP8), scales=w1_s[0][:, lo : lo + 64], in_=w1_bf[0][:, 4 * lo : 4 * (lo + 64)]
                )

        def quantise_h(g, b, tag=None):
            h_q[g, b], h_s[g, b] = quantise(h_bf[g, b][:].rearrange("p n t -> p (n t)"), "h_%d%d" % (g, b), tag)

        def round_late(rounded, raw, on_gpsimd):
            if on_gpsimd:
                round_on_gpsimd(rounded.rearrange("p (n j) -> p n j", j=4), raw.rearrange("p j n -> p n j"))
            else:
                nc.scalar.copy(
                    out=rounded.rearrange("p (a i j) -> p a j i", i=4, j=4), in_=raw.rearrange("p j (a i) -> p a j i", i=4)
                )

        def quantise_late(part, lo, hi, rounded):
            nc.vector.quantize_mx(out=late_q[part][:, lo:hi].bitcast(FP8), scales=late_s[part][:, lo:hi], in_=rounded)

        def late_weight(s, c):
            cols = slice(256 * s + P * (c % 2), 256 * s + P * (c % 2 + 1))
            return late_q[c // 2][:, cols].bitcast(FP8), late_s[c // 2][:, cols]

        b_sb, b_first = {}, {}

        def fp4_products(g, b, tags, halves=(0, 1)):
            for half in halves:
                b_sb[g, b, half] = held([P, 2, 256, 2], F32, "b_sb%d%d%d" % (g, b, half), tags[half])
                step = 4 * b + 2 * g + half
                cols = slice(256 * half, 256 * (half + 1))
                for pair in range(2):
                    b_ps = bank((3, 4, 5, 6, 3, 4, 7, 5, 3, 4, 6, 7, 5, 3, 6, 4)[2 * step + pair], [P, 2, 256])
                    for e in range(2):
                        lo = HALF * g + P * (2 * pair + e)
                        nc.tensor.matmul_mx(
                            out=b_ps[:, e, :],
                            lhsT=w2_w[:, 2 * lo : 2 * (lo + P)].bitcast(FP4), lhsT_scale=w2_s[:, lo : lo + P],
                            rhs=v_w[2 * b + half].bitcast(FP8), rhs_scale=v_s[b][:, cols], start=True, stop=True,
                        )
                    nc.scalar.copy(out=b_sb[g, b, half][:, pair], in_=b_ps[:].rearrange("p e n -> p n e"))

        def first_fp4_products():
            for jb in range(2):
                b_first[jb] = held([P, P, 4], F32, "b_first%d" % jb, (148, 101)[jb])
                cols = slice(P * jb, P * (jb + 1))
                b_ps = bank(3 + jb, [P, 4, P])
                for t in range(4):
                    nc.tensor.matmul_mx(
                        out=b_ps[:, t, :],
                        lhsT=w2_w[:, 2 * P * t : 2 * P * (t + 1)].bitcast(FP4), lhsT_scale=w2_s[:, P * t : P * (t + 1)],
                        rhs=v_w[0][:, cols].bitcast(FP8), rhs_scale=v_s[0][:, cols], start=True, stop=True,
                    )
                nc.scalar.copy(out=b_first[jb][:], in_=b_ps[:].rearrange("p t n -> p n t"))

        def features(g, b, tag, pieces=range(4), last_bank=None):
            if 0 in pieces:
                h_bf[g, b] = held([P, HALF, 4], BF16, "h_bf%d%d" % (g, b), tag)
            for piece in pieces:
                half, jb = divmod(piece, 2)
                cols = slice(P * piece, P * (piece + 1))
                a_ps = bank(last_bank or {0: 7}.get(8 * b + 4 * g + piece, (8 * b + 4 * g + piece) % 3), [P, 4, P])
                for t in range(4):
                    nc.tensor.matmul_mx(
                        out=a_ps[:, t, :],
                        lhsT=w1_q[g][:, P * t : P * (t + 1)].bitcast(FP8), lhsT_scale=w1_s[g][:, P * t : P * (t + 1)],
                        rhs=v_w[2 * b + half][:, P * jb : P * (jb + 1)].bitcast(FP8), rhs_scale=v_s[b][:, cols], start=True, stop=True,
                    )
                if (g, b, half) == (0, 0, 0):
                    b_piece = b_first[jb][:].rearrange("p n (q e) -> p n q e", q=2)
                else:
                    b_piece = b_sb[g, b, half][:, :, P * jb : P * (jb + 1), :].rearrange("p q n e -> p n q e")
                nc.vector.tensor_tensor(
                    out=h_bf[g, b][:, cols, :].rearrange("p n (q e) -> p n q e", q=2),
                    in0=a_ps[:].rearrange("p (q e) n -> p n q e", q=2),
                    in1=b_piece, op=MULT,
                )

        d_neg, e_sb, votes, page = {}, {}, {}, {}

        def first_sum(k, number):
            c, b = divmod(k, 2)
            rows = slice(P * c, P * (c + 1))
            d_ps = bank(number, [P, HALF])
            table_passes(d_ps, w4_w[:, rows].bitcast(FP8), w4_s[:, rows], b)
            for g in range(2):
                nc.tensor.matmul_mx(
                    out=d_ps[:], lhsT=late_weight(g, c)[0], lhsT_scale=late_weight(g, c)[1],
                    rhs=h_q[g, b].bitcast(FP8), rhs_scale=h_s[g, b], start=False, stop=(g == 1),
                )
            nc.scalar.activation(out=d_neg[k], in_=d_ps[:], func=ACT.Copy, scale=-1.0)

        def second_sum(k, number):
            c, b = divmod(k, 2)
            rows = slice(P * c, P * (c + 1))
            e_ps = bank(number, [P, HALF])
            table_passes(e_ps, *late_weight(2, c), b)
            for g in range(2):
                nc.tensor.matmul_mx(
                    out=e_ps[:], lhsT=w5_w[:, g, 2 * P * c : 2 * P * (c + 1)].bitcast(FP4), lhsT_scale=w5_s[:, g, rows],
                    rhs=h_q[g, b].bitcast(FP8), rhs_scale=h_s[g, b], start=False, stop=(g == 1),
                )
            return e_ps

        def weigh(k, tag):
            votes[k] = held([P, HALF], F32, "votes%d" % k, tag)[:]
            nc.gpsimd.tensor_tensor(out=votes[k], in0=d_neg[k], in1=wgo_sb[:, HALF * (k % 2) : HALF * (k % 2 + 1)], op=MULT)

        def place(k):
            c, b = divmod(k, 2)
            if b == 0:
                page[c] = held([P, WINDOW], F32, "page%d" % c, (78, 147, 128)[c])
            nc.vector.tensor_copy(out=page[c][:].indirect(idx2[:, 32 * b : 32 * (b + 1)]), in_=votes[k])

        def turn(c, z_banks, y_spot, sig):
            z_ps = [bank(number, [P, 4, P]) for number in z_banks]
            for src in (x0_sb[c], page[c]):
                for hh in range(2):
                    for u in range(4):
                        lo = 256 * u + P * hh
                        nc.tensor.matmul(
                            out=z_ps[hh][:, u, :], lhsT=src[:, lo : lo + P], rhs=ident[:], is_transpose=True,
                            start=(src is x0_sb[c] and u == 0), stop=(src is page[c] and u == 3),
                        )
            for hh in range(2):
                nc.scalar.activation(
                    out=sig[hh],
                    in_=z_ps[hh][:].rearrange("p u (a t) -> p t (u a)", t=4),
                    func=ACT.Sigmoid,
                )
            for hh in range(2):
                for t in range(4):
                    nc.tensor.transpose(y_spot(hh, t), sig[hh][:, t, :], ident[:])

        y_s = held([P, 256], U8, "y_s")
        z_banks = ((4, 3), (7, 5))
        y_banks = ((0, 1), (2, 6))

        def finish(c):
            y_ps = [bank(number, [P, 4, P]) for number in y_banks[c % 2]]
            both = held([P, 2, 4, P], F32, "sig", "sig%d" % (c % 2))
            turn(c, z_banks[c % 2], lambda hh, t: y_ps[hh][:, t, :], [both[:, hh] for hh in range(2)])
            y = held([P, 4, 256], F32, "y%d" % c)
            for hh in range(2):
                cols = slice(P * hh, P * (hh + 1))
                for t in range(4):
                    nc.scalar.activation(out=y[:, t, cols], in_=y_ps[hh][:, t, :], func=ACT.Copy, scale=amp_sb[:, c, t : t + 1])
                if c == 2:
                    round_on_gpsimd(
                        y_bf[c][:, HALF * hh : HALF * (hh + 1)].rearrange("p (m t) -> p m t", t=4), y[:, :, cols].rearrange("p t m -> p m t")
                    )
            if c == 1:
                round_on_gpsimd(y_bf[c].rearrange("p (m t) -> p m t", t=4), y[:].rearrange("p t m -> p m t"))
            if c == 0:
                nc.scalar.copy(out=y_bf[c].rearrange("p (a i t) -> p a t i", i=4, t=4), in_=y[:].rearrange("p t (a i) -> p a t i", i=4))
            rows = out_0[P * c : P * (c + 1), :].rearrange("(a t) m -> a t m", t=4)
            for u in QUADRANTS:
                nc.sync.dma_start(out=rows[:, :, 256 * u : 256 * (u + 1)], in_=y[32 * u : 32 * (u + 1)])

        def store_early_planes():
            y_q = held([P, 3, 256], U32, "y_q_early", 8)
            for c in range(3):
                nc.vector.quantize_mx(out=y_q[:, c, :].bitcast(FP8), scales=y_s[4 * c : P, :], in_=y_bf[c])
            words = out_1[0].rearrange("(c a) m t -> a c (m t)", c=4).bitcast(I32)
            for u in QUADRANTS:
                nc.sync.dma_start(
                    out=words[:, 0:3, 256 * u : 256 * (u + 1)], in_=y_q[32 * u : 32 * (u + 1)].bitcast(I32)
                )

        def finish_last():
            c = 3
            halves = [slice(HALF * hh, HALF * (hh + 1)) for hh in range(2)]
            z = held([P, S], F32, "z_last")
            y_last_bf = held([P, S], BF16, "y_last_bf")
            y_q = held([P, 256], U32, "y_q_last")
            early = [slice(0, 256), slice(256, HALF)]
            for cols in early + halves[1:]:
                nc.vector.tensor_tensor(out=z[:, cols], in0=page[c][:, cols], in1=x0_sb[c][:, cols], op=ADD)
            store_early_planes()
            s_rows = [held([P, HALF], F32, "s_rows0", "sig0")]
            for cols in early:
                nc.scalar.activation(out=s_rows[0][:, cols], in_=z[:, cols], func=ACT.Sigmoid)
            y_ps = [bank(number, [P, 4, P]) for number in y_banks[c % 2]]
            sig = [held([P, 4, P], F32, "sig", "sig3%d" % hh)[:] for hh in range(2)]
            turn(c, z_banks[c % 2], lambda hh, t: y_ps[hh][:, t, :], sig)
            s_rows.append(held([P, HALF], F32, "s_rows1", "page3"))
            nc.scalar.activation(out=s_rows[1][:], in_=z[:, halves[1]], func=ACT.Sigmoid)
            y = [held([P, HALF], F32, "y_last0", 0), held([P, HALF], F32, "y_last1")]
            nc.gpsimd.tensor_scalar(out=y[0][:], in0=s_rows[0][:], scalar1=amp_last[:, 0:1], scalar2=0.0, op0=MULT, op1=ADD)
            nc.scalar.activation(out=y[1][:], in_=s_rows[1][:], func=ACT.Copy, scale=amp_last[:, 0:1])
            for hh in range(2):
                nc.sync.dma_start(out=out_0[N - P : N, halves[hh]], in_=y[hh][:])
            for hh in range(2):
                nc.vector.tensor_tensor(
                    out=y_last_bf[:, halves[hh]].rearrange("p (m t) -> p m t", t=4), in0=y_ps[hh][:].rearrange("p t m -> p m t"),
                    in1=amp_sb[:, c, :].unsqueeze(1).to_broadcast([P, P, 4]), op=MULT,
                )
            words = out_1[0, 32 * c : 32 * (c + 1)].rearrange("a (u m) t -> u a (m t)", u=4).bitcast(I32)
            for hh in range(2):
                cols = slice(P * hh, P * (hh + 1))
                nc.vector.quantize_mx(out=y_q[:, cols].bitcast(FP8), scales=y_s[4 * c : P, cols], in_=y_last_bf[:, halves[hh]])
                nc.sync.dma_start(out=words[:, :, cols], in_=y_q[:, cols].bitcast(I32))
            for u in QUADRANTS:
                nc.sync.dma_start(
                    out=out_2[0][:, 256 * u : 256 * (u + 1)].bitcast(I32), in_=y_s[32 * u : 32 * u + 16, :].bitcast(I32)
                )

        nc.vector.tensor_copy(out=v_s_all[:], in_=tab_s[:].indirect(idx[:]))
        for g in range(2):
            nc.scalar.copy(
                out=w2_w[:].bitcast(U16).rearrange("p (g t m) -> p g t m", g=2, t=4)[:, g],
                in_=w2_raw[:].bitcast(U16).rearrange("p (g m t) -> p g t m", g=2, t=4)[:, g],
            )
        gather_words(0, 1, None)
        nc.vector.tensor_copy(
            out=w2_s[:].rearrange("p (g t m) -> p g t m", g=2, t=4),
            in_=w2_raw_s[:].rearrange("p (g m t) -> p g t m", g=2, t=4),
        )
        gather_words(1, 1, "w2_raw_s")
        w1_bf[0] = held([P, 4 * HALF], BF16, "w1_bf0", 0)
        round_w1(0, 0, 40, False)
        round_w1(0, 40, 64, False, nc.vector.tensor_copy)
        w1_q[0], w1_s[0] = held([P, HALF], U32, "w1_0_q")[:], held([P, HALF], U8, "w1_0_s")[:]
        quantise_w1_load(0)
        round_w1(0, 64, 84, False)
        round_w1(0, 84, 128, False, nc.vector.tensor_copy)
        quantise_w1_load(1)
        gather_words(2, 2, 105)
        w1_bf[1] = held([P, 4 * HALF], BF16, "w1_bf1", 4)
        round_w1(1, 72, 88, True)
        round_w1(1, 88, 128, True)

        first_fp4_products()
        features(0, 0, 12, (0, 1))
        fp4_products(0, 0, (None, 111), (1,))
        round_w1(1, 0, 72, False)
        features(0, 0, 12, (2, 3))
        fp4_products(1, 0, (133, 125))
        quantise_w1(1)
        quantise_h(0, 0, 120)
        first_w3 = held([P, 2048], BF16, "first_w3", 11)
        round_late(first_w3[:, 0:1024], first_raw[0], True)
        round_late(first_w3[:, 1024:2048], first_raw[1], False)
        features(1, 0, 20)
        fp4_products(0, 1, (158, 172))
        late_q[0] = held([P, 768], U32, "late_q0")
        quantise_late(0, 0, 512, first_w3[:])
        quantise_h(1, 0, 32)
        first_w6 = held([P, 1024], BF16, "first_w6", 18)
        round_late(first_w6[:], first_raw[2], True)
        features(0, 1, 36)
        d_neg[0] = held([P, HALF], F32, "d0")[:]
        first_sum(0, 7)
        fp4_products(1, 1, (133, 125))
        quantise_late(0, 512, 768, first_w6[:])
        quantise_h(0, 1, 52)
        weigh(0, 36)
        features(1, 1, 56, range(3))
        features(1, 1, 56, (3,), 5)
        e_first = second_sum(0, 6)
        rest_bf = held([P, 3072], BF16, "rest_bf", 64)
        for s in range(3):
            round_late(rest_bf[:, 1024 * s : 1024 * (s + 1)], rest_raw[s], False)
        nc.vector.tensor_tensor(out=votes[0], in0=e_first[:], in1=votes[0], op=MULT)
        quantise_h(1, 1)
        late_q[1] = held([P, 768], U32, "late_q1", "d0")
        quantise_late(1, 0, 512, rest_bf[:, 0:2048])
        quantise_late(1, 512, 768, rest_bf[:, 2048:3072])
        place(0)

        last = held([P, 2, S], F32, "last", 0)
        d_pair = held([P, 2, HALF], F32, "d_pair")
        order = (2, 1, 4, 3, 5, 6, 7)
        for i, k in enumerate(order):
            if k < 6:
                d_neg[k] = d_pair[:, k // 5] if k in (3, 5) else held([P, HALF], F32, "d%d" % k, {2: 89}.get(k))[:]
                e_sb[k] = held([P, HALF], F32, "e%d" % k, {2: 93}.get(k))[:]
            else:
                d_neg[k], e_sb[k] = (last[:, i, HALF * (k - 6) : HALF * (k - 5)] for i in range(2))
            d_bank, e_bank = ((4, 3), (7, 5))[max(i - 1, 0) % 2]
            first_sum(k, d_bank)
            nc.scalar.copy(out=e_sb[k], in_=second_sum(k, e_bank)[:])
        freed = 62
        for k in order[:5]:
            if k == 3:
                pair = held([P, 2, HALF], F32, "votes_pair", freed)
                nc.gpsimd.tensor_tensor(
                    out=pair[:], in0=d_pair[:], in1=wgo_sb[:, HALF:S].unsqueeze(1).to_broadcast([P, 2, HALF]), op=MULT
                )
                votes[3], votes[5] = pair[:, 0], pair[:, 1]
            elif k != 5:
                weigh(k, freed)
            nc.gpsimd.tensor_tensor(out=votes[k], in0=e_sb[k], in1=votes[k], op=MULT)
            freed = {2: 93}.get(k, "e%d" % k)
            place(k)
        weighed_last = held([P, S], F32, "weighed_last", freed)
        nc.gpsimd.tensor_tensor(out=weighed_last[:], in0=last[:, 0, :], in1=wgo_sb[:], op=MULT)
        page[3] = held([P, WINDOW], F32, "page3")
        nc.gpsimd.tensor_tensor(out=weighed_last[:], in0=last[:, 1, :], in1=weighed_last[:], op=MULT)
        nc.vector.tensor_copy(out=page[3][:].indirect(idx2[:]), in_=weighed_last[:])
        y_late = held([P, 2, S], BF16, "y_late", 0)
        y_bf = [held([P, S], BF16, "y_bf0")[:], y_late[:, 0], y_late[:, 1]]
        for c in range(3):
            finish(c)
        finish_last()
